import numpy as np
import ml_dtypes


def mxq(x, axis, fmt="e4m3"):
    dtype, down = {"e4m3": (ml_dtypes.float8_e4m3fn, 7), "e5m2": (ml_dtypes.float8_e5m2, 14)}[fmt]
    v = np.moveaxis(np.asarray(x, np.float32).astype(ml_dtypes.bfloat16).astype(np.float64), axis, -1)
    blocks = v.reshape(v.shape[:-1] + (-1, 32))
    amax = np.abs(blocks).max(-1, keepdims=True)
    byte = np.maximum(np.where(amax > 0, np.frexp(amax)[1] - 1 + 127, 0) - down, 1)
    scale = np.exp2(byte - 127.0)
    codes = (blocks / scale).astype(np.float32).astype(dtype).astype(np.float64)
    return np.moveaxis((codes * scale).reshape(v.shape), -1, axis)


WIDE = False


def mx_kscale(k):
    if not WIDE:
        return np.ones(k)
    levels = np.array([24, -24, 12, -12, 0])
    if k % 512:
        return np.exp2(np.random.permutation(np.resize(levels, k // 32))).repeat(32)
    a = np.empty((k // 512, 16))
    for p in range(k // 512):
        a[p, :8] = np.random.permutation(np.resize(levels, 8))
        for g in range(8):
            far = levels[np.abs(levels - a[p, g]) >= 10]
            a[p, g + 8] = far[np.random.randint(len(far))]
    return np.exp2(a.ravel()).repeat(32)


def f64(x):
    return np.asarray(x).astype(np.float64)


def striped(idx):
    return np.tile(idx.reshape(-1, 16).T, (8, 1)).astype(np.uint16)


def unstriped(offs):
    return offs[:16].T.reshape(-1).astype(np.int64)


E2M1 = np.array([0.0, 0.5, 1.0, 1.5, 2.0, 3.0, 4.0, 6.0, -0.0, -0.5, -1.0, -1.5, -2.0, -3.0, -4.0, -6.0])


def pack_weight(w, fmt):
    k, n = w.shape
    w = f64(np.asarray(w, np.float32).astype(ml_dtypes.bfloat16)).reshape(k // 32, 32, n)
    amax = np.abs(w).max(1)
    if fmt == "e4m3":
        byte = np.frexp(amax)[1] - 1 + 127 - 7
    else:
        mant, ex = np.frexp(amax / 6.0)
        byte = np.where(mant > 0.5, ex, ex - 1) + 127
    byte = np.clip(np.where(amax > 0, byte, 1), 1, 254)
    scaled = (w * np.exp2(127.0 - byte)[:, None, :]).reshape(k, n).astype(np.float32)
    by_word = np.ascontiguousarray(scaled.reshape(k // 512, 128, 4, n).transpose(0, 1, 3, 2))
    if fmt == "e4m3":
        words = by_word.astype(ml_dtypes.float8_e4m3fn).view(np.uint8)
    else:
        c = by_word.astype(ml_dtypes.float4_e2m1fn).view(np.uint8) & 0xF
        words = (c[..., 0::2] | (c[..., 1::2] << 4)).reshape(k // 512, 128, 2 * n)
    return np.ascontiguousarray(words), np.ascontiguousarray(byte.astype(np.uint8).reshape(k // 512, 16, n))


def unpack_weight(words, scales, fmt):
    g, _, n = scales.shape
    words = np.ascontiguousarray(words).reshape(g, 128, n, -1)
    if fmt == "e4m3":
        vals = words.view(ml_dtypes.float8_e4m3fn).astype(np.float64)
    else:
        nib = np.empty((g, 128, n, 4), np.uint8)
        nib[..., 0::2] = words & 0xF
        nib[..., 1::2] = words >> 4
        vals = E2M1[nib]
    vals = vals * np.repeat(np.exp2(scales.astype(np.float64) - 127.0), 8, axis=1)[..., None]
    return vals.transpose(0, 1, 3, 2).reshape(g * 512, n)


def gelu(f):
    return 0.5 * f * (1.0 + np.tanh(np.sqrt(2.0 / np.pi) * (f + 0.044715 * f**3)))


K, R, N, T, J = 1024, 1024, 256, 2048, 1024


def setup_inputs():
    n = np.random.standard_normal
    s = mx_kscale(K)[:, None]
    u = mx_kscale(R)[:, None]
    p_tab = pack_weight(n((K, T)) * s, "e4m3")
    p_wg = pack_weight(n((K, R)) / np.sqrt(K) / s, "e4m3")
    p_wd = pack_weight(n((R, N)) / np.sqrt(R) / u, "e4m3")
    return {
        "tab_words": p_tab[0],
        "tab_scales": p_tab[1],
        "wg_words": p_wg[0],
        "wg_scales": p_wg[1],
        "wu": (n((K, R)) / np.sqrt(K) / s * u.T).astype(np.float32),
        "wd_words": p_wd[0],
        "wd_scales": p_wd[1],
        "ts": np.tile(np.exp(0.5 * n(T)), (128, 1)).astype(np.float32),
        "offs": striped(np.random.permutation(T)[:J]),
    }


def reference(tab_words, tab_scales, wg_words, wg_scales, wu, wd_words, wd_scales, ts, offs):
    idx = unstriped(offs)
    tab_ = unpack_weight(tab_words, tab_scales, "e4m3")[:, idx]
    wg_ = unpack_weight(wg_words, wg_scales, "e4m3")
    wu_ = mxq(f64(wu), 0, "e4m3")
    ga = wg_.T @ tab_
    ub = wu_.T @ tab_
    h = gelu(ga) * ub
    h_ = mxq(h, 0, "e4m3")
    wd_ = unpack_weight(wd_words, wd_scales, "e4m3")
    y = wd_.T @ h_
    return y * f64(ts)[0, idx][None, :]

@@ -1,0 +1,240 @@
+from contextlib import ExitStack
+
+import concourse.mybir as mybir
+from concourse.masks import make_identity
+
+K, R, N, T, J = 1024, 1024, 256, 2048, 1024
+FLOPS = 2 * (2 * K * R * J + R * N * J)
+
+F32 = mybir.dt.float32
+BF16 = mybir.dt.bfloat16
+I32 = mybir.dt.int32
+U32 = mybir.dt.uint32
+U16 = mybir.dt.uint16
+U8 = mybir.dt.uint8
+FP8X4 = mybir.dt.float8_e4m3fn_x4
+GELU = mybir.ActivationFunctionType.Gelu_apprx_tanh
+MULT = mybir.AluOpType.mult
+
+ADD = mybir.AluOpType.add
+P = 128
+GOUT = 0
+PERM = 'VVVV'
+BANKS = (5, 3)
+CAST = 'SSSVSSSS'
+LOADS = [('offs',), ('tab', 0), ('ts',), ('wg', 0, 0, 1), ('tabs',), ('wg', 0, 1, 2), ('tab', 1), ('wu', 0, 0, 1), ('wgs',), ('wu', 0, 0, 0), ('wu', 0, 1, 0), ('wu', 0, 1, 1), ('wg', 1, 0, 2), ('wu', 1, 0, 0), ('wu', 1, 1, 1), ('wd',), ('wu', 1, 0, 1), ('wu', 1, 1, 0), ('wds',)]
+STEPS = [('pw', 0), ('gs', 0, 256), ('g0', 0, 512), ('gs', 256, 512), ('g1', 256, 512), ('gs', 512, 1024), ('g1', 0, 256), ('ps', 0), ('g0', 512, 1024), ('g1', 512, 1024), ('cast', 0, 0, 0), ('cast', 0, 0, 1), ('gate', 0, 0, 0), ('gate', 0, 0, 1), ('cast', 0, 1, 0), ('cast', 0, 1, 1), ('qw', 0, 0), ('qw', 0, 1), ('gate', 0, 1, 0), ('gate', 0, 1, 1), ('gt', 0, 1024), ('gate', 0, 2, 0), ('gate', 0, 2, 1), ('up', 0, 1, 0), ('pw', 1), ('up', 0, 0, 0), ('gate', 0, 3, 0), ('up', 0, 0, 1), ('cast', 1, 0, 1), ('ps', 1), ('gate', 0, 3, 1), ('cast', 1, 0, 0), ('up', 0, 1, 1), ('gate', 1, 0, 0), ('qw', 1, 0), ('up', 0, 2, 0), ('qh', 0, 0, 512), ('cast', 1, 1, 0), ('gate', 1, 0, 1), ('up', 0, 2, 1), ('cast', 1, 1, 1), ('up', 0, 3, 0), ('qw', 1, 1), ('up', 0, 3, 1), ('gate', 1, 1, 1), ('gate', 1, 1, 0), ('up', 1, 0, 0), ('qh', 0, 512, 1024), ('gate', 1, 2, 0), ('up', 1, 0, 1), ('gate', 1, 2, 1), ('up', 1, 1, 0), ('qh', 1, 0, 256), ('gate', 1, 3, 0), ('up', 1, 1, 1), ('gate', 1, 3, 1), ('up', 1, 2, 0), ('qh', 1, 256, 512), ('up', 1, 2, 1), ('down', 0, 256), ('down', 256, 512), ('up', 1, 3, 0), ('qh', 1, 512, 768), ('up', 1, 3, 1), ('qh', 1, 768, 896), ('down', 512, 768), ('qh', 1, 896, 1024), ('down', 768, 896), ('down', 896, 1024)]
+
+
+def tile_list_gmlpt_gelu_tsL_kernel(tc, tab_words, tab_scales, wg_words, wg_scales, wu, wd_words, wd_scales, ts, offs, out):
+    nc = tc.nc
+    with ExitStack() as ctx:
+        keep = ctx.enter_context(tc.tile_pool(name="keep", bufs=1))
+        ps_g = ctx.enter_context(tc.psum_pool(name="ps_g", bufs=BANKS[0]))
+        ps_u = ctx.enter_context(tc.psum_pool(name="ps_u", bufs=BANKS[1]))
+
+        offsets = keep.tile([P, J // 16], U16, name="offsets")
+
+        tab_s = keep.tile([P, T], U8, name="tab_s", align_bytes=64)
+        wg_s_raw = keep.tile([P, R], U8, name="wg_s_raw", align_bytes=64)
+        wd_s = keep.tile([P, N], U8, name="wd_s", align_bytes=64)
+        for plane in (tab_s, wg_s_raw, wd_s):
+            nc.vector.memset(plane[:].bitcast(I32), 0)
+
+        def load_scales(queue, plane, src):
+            for q in range(4):
+                queue.dma_start(plane[32 * q : 32 * q + 8, :].bitcast(I32), src[:, 4 * q : 4 * q + 4, :].bitcast(I32))
+
+        tab_w = [keep.tile([P, T], U32, name="tab_w%d" % a, align_bytes=64) for a in range(2)]
+        wg_raw = [keep.tile([P, 2, 512], I32, name="wg_raw%d" % b, align_bytes=64) for b in range(2)]
+        wu_raw = {(b, a): keep.tile([P, 4, 512], F32, name="wu_raw%d%d" % (b, a), align_bytes=64) for b in range(2) for a in range(2)}
+        wd_w = keep.tile([P, 2, N], U32, name="wd_w", align_bytes=64)
+        ts_all = keep.tile([P, T], F32, name="ts_all", align_bytes=64)
+        wg_src = wg_words.rearrange("a p r i -> p a (r i)")
+
+        def load_tab(a):
+            nc.sync.dma_start(tab_w[a][:].bitcast(I32), tab_words[a].rearrange("p t i -> p (t i)").bitcast(I32))
+
+        def load_wg(b, a0, a1):
+            nc.sync.dma_start(wg_raw[b][:, a0:a1, :], wg_src[:, a0:a1, 2048 * b : 2048 * (b + 1)].bitcast(I32))
+
+        def load_wu(b, a, h):
+            if True:
+                src = wu[512 * a : 512 * (a + 1), 512 * b + 256 * h : 512 * b + 256 * (h + 1)]
+                nc.sync.dma_start(wu_raw[b, a][:, :, 256 * h : 256 * (h + 1)], src.rearrange("(p i) c -> p i c", i=4))
+
+        ts_row = keep.tile([P, 16], F32, name="ts_row", align_bytes=64)
+
+        def load(kind, *x):
+            if kind == "offs":
+                nc.sync.dma_start(offsets[:], offs)
+            elif kind == "ts":
+                nc.sync.dma_start(ts_row[:], ts[0].rearrange("(p c) -> p c", c=16))
+            elif kind == "wd":
+                nc.sync.dma_start(wd_w[:].bitcast(I32), wd_words.rearrange("a p n i -> p a (n i)").bitcast(I32))
+            elif kind == "tabs":
+                load_scales(nc.sync, tab_s, tab_scales)
+            elif kind == "wgs":
+                load_scales(nc.sync, wg_s_raw, wg_scales)
+            elif kind == "wds":
+                load_scales(nc.gpsimd, wd_s, wd_scales)
+            elif kind == "tab":
+                load_tab(*x)
+            elif kind == "wg":
+                load_wg(*x)
+            else:
+                load_wu(*x)
+
+        for item in LOADS:
+            load(*item)
+
+        warm = keep.tile([P, 8], F32, name="warm")
+        nc.vector.memset(warm[:], 0.0)
+        nc.scalar.activation(warm[:, 0:1], warm[:, 1:2], GELU)
+
+        ident = keep.tile([P, P], F32, name="ident", align_bytes=64)
+        make_identity(nc, ident[:])
+        for c0 in range(0, 16, 4):
+            bank = ps_u.tile([P, 4, P], F32, name="ub")
+            for c in range(4):
+                nc.tensor.transpose(bank[:, c, :], ts_row[:, c0 + c : c0 + c + 1].to_broadcast([P, P]), ident[:])
+            nc.scalar.copy(ts_all[:].rearrange("q (p c) -> q p c", c=16)[:, :, c0 : c0 + 4], bank[:].rearrange("q c p -> q p c"))
+
+        v_w = [keep.tile([P, J], U32, name="v_w%d" % a, align_bytes=64) for a in range(2)]
+        v_s = keep.tile([P, J], U8, name="v_s", align_bytes=64)
+        ts_g = keep.tile([P, J], F32, name="ts_g", align_bytes=64)
+
+        def gather(dst, window, j0, j1):
+            nc.vector.tensor_copy(dst[:, j0:j1], window[:].indirect(offsets[:, j0 // 16 : j1 // 16]))
+
+        wg_w = [keep.tile([P, 2, 4, P], U32, name="wg_w%d" % b, align_bytes=64) for b in range(2)]
+        wg_s = keep.tile([P, 2, 4, P], U8, name="wg_s", align_bytes=64)
+
+        def permute_wg(b):
+            (nc.vector if PERM[b] == "V" else nc.gpsimd).tensor_copy(
+                wg_w[b][:].bitcast(I32).rearrange("p a t m -> p a m t"),
+                wg_raw[b][:].rearrange("p a (m t) -> p a m t", t=4),
+            )
+
+        def permute_scales(b):
+            (nc.vector if PERM[2 + b] == "V" else nc.gpsimd).tensor_copy(wg_s[:, b, :, :].rearrange("p t m -> p m t"), wg_s_raw[:, 512 * b : 512 * (b + 1)].rearrange("p (m t) -> p m t", t=4))
+
+        wu_bf = {(b, a): keep.tile([P, 4, P, 4], BF16, name="wu_bf%d%d" % (b, a), align_bytes=64) for b in range(2) for a in range(2)}
+        wu_w = {(b, a): keep.tile([P, 512], U32, name="wu_w%d%d" % (b, a), align_bytes=64) for b in range(2) for a in range(2)}
+        wu_s = {(b, a): keep.tile([P, 512], U8, name="wu_s%d%d" % (b, a), align_bytes=64) for b in range(2) for a in range(2)}
+
+        def cast_wu(b, a, h):
+            dst = wu_bf[b, a][:, :, 64 * h : 64 * (h + 1), :].rearrange("p t m i -> p m i t")
+            src = wu_raw[b, a][:, :, 256 * h : 256 * (h + 1)].rearrange("p i (m t) -> p m i t", t=4)
+            who = CAST[4 * b + 2 * a + h]
+            if who == "S":
+                nc.scalar.copy(dst, src)
+            elif who == "V":
+                nc.vector.tensor_copy(dst, src)
+            else:
+                nc.gpsimd.tensor_scalar(dst, src, 1.0, 0.0, MULT, ADD)
+
+        def quantize_wu(b, a):
+            nc.vector.quantize_mx(wu_w[b, a][:].bitcast(FP8X4), wu_s[b, a][:], wu_bf[b, a][:].rearrange("p t m i -> p (t m i)"))
+
+        g = {(b, c): keep.tile([P, 2, 256, 2], F32, name="g%d%d" % (b, c), align_bytes=64) for b in range(2) for c in range(4)}
+
+        def gate(b, c, u):
+            cols = slice(256 * c, 256 * (c + 1))
+            if True:
+                bank = ps_g.tile([P, 2, 256], F32, name="ga")
+                for e in range(2):
+                    t = 2 * u + e
+                    for a in range(2):
+                        nc.tensor.matmul_mx(
+                            bank[:, e, :],
+                            lhsT=wg_w[b][:, a, t, :].bitcast(FP8X4),
+                            lhsT_scale=wg_s[4 * a : P, b, t, :],
+                            rhs=v_w[a][:, cols].bitcast(FP8X4),
+                            rhs_scale=v_s[4 * a : P, cols],
+                            start=(a == 0),
+                            stop=(a == 1),
+                        )
+                nc.scalar.activation(g[b, c][:, u, :, :], bank[:].rearrange("p e j -> p j e"), GELU)
+
+        h_bf = [keep.tile([P, J, 4], BF16, name="h_bf%d" % b, align_bytes=64) for b in range(2)]
+        h_w = [keep.tile([P, J], U32, name="h_w%d" % b, align_bytes=64) for b in range(2)]
+        h_s = [keep.tile([P, J], U8, name="h_s%d" % b, align_bytes=64) for b in range(2)]
+
+        def up(b, c, d):
+            if True:
+                cols = slice(256 * c + P * d, 256 * c + P * (d + 1))
+                bank = ps_u.tile([P, 4, P], F32, name="ub")
+                for t in range(4):
+                    for a in range(2):
+                        nc.tensor.matmul_mx(
+                            bank[:, t, :],
+                            lhsT=wu_w[b, a][:, P * t : P * (t + 1)].bitcast(FP8X4),
+                            lhsT_scale=wu_s[b, a][:, P * t : P * (t + 1)],
+                            rhs=v_w[a][:, cols].bitcast(FP8X4),
+                            rhs_scale=v_s[4 * a : P, cols],
+                            start=(a == 0),
+                            stop=(a == 1),
+                        )
+                nc.vector.tensor_tensor(
+                    h_bf[b][:, cols, :].rearrange("p j (u e) -> p j u e", u=2),
+                    bank[:].rearrange("p (u e) j -> p j u e", u=2),
+                    g[b, c][:, :, P * d : P * (d + 1), :].rearrange("p u j e -> p j u e"),
+                    MULT,
+                )
+
+        def quantize_h(b, j0, j1):
+            nc.vector.quantize_mx(h_w[b][:, j0:j1].bitcast(FP8X4), h_s[b][:, j0:j1], h_bf[b][:, j0:j1, :].rearrange("p j t -> p (j t)"))
+
+        def down(j0, j1):
+            w = j1 - j0
+            bank = ps_g.tile([P, 2, w], F32, name="ga")
+            for n in range(2):
+                for b in range(2):
+                    nc.tensor.matmul_mx(
+                        bank[:, n, :],
+                        lhsT=wd_w[:, b, P * n : P * (n + 1)].bitcast(FP8X4),
+                        lhsT_scale=wd_s[4 * b : P, P * n : P * (n + 1)],
+                        rhs=h_w[b][:, j0:j1].bitcast(FP8X4),
+                        rhs_scale=h_s[b][:, j0:j1],
+                        start=(b == 0),
+                        stop=(b == 1),
+                    )
+            res = keep.tile([P, 2, w], F32, name="res%d" % j0)
+            factor = ts_g[:, j0:j1].unsqueeze(1).to_broadcast([P, 2, w])
+            if j0 < GOUT:
+                y_sb = keep.tile([P, 2, w], F32, name="y_sb%d" % j0)
+                nc.scalar.copy(y_sb[:], bank[:])
+                nc.gpsimd.tensor_tensor(res[:], y_sb[:], factor, MULT)
+            else:
+                nc.vector.tensor_tensor(res[:], bank[:], factor, MULT)
+            nc.sync.dma_start(out[:, j0:j1].rearrange("(n p) j -> p n j", p=P), res[:])
+
+        def step(kind, *x):
+            if kind == "gs":
+                gather(v_s, tab_s, *x)
+            elif kind == "g0":
+                gather(v_w[0], tab_w[0], *x)
+            elif kind == "g1":
+                gather(v_w[1], tab_w[1], *x)
+            elif kind == "gt":
+                gather(ts_g, ts_all, *x)
+            elif kind == "pw":
+                permute_wg(*x)
+            elif kind == "ps":
+                permute_scales(*x)
+            elif kind == "cast":
+                cast_wu(*x)
+            elif kind == "qw":
+                quantize_wu(*x)
+            elif kind == "gate":
+                gate(*x)
+            elif kind == "up":
+                up(*x)
+            elif kind == "qh":
+                quantize_h(*x)
+            else:
+                down(*x)
+
+        for item in STEPS:
+            step(*item)

@@ -18,18 +18,22 @@ MULT = mybir.AluOpType.mult
 
 ADD = mybir.AluOpType.add
 P = 128
+TIES = []
+TSTIE = 512
 GOUT = 0
 PERM = 'VVVV'
 BANKS = (5, 3)
-CAST = 'SSSVSSSS'
-LOADS = [('offs',), ('tab', 0), ('ts',), ('wg', 0, 0, 1), ('tabs',), ('wg', 0, 1, 2), ('tab', 1), ('wu', 0, 0, 1), ('wgs',), ('wu', 0, 0, 0), ('wu', 0, 1, 0), ('wu', 0, 1, 1), ('wg', 1, 0, 2), ('wu', 1, 0, 0), ('wu', 1, 1, 1), ('wd',), ('wu', 1, 0, 1), ('wu', 1, 1, 0), ('wds',)]
-STEPS = [('pw', 0), ('gs', 0, 256), ('g0', 0, 512), ('gs', 256, 512), ('g1', 256, 512), ('gs', 512, 1024), ('g1', 0, 256), ('ps', 0), ('g0', 512, 1024), ('g1', 512, 1024), ('cast', 0, 0, 0), ('cast', 0, 0, 1), ('gate', 0, 0, 0), ('gate', 0, 0, 1), ('cast', 0, 1, 0), ('cast', 0, 1, 1), ('qw', 0, 0), ('qw', 0, 1), ('gate', 0, 1, 0), ('gate', 0, 1, 1), ('gt', 0, 1024), ('gate', 0, 2, 0), ('gate', 0, 2, 1), ('up', 0, 1, 0), ('pw', 1), ('up', 0, 0, 0), ('gate', 0, 3, 0), ('up', 0, 0, 1), ('cast', 1, 0, 1), ('ps', 1), ('gate', 0, 3, 1), ('cast', 1, 0, 0), ('up', 0, 1, 1), ('gate', 1, 0, 0), ('qw', 1, 0), ('up', 0, 2, 0), ('qh', 0, 0, 512), ('cast', 1, 1, 0), ('gate', 1, 0, 1), ('up', 0, 2, 1), ('cast', 1, 1, 1), ('up', 0, 3, 0), ('qw', 1, 1), ('up', 0, 3, 1), ('gate', 1, 1, 1), ('gate', 1, 1, 0), ('up', 1, 0, 0), ('qh', 0, 512, 1024), ('gate', 1, 2, 0), ('up', 1, 0, 1), ('gate', 1, 2, 1), ('up', 1, 1, 0), ('qh', 1, 0, 256), ('gate', 1, 3, 0), ('up', 1, 1, 1), ('gate', 1, 3, 1), ('up', 1, 2, 0), ('qh', 1, 256, 512), ('up', 1, 2, 1), ('down', 0, 256), ('down', 256, 512), ('up', 1, 3, 0), ('qh', 1, 512, 768), ('up', 1, 3, 1), ('qh', 1, 768, 896), ('down', 512, 768), ('qh', 1, 896, 1024), ('down', 768, 896), ('down', 896, 1024)]
+CAST = 'SSVVSSSS'
+LOADS = [('S', 'offs'), ('A', 'ts'), ('A', 'tabs'), ('A', 'wgs'), ('S', 'tab', 0), ('S', 'wg', 0, 0, 2), ('S', 'wu', 0, 0, 0, 2), ('S', 'tab', 1), ('S', 'wu', 0, 1, 0, 2), ('S', 'wg', 1, 0, 2), ('S', 'wu', 1, 0, 0, 2), ('S', 'wu', 1, 1, 0, 2), ('S', 'wd'), ('S', 'wds')]
+STEPS = [('g0', 0, 512), ('gs', 0, 512), ('pw', 0), ('ps', 0), ('g1', 0, 256), ('g1', 256, 512), ('g0', 512, 1024), ('gs', 512, 1024), ('g1', 512, 1024), ('cast', 0, 0, 0), ('cast', 0, 0, 1), ('cast', 0, 1, 0), ('cast', 0, 1, 1), ('qw', 0, 0, 2), ('gate', 0, 0, 0), ('gate', 0, 0, 1), ('up', 0, 0, 0), ('up', 0, 0, 1), ('gate', 0, 1, 0), ('gate', 0, 1, 1), ('gt', 0, 512), ('gt', 512, 1024), ('up', 0, 1, 0), ('up', 0, 1, 1), ('gate', 0, 2, 0), ('gate', 0, 2, 1), ('cast', 1, 0, 0), ('cast', 1, 0, 1), ('pw', 1), ('ps', 1), ('up', 0, 2, 0), ('gate', 0, 3, 0), ('gate', 0, 3, 1), ('up', 0, 2, 1), ('cast', 1, 1, 0), ('cast', 1, 1, 1), ('qw', 1, 0, 1), ('up', 0, 3, 0), ('gate', 1, 0, 0), ('gate', 1, 0, 1), ('qw', 1, 1, 2), ('up', 0, 3, 1), ('qh', 0, 0, 512), ('gate', 1, 1, 0), ('up', 1, 0, 0), ('gate', 1, 1, 1), ('up', 1, 0, 1), ('qh', 0, 512, 1024), ('gate', 1, 2, 0), ('up', 1, 1, 0), ('qh', 1, 0, 256), ('gate', 1, 2, 1), ('up', 1, 1, 1), ('gate', 1, 3, 0), ('down', 0, 256), ('up', 1, 2, 0), ('qh', 1, 256, 512), ('gate', 1, 3, 1), ('up', 1, 2, 1), ('down', 256, 512), ('up', 1, 3, 0), ('qh', 1, 512, 768), ('up', 1, 3, 1), ('qh', 1, 768, 896), ('down', 512, 768), ('qh', 1, 896, 1024), ('down', 768, 896), ('down', 896, 1024)]
 
 
 def tile_list_gmlpt_gelu_tsL_kernel(tc, tab_words, tab_scales, wg_words, wg_scales, wu, wd_words, wd_scales, ts, offs, out):
     nc = tc.nc
     with ExitStack() as ctx:
         keep = ctx.enter_context(tc.tile_pool(name="keep", bufs=1))
+        shared = ctx.enter_context(tc.tile_pool(name="shared", bufs=1))
+        place = {"wu_raw00": 0, "wu_raw01": 8192, "wu_raw10": 16384, "wu_raw11": 24576, "wu_bf0": 32768, "wu_bf1": 40960}
         ps_g = ctx.enter_context(tc.psum_pool(name="ps_g", bufs=BANKS[0]))
         ps_u = ctx.enter_context(tc.psum_pool(name="ps_u", bufs=BANKS[1]))
 
@@ -47,43 +51,46 @@ def tile_list_gmlpt_gelu_tsL_kernel(tc, tab_words, tab_scales, wg_words, wg_scal
 
         tab_w = [keep.tile([P, T], U32, name="tab_w%d" % a, align_bytes=64) for a in range(2)]
         wg_raw = [keep.tile([P, 2, 512], I32, name="wg_raw%d" % b, align_bytes=64) for b in range(2)]
-        wu_raw = {(b, a): keep.tile([P, 4, 512], F32, name="wu_raw%d%d" % (b, a), align_bytes=64) for b in range(2) for a in range(2)}
+        wu_raw = {(b, a): shared.tile([P, 4, 512], F32, name="wu_raw%d%d" % (b, a), offset=place["wu_raw%d%d" % (b, a)], align_bytes=64) for b in range(2) for a in range(2)}
         wd_w = keep.tile([P, 2, N], U32, name="wd_w", align_bytes=64)
         ts_all = keep.tile([P, T], F32, name="ts_all", align_bytes=64)
         wg_src = wg_words.rearrange("a p r i -> p a (r i)")
 
-        def load_tab(a):
-            nc.sync.dma_start(tab_w[a][:].bitcast(I32), tab_words[a].rearrange("p t i -> p (t i)").bitcast(I32))
+        def load_tab(queue, a):
+            queue.dma_start(tab_w[a][:].bitcast(I32), tab_words[a].rearrange("p t i -> p (t i)").bitcast(I32))
 
-        def load_wg(b, a0, a1):
-            nc.sync.dma_start(wg_raw[b][:, a0:a1, :], wg_src[:, a0:a1, 2048 * b : 2048 * (b + 1)].bitcast(I32))
+        def load_wg(queue, b, a0, a1):
+            queue.dma_start(wg_raw[b][:, a0:a1, :], wg_src[:, a0:a1, 2048 * b : 2048 * (b + 1)].bitcast(I32))
 
-        def load_wu(b, a, h):
+        def load_wu(queue, b, a, h0, h1):
             if True:
-                src = wu[512 * a : 512 * (a + 1), 512 * b + 256 * h : 512 * b + 256 * (h + 1)]
-                nc.sync.dma_start(wu_raw[b, a][:, :, 256 * h : 256 * (h + 1)], src.rearrange("(p i) c -> p i c", i=4))
+                src = wu[512 * a : 512 * (a + 1), 512 * b + 256 * h0 : 512 * b + 256 * h1]
+                queue.dma_start(wu_raw[b, a][:, :, 256 * h0 : 256 * h1], src.rearrange("(p i) c -> p i c", i=4))
 
         ts_row = keep.tile([P, 16], F32, name="ts_row", align_bytes=64)
 
-        def load(kind, *x):
+        queues = {"S": nc.sync, "A": nc.scalar, "G": nc.gpsimd}
+
+        def load(queue, kind, *x):
+            queue = queues[queue]
             if kind == "offs":
                 nc.sync.dma_start(offsets[:], offs)
             elif kind == "ts":
-                nc.sync.dma_start(ts_row[:], ts[0].rearrange("(p c) -> p c", c=16))
+                queue.dma_start(ts_row[:], ts[0].rearrange("(p c) -> p c", c=16))
             elif kind == "wd":
-                nc.sync.dma_start(wd_w[:].bitcast(I32), wd_words.rearrange("a p n i -> p a (n i)").bitcast(I32))
+                queue.dma_start(wd_w[:].bitcast(I32), wd_words.rearrange("a p n i -> p a (n i)").bitcast(I32))
             elif kind == "tabs":
-                load_scales(nc.sync, tab_s, tab_scales)
+                load_scales(queue, tab_s, tab_scales)
             elif kind == "wgs":
-                load_scales(nc.sync, wg_s_raw, wg_scales)
+                load_scales(queue, wg_s_raw, wg_scales)
             elif kind == "wds":
-                load_scales(nc.gpsimd, wd_s, wd_scales)
+                load_scales(queue, wd_s, wd_scales)
             elif kind == "tab":
-                load_tab(*x)
+                load_tab(queue, *x)
             elif kind == "wg":
-                load_wg(*x)
+                load_wg(queue, *x)
             else:
-                load_wu(*x)
+                load_wu(queue, *x)
 
         for item in LOADS:
             load(*item)
@@ -95,14 +102,14 @@ def tile_list_gmlpt_gelu_tsL_kernel(tc, tab_words, tab_scales, wg_words, wg_scal
         ident = keep.tile([P, P], F32, name="ident", align_bytes=64)
         make_identity(nc, ident[:])
         for c0 in range(0, 16, 4):
-            bank = ps_u.tile([P, 4, P], F32, name="ub")
+            bank = ps_g.tile([P, 4, P], F32, name="ga")
             for c in range(4):
                 nc.tensor.transpose(bank[:, c, :], ts_row[:, c0 + c : c0 + c + 1].to_broadcast([P, P]), ident[:])
             nc.scalar.copy(ts_all[:].rearrange("q (p c) -> q p c", c=16)[:, :, c0 : c0 + 4], bank[:].rearrange("q c p -> q p c"))
 
         v_w = [keep.tile([P, J], U32, name="v_w%d" % a, align_bytes=64) for a in range(2)]
         v_s = keep.tile([P, J], U8, name="v_s", align_bytes=64)
-        ts_g = keep.tile([P, J], F32, name="ts_g", align_bytes=64)
+        ts_g = {}
 
         def gather(dst, window, j0, j1):
             nc.vector.tensor_copy(dst[:, j0:j1], window[:].indirect(offsets[:, j0 // 16 : j1 // 16]))
@@ -119,12 +126,12 @@ def tile_list_gmlpt_gelu_tsL_kernel(tc, tab_words, tab_scales, wg_words, wg_scal
         def permute_scales(b):
             (nc.vector if PERM[2 + b] == "V" else nc.gpsimd).tensor_copy(wg_s[:, b, :, :].rearrange("p t m -> p m t"), wg_s_raw[:, 512 * b : 512 * (b + 1)].rearrange("p (m t) -> p m t", t=4))
 
-        wu_bf = {(b, a): keep.tile([P, 4, P, 4], BF16, name="wu_bf%d%d" % (b, a), align_bytes=64) for b in range(2) for a in range(2)}
-        wu_w = {(b, a): keep.tile([P, 512], U32, name="wu_w%d%d" % (b, a), align_bytes=64) for b in range(2) for a in range(2)}
-        wu_s = {(b, a): keep.tile([P, 512], U8, name="wu_s%d%d" % (b, a), align_bytes=64) for b in range(2) for a in range(2)}
+        wu_bf = [shared.tile([P, 2, 4, P, 4], BF16, name="wu_bf%d" % b, offset=place["wu_bf%d" % b], align_bytes=64) for b in range(2)]
+        wu_w = [keep.tile([P, 2, 512], U32, name="wu_w%d" % b, align_bytes=64) for b in range(2)]
+        wu_s = [keep.tile([P, 2, 512], U8, name="wu_s%d" % b, align_bytes=64) for b in range(2)]
 
         def cast_wu(b, a, h):
-            dst = wu_bf[b, a][:, :, 64 * h : 64 * (h + 1), :].rearrange("p t m i -> p m i t")
+            dst = wu_bf[b][:, a, :, 64 * h : 64 * (h + 1), :].rearrange("p t m i -> p m i t")
             src = wu_raw[b, a][:, :, 256 * h : 256 * (h + 1)].rearrange("p i (m t) -> p m i t", t=4)
             who = CAST[4 * b + 2 * a + h]
             if who == "S":
@@ -134,10 +141,26 @@ def tile_list_gmlpt_gelu_tsL_kernel(tc, tab_words, tab_scales, wg_words, wg_scal
             else:
                 nc.gpsimd.tensor_scalar(dst, src, 1.0, 0.0, MULT, ADD)
 
-        def quantize_wu(b, a):
-            nc.vector.quantize_mx(wu_w[b, a][:].bitcast(FP8X4), wu_s[b, a][:], wu_bf[b, a][:].rearrange("p t m i -> p (t m i)"))
+        def quantize_wu(b, a0, a1):
+            nc.vector.quantize_mx(
+                wu_w[b][:, a0:a1, :].rearrange("p a c -> p (a c)").bitcast(FP8X4),
+                wu_s[b][:, a0:a1, :].rearrange("p a c -> p (a c)"),
+                wu_bf[b][:, a0:a1, :, :, :].rearrange("p a t m i -> p (a t m i)"),
+            )
 
-        g = {(b, c): keep.tile([P, 2, 256, 2], F32, name="g%d%d" % (b, c), align_bytes=64) for b in range(2) for c in range(4)}
+        g = {}
+
+        def g_tile(b, c):
+            if (b, c) not in g:
+                for tag, members in TIES:
+                    if (b, c) in members:
+                        both = shared.tile([P, len(members), 2, 256, 2], F32, name="g%d%d" % (b, c), offset=place[tag], align_bytes=64)
+                        for x, key in enumerate(members):
+                            g[key] = both[:, x, :, :, :]
+            if (b, c) not in g:
+                own = keep.tile([P, 2, 256, 2], F32, name="g%d%d" % (b, c), align_bytes=64)
+                g[b, c] = own[:]
+            return g[b, c]
 
         def gate(b, c, u):
             cols = slice(256 * c, 256 * (c + 1))
@@ -155,7 +178,7 @@ def tile_list_gmlpt_gelu_tsL_kernel(tc, tab_words, tab_scales, wg_words, wg_scal
                             start=(a == 0),
                             stop=(a == 1),
                         )
-                nc.scalar.activation(g[b, c][:, u, :, :], bank[:].rearrange("p e j -> p j e"), GELU)
+                nc.scalar.activation(g_tile(b, c)[:, u, :, :], bank[:].rearrange("p e j -> p j e"), GELU)
 
         h_bf = [keep.tile([P, J, 4], BF16, name="h_bf%d" % b, align_bytes=64) for b in range(2)]
         h_w = [keep.tile([P, J], U32, name="h_w%d" % b, align_bytes=64) for b in range(2)]
@@ -169,8 +192,8 @@ def tile_list_gmlpt_gelu_tsL_kernel(tc, tab_words, tab_scales, wg_words, wg_scal
                     for a in range(2):
                         nc.tensor.matmul_mx(
                             bank[:, t, :],
-                            lhsT=wu_w[b, a][:, P * t : P * (t + 1)].bitcast(FP8X4),
-                            lhsT_scale=wu_s[b, a][:, P * t : P * (t + 1)],
+                            lhsT=wu_w[b][:, a, P * t : P * (t + 1)].bitcast(FP8X4),
+                            lhsT_scale=wu_s[b][:, a, P * t : P * (t + 1)],
                             rhs=v_w[a][:, cols].bitcast(FP8X4),
                             rhs_scale=v_s[4 * a : P, cols],
                             start=(a == 0),
@@ -201,7 +224,7 @@ def tile_list_gmlpt_gelu_tsL_kernel(tc, tab_words, tab_scales, wg_words, wg_scal
                         stop=(b == 1),
                     )
             res = keep.tile([P, 2, w], F32, name="res%d" % j0)
-            factor = ts_g[:, j0:j1].unsqueeze(1).to_broadcast([P, 2, w])
+            factor = ts_g[j0][0][:, ts_g[j0][1] : ts_g[j0][1] + w].unsqueeze(1).to_broadcast([P, 2, w])
             if j0 < GOUT:
                 y_sb = keep.tile([P, 2, w], F32, name="y_sb%d" % j0)
                 nc.scalar.copy(y_sb[:], bank[:])
@@ -218,7 +241,14 @@ def tile_list_gmlpt_gelu_tsL_kernel(tc, tab_words, tab_scales, wg_words, wg_scal
             elif kind == "g1":
                 gather(v_w[1], tab_w[1], *x)
             elif kind == "gt":
-                gather(ts_g, ts_all, *x)
+                j0, j1 = x
+                if j0 == TSTIE:
+                    picked = shared.tile([P, j1 - j0], F32, name="ts_g%d" % j0, offset=place["wu_bf0"], align_bytes=64)
+                else:
+                    picked = keep.tile([P, j1 - j0], F32, name="ts_g%d" % j0, align_bytes=64)
+                nc.vector.tensor_copy(picked[:], ts_all[:].indirect(offsets[:, j0 // 16 : j1 // 16]))
+                for j in range(j0, j1, P):
+                    ts_g[j] = (picked, j - j0)
             elif kind == "pw":
                 permute_wg(*x)
             elif kind == "ps":

@@ -18,14 +18,13 @@ MULT = mybir.AluOpType.mult
 
 ADD = mybir.AluOpType.add
 P = 128
-TIES = []
-TSTIE = 512
+OVER = {'ts_g512': 'wu_bf0', 'g10': 'wu_raw10', 'g11': 'wu_raw11'}
 GOUT = 0
 PERM = 'VVVV'
 BANKS = (5, 3)
 CAST = 'SSVVSSSS'
-LOADS = [('S', 'offs'), ('A', 'ts'), ('A', 'tabs'), ('A', 'wgs'), ('S', 'tab', 0), ('S', 'wg', 0, 0, 2), ('S', 'wu', 0, 0, 0, 2), ('S', 'tab', 1), ('S', 'wu', 0, 1, 0, 2), ('S', 'wg', 1, 0, 2), ('S', 'wu', 1, 0, 0, 2), ('S', 'wu', 1, 1, 0, 2), ('S', 'wd'), ('S', 'wds')]
-STEPS = [('g0', 0, 512), ('gs', 0, 512), ('pw', 0), ('ps', 0), ('g1', 0, 256), ('g1', 256, 512), ('g0', 512, 1024), ('gs', 512, 1024), ('g1', 512, 1024), ('cast', 0, 0, 0), ('cast', 0, 0, 1), ('cast', 0, 1, 0), ('cast', 0, 1, 1), ('qw', 0, 0, 2), ('gate', 0, 0, 0), ('gate', 0, 0, 1), ('up', 0, 0, 0), ('up', 0, 0, 1), ('gate', 0, 1, 0), ('gate', 0, 1, 1), ('gt', 0, 512), ('gt', 512, 1024), ('up', 0, 1, 0), ('up', 0, 1, 1), ('gate', 0, 2, 0), ('gate', 0, 2, 1), ('cast', 1, 0, 0), ('cast', 1, 0, 1), ('pw', 1), ('ps', 1), ('up', 0, 2, 0), ('gate', 0, 3, 0), ('gate', 0, 3, 1), ('up', 0, 2, 1), ('cast', 1, 1, 0), ('cast', 1, 1, 1), ('qw', 1, 0, 1), ('up', 0, 3, 0), ('gate', 1, 0, 0), ('gate', 1, 0, 1), ('qw', 1, 1, 2), ('up', 0, 3, 1), ('qh', 0, 0, 512), ('gate', 1, 1, 0), ('up', 1, 0, 0), ('gate', 1, 1, 1), ('up', 1, 0, 1), ('qh', 0, 512, 1024), ('gate', 1, 2, 0), ('up', 1, 1, 0), ('qh', 1, 0, 256), ('gate', 1, 2, 1), ('up', 1, 1, 1), ('gate', 1, 3, 0), ('down', 0, 256), ('up', 1, 2, 0), ('qh', 1, 256, 512), ('gate', 1, 3, 1), ('up', 1, 2, 1), ('down', 256, 512), ('up', 1, 3, 0), ('qh', 1, 512, 768), ('up', 1, 3, 1), ('qh', 1, 768, 896), ('down', 512, 768), ('qh', 1, 896, 1024), ('down', 768, 896), ('down', 896, 1024)]
+LOADS = [('S', 'wg', 0, 0, 2), ('S', 'tabs'), ('S', 'ts'), ('S', 'offs'), ('S', 'tab', 0), ('S', 'wgs'), ('S', 'wu', 0, 0, 0, 2), ('S', 'tab', 1), ('S', 'wu', 0, 1, 0, 2), ('S', 'wg', 1, 0, 2), ('S', 'wu', 1, 0, 0, 2), ('S', 'wu', 1, 1, 0, 2), ('S', 'wds'), ('S', 'wd')]
+STEPS = [('gs', 0, 1024), ('g0', 0, 1024), ('pw', 0), ('ps', 0), ('g1', 0, 256), ('g1', 256, 512), ('g1', 512, 1024), ('cast', 0, 0, 0), ('cast', 0, 0, 1), ('cast', 0, 1, 0), ('cast', 0, 1, 1), ('qw', 0, 0, 2), ('gate', 0, 0, 0), ('gate', 0, 0, 1), ('up', 0, 0, 0), ('up', 0, 0, 1), ('gate', 0, 1, 0), ('gate', 0, 1, 1), ('gt', 0, 512), ('gt', 512, 1024), ('up', 0, 1, 0), ('up', 0, 1, 1), ('gate', 0, 2, 0), ('gate', 0, 2, 1), ('cast', 1, 0, 0), ('cast', 1, 0, 1), ('pw', 1), ('ps', 1), ('up', 0, 2, 0), ('gate', 0, 3, 0), ('gate', 0, 3, 1), ('up', 0, 2, 1), ('cast', 1, 1, 0), ('cast', 1, 1, 1), ('qw', 1, 0, 1), ('up', 0, 3, 0), ('gate', 1, 0, 0), ('gate', 1, 0, 1), ('qw', 1, 1, 2), ('up', 0, 3, 1), ('qh', 0, 0, 512), ('gate', 1, 1, 0), ('up', 1, 0, 0), ('gate', 1, 1, 1), ('up', 1, 0, 1), ('qh', 0, 512, 1024), ('gate', 1, 2, 0), ('up', 1, 1, 0), ('qh', 1, 0, 256), ('gate', 1, 2, 1), ('up', 1, 1, 1), ('gate', 1, 3, 0), ('down', 0, 256), ('up', 1, 2, 0), ('qh', 1, 256, 512), ('gate', 1, 3, 1), ('up', 1, 2, 1), ('down', 256, 512), ('up', 1, 3, 0), ('qh', 1, 512, 768), ('up', 1, 3, 1), ('qh', 1, 768, 896), ('down', 512, 768), ('qh', 1, 896, 1024), ('down', 768, 896), ('down', 896, 1024)]
 
 
 def tile_list_gmlpt_gelu_tsL_kernel(tc, tab_words, tab_scales, wg_words, wg_scales, wu, wd_words, wd_scales, ts, offs, out):
@@ -33,7 +32,18 @@ def tile_list_gmlpt_gelu_tsL_kernel(tc, tab_words, tab_scales, wg_words, wg_scal
     with ExitStack() as ctx:
         keep = ctx.enter_context(tc.tile_pool(name="keep", bufs=1))
         shared = ctx.enter_context(tc.tile_pool(name="shared", bufs=1))
-        place = {"wu_raw00": 0, "wu_raw01": 8192, "wu_raw10": 16384, "wu_raw11": 24576, "wu_bf0": 32768, "wu_bf1": 40960}
+        place = {"wu_raw00": 0, "wu_raw01": 8192, "wu_raw10": 16384, "wu_raw11": 24576, "wu_bf0": 32768, "wu_bf1": 40960, "tab_w0": 49152, "tab_w1": 57344}
+        used = {}
+
+        def late_tile(shape, dtype, nbytes, name):
+            host = OVER.get(name)
+            if host is None:
+                return keep.tile(shape, dtype, name=name, align_bytes=64)
+            at = place[host] + used.get(host, 0)
+            used[host] = used.get(host, 0) + nbytes
+            assert used[host] <= 8192
+            return shared.tile(shape, dtype, name=name, offset=at, align_bytes=64)
+
         ps_g = ctx.enter_context(tc.psum_pool(name="ps_g", bufs=BANKS[0]))
         ps_u = ctx.enter_context(tc.psum_pool(name="ps_u", bufs=BANKS[1]))
 
@@ -49,7 +59,7 @@ def tile_list_gmlpt_gelu_tsL_kernel(tc, tab_words, tab_scales, wg_words, wg_scal
             for q in range(4):
                 queue.dma_start(plane[32 * q : 32 * q + 8, :].bitcast(I32), src[:, 4 * q : 4 * q + 4, :].bitcast(I32))
 
-        tab_w = [keep.tile([P, T], U32, name="tab_w%d" % a, align_bytes=64) for a in range(2)]
+        tab_w = [shared.tile([P, T], U32, name="tab_w%d" % a, offset=place["tab_w%d" % a], align_bytes=64) for a in range(2)]
         wg_raw = [keep.tile([P, 2, 512], I32, name="wg_raw%d" % b, align_bytes=64) for b in range(2)]
         wu_raw = {(b, a): shared.tile([P, 4, 512], F32, name="wu_raw%d%d" % (b, a), offset=place["wu_raw%d%d" % (b, a)], align_bytes=64) for b in range(2) for a in range(2)}
         wd_w = keep.tile([P, 2, N], U32, name="wd_w", align_bytes=64)
@@ -114,25 +124,27 @@ def tile_list_gmlpt_gelu_tsL_kernel(tc, tab_words, tab_scales, wg_words, wg_scal
         def gather(dst, window, j0, j1):
             nc.vector.tensor_copy(dst[:, j0:j1], window[:].indirect(offsets[:, j0 // 16 : j1 // 16]))
 
-        wg_w = [keep.tile([P, 2, 4, P], U32, name="wg_w%d" % b, align_bytes=64) for b in range(2)]
-        wg_s = keep.tile([P, 2, 4, P], U8, name="wg_s", align_bytes=64)
+        wg_w = {}
+        wg_s = {}
 
         def permute_wg(b):
+            wg_w[b] = late_tile([P, 2, 4, P], U32, 4096, "wg_w%d" % b)
             (nc.vector if PERM[b] == "V" else nc.gpsimd).tensor_copy(
                 wg_w[b][:].bitcast(I32).rearrange("p a t m -> p a m t"),
                 wg_raw[b][:].rearrange("p a (m t) -> p a m t", t=4),
             )
 
         def permute_scales(b):
-            (nc.vector if PERM[2 + b] == "V" else nc.gpsimd).tensor_copy(wg_s[:, b, :, :].rearrange("p t m -> p m t"), wg_s_raw[:, 512 * b : 512 * (b + 1)].rearrange("p (m t) -> p m t", t=4))
+            wg_s[b] = late_tile([P, 4, P], U8, 512, "wg_s%d" % b)
+            (nc.vector if PERM[2 + b] == "V" else nc.gpsimd).tensor_copy(wg_s[b][:], wg_s_raw[:, 512 * b : 512 * (b + 1)].rearrange("p (m t) -> p t m", t=4))
 
         wu_bf = [shared.tile([P, 2, 4, P, 4], BF16, name="wu_bf%d" % b, offset=place["wu_bf%d" % b], align_bytes=64) for b in range(2)]
         wu_w = [keep.tile([P, 2, 512], U32, name="wu_w%d" % b, align_bytes=64) for b in range(2)]
         wu_s = [keep.tile([P, 2, 512], U8, name="wu_s%d" % b, align_bytes=64) for b in range(2)]
 
         def cast_wu(b, a, h):
-            dst = wu_bf[b][:, a, :, 64 * h : 64 * (h + 1), :].rearrange("p t m i -> p m i t")
-            src = wu_raw[b, a][:, :, 256 * h : 256 * (h + 1)].rearrange("p i (m t) -> p m i t", t=4)
+            dst = wu_bf[b][:, a, 2 * h : 2 * (h + 1), :, :].rearrange("p t m i -> p m i t")
+            src = wu_raw[b, a][:].rearrange("p i (m t) -> p m i t", t=4)[:, :, :, 2 * h : 2 * (h + 1)]
             who = CAST[4 * b + 2 * a + h]
             if who == "S":
                 nc.scalar.copy(dst, src)
@@ -152,14 +164,7 @@ def tile_list_gmlpt_gelu_tsL_kernel(tc, tab_words, tab_scales, wg_words, wg_scal
 
         def g_tile(b, c):
             if (b, c) not in g:
-                for tag, members in TIES:
-                    if (b, c) in members:
-                        both = shared.tile([P, len(members), 2, 256, 2], F32, name="g%d%d" % (b, c), offset=place[tag], align_bytes=64)
-                        for x, key in enumerate(members):
-                            g[key] = both[:, x, :, :, :]
-            if (b, c) not in g:
-                own = keep.tile([P, 2, 256, 2], F32, name="g%d%d" % (b, c), align_bytes=64)
-                g[b, c] = own[:]
+                g[b, c] = late_tile([P, 2, 256, 2], F32, 4096, "g%d%d" % (b, c))
             return g[b, c]
 
         def gate(b, c, u):
@@ -172,7 +177,7 @@ def tile_list_gmlpt_gelu_tsL_kernel(tc, tab_words, tab_scales, wg_words, wg_scal
                         nc.tensor.matmul_mx(
                             bank[:, e, :],
                             lhsT=wg_w[b][:, a, t, :].bitcast(FP8X4),
-                            lhsT_scale=wg_s[4 * a : P, b, t, :],
+                            lhsT_scale=wg_s[b][4 * a : P, t, :],
                             rhs=v_w[a][:, cols].bitcast(FP8X4),
                             rhs_scale=v_s[4 * a : P, cols],
                             start=(a == 0),
@@ -242,10 +247,7 @@ def tile_list_gmlpt_gelu_tsL_kernel(tc, tab_words, tab_scales, wg_words, wg_scal
                 gather(v_w[1], tab_w[1], *x)
             elif kind == "gt":
                 j0, j1 = x
-                if j0 == TSTIE:
-                    picked = shared.tile([P, j1 - j0], F32, name="ts_g%d" % j0, offset=place["wu_bf0"], align_bytes=64)
-                else:
-                    picked = keep.tile([P, j1 - j0], F32, name="ts_g%d" % j0, align_bytes=64)
+                picked = late_tile([P, j1 - j0], F32, 4 * (j1 - j0), "ts_g%d" % j0)
                 nc.vector.tensor_copy(picked[:], ts_all[:].indirect(offsets[:, j0 // 16 : j1 // 16]))
                 for j in range(j0, j1, P):
                     ts_g[j] = (picked, j - j0)

@@ -18,12 +18,12 @@ MULT = mybir.AluOpType.mult
 
 ADD = mybir.AluOpType.add
 P = 128
-OVER = {'ts_g512': 'wu_bf0', 'g10': 'wu_raw10', 'g11': 'wu_raw11'}
+OVER = {'ts_g512': 'wu_bf0', 'wg_s0': 'tab_w0', 'wg_s1': 'tab_w0', 'g10': 'wu_raw10', 'g11': 'wu_raw11'}
 GOUT = 0
 PERM = 'VVVV'
 BANKS = (5, 3)
 CAST = 'SSVVSSSS'
-LOADS = [('S', 'wg', 0, 0, 2), ('S', 'tabs'), ('S', 'ts'), ('S', 'offs'), ('S', 'tab', 0), ('S', 'wgs'), ('S', 'wu', 0, 0, 0, 2), ('S', 'tab', 1), ('S', 'wu', 0, 1, 0, 2), ('S', 'wg', 1, 0, 2), ('S', 'wu', 1, 0, 0, 2), ('S', 'wu', 1, 1, 0, 2), ('S', 'wds'), ('S', 'wd')]
+LOADS = [('S', 'wg', 0, 0, 2), ('S', 'tabs'), ('S', 'ts'), ('S', 'offs'), ('S', 'tab', 0), ('G', 'wgs'), ('S', 'wu', 0, 0, 0, 2), ('S', 'tab', 1), ('S', 'wu', 0, 1, 0, 2), ('S', 'wg', 1, 0, 2), ('S', 'wu', 1, 0, 0, 2), ('S', 'wu', 1, 1, 0, 2), ('S', 'wds'), ('S', 'wd')]
 STEPS = [('gs', 0, 1024), ('g0', 0, 1024), ('pw', 0), ('ps', 0), ('g1', 0, 256), ('g1', 256, 512), ('g1', 512, 1024), ('cast', 0, 0, 0), ('cast', 0, 0, 1), ('cast', 0, 1, 0), ('cast', 0, 1, 1), ('qw', 0, 0, 2), ('gate', 0, 0, 0), ('gate', 0, 0, 1), ('up', 0, 0, 0), ('up', 0, 0, 1), ('gate', 0, 1, 0), ('gate', 0, 1, 1), ('gt', 0, 512), ('gt', 512, 1024), ('up', 0, 1, 0), ('up', 0, 1, 1), ('gate', 0, 2, 0), ('gate', 0, 2, 1), ('cast', 1, 0, 0), ('cast', 1, 0, 1), ('pw', 1), ('ps', 1), ('up', 0, 2, 0), ('gate', 0, 3, 0), ('gate', 0, 3, 1), ('up', 0, 2, 1), ('cast', 1, 1, 0), ('cast', 1, 1, 1), ('qw', 1, 0, 1), ('up', 0, 3, 0), ('gate', 1, 0, 0), ('gate', 1, 0, 1), ('qw', 1, 1, 2), ('up', 0, 3, 1), ('qh', 0, 0, 512), ('gate', 1, 1, 0), ('up', 1, 0, 0), ('gate', 1, 1, 1), ('up', 1, 0, 1), ('qh', 0, 512, 1024), ('gate', 1, 2, 0), ('up', 1, 1, 0), ('qh', 1, 0, 256), ('gate', 1, 2, 1), ('up', 1, 1, 1), ('gate', 1, 3, 0), ('down', 0, 256), ('up', 1, 2, 0), ('qh', 1, 256, 512), ('gate', 1, 3, 1), ('up', 1, 2, 1), ('down', 256, 512), ('up', 1, 3, 0), ('qh', 1, 512, 768), ('up', 1, 3, 1), ('qh', 1, 768, 896), ('down', 512, 768), ('qh', 1, 896, 1024), ('down', 768, 896), ('down', 896, 1024)]
 
 
@@ -55,9 +55,9 @@ def tile_list_gmlpt_gelu_tsL_kernel(tc, tab_words, tab_scales, wg_words, wg_scal
         for plane in (tab_s, wg_s_raw, wd_s):
             nc.vector.memset(plane[:].bitcast(I32), 0)
 
-        def load_scales(queue, plane, src):
+        def load_scales(queue, plane, src, c0, c1):
             for q in range(4):
-                queue.dma_start(plane[32 * q : 32 * q + 8, :].bitcast(I32), src[:, 4 * q : 4 * q + 4, :].bitcast(I32))
+                queue.dma_start(plane[32 * q : 32 * q + 8, c0:c1].bitcast(I32), src[:, 4 * q : 4 * q + 4, c0:c1].bitcast(I32))
 
         tab_w = [shared.tile([P, T], U32, name="tab_w%d" % a, offset=place["tab_w%d" % a], align_bytes=64) for a in range(2)]
         wg_raw = [keep.tile([P, 2, 512], I32, name="wg_raw%d" % b, align_bytes=64) for b in range(2)]
@@ -90,11 +90,11 @@ def tile_list_gmlpt_gelu_tsL_kernel(tc, tab_words, tab_scales, wg_words, wg_scal
             elif kind == "wd":
                 queue.dma_start(wd_w[:].bitcast(I32), wd_words.rearrange("a p n i -> p a (n i)").bitcast(I32))
             elif kind == "tabs":
-                load_scales(queue, tab_s, tab_scales)
+                load_scales(queue, tab_s, tab_scales, 0, T)
             elif kind == "wgs":
-                load_scales(queue, wg_s_raw, wg_scales)
+                load_scales(queue, wg_s_raw, wg_scales, *(x or (0, R)))
             elif kind == "wds":
-                load_scales(queue, wd_s, wd_scales)
+                load_scales(queue, wd_s, wd_scales, 0, N)
             elif kind == "tab":
                 load_tab(queue, *x)
             elif kind == "wg":
@@ -146,6 +146,10 @@ def tile_list_gmlpt_gelu_tsL_kernel(tc, tab_words, tab_scales, wg_words, wg_scal
             dst = wu_bf[b][:, a, 2 * h : 2 * (h + 1), :, :].rearrange("p t m i -> p m i t")
             src = wu_raw[b, a][:].rearrange("p i (m t) -> p m i t", t=4)[:, :, :, 2 * h : 2 * (h + 1)]
             who = CAST[4 * b + 2 * a + h]
+            if who in "sv":
+                who = {"s": "S", "v": "V"}[who]
+                dst = wu_bf[b][:, a, :, 64 * h : 64 * (h + 1), :].rearrange("p t m i -> p m i t")
+                src = wu_raw[b, a][:, :, 256 * h : 256 * (h + 1)].rearrange("p i (m t) -> p m i t", t=4)
             if who == "S":
                 nc.scalar.copy(dst, src)
             elif who == "V":

@@ -16,15 +16,9 @@ FP8X4 = mybir.dt.float8_e4m3fn_x4
 GELU = mybir.ActivationFunctionType.Gelu_apprx_tanh
 MULT = mybir.AluOpType.mult
 
-ADD = mybir.AluOpType.add
 P = 128
-OVER = {'ts_g512': 'wu_bf0', 'wg_s0': 'tab_w0', 'wg_s1': 'tab_w0', 'g10': 'wu_raw10', 'g11': 'wu_raw11'}
-GOUT = 0
-PERM = 'VVVV'
-BANKS = (5, 3)
-CAST = 'SSVVSSSS'
-LOADS = [('S', 'wg', 0, 0, 2), ('S', 'tabs'), ('S', 'ts'), ('S', 'offs'), ('S', 'tab', 0), ('G', 'wgs'), ('S', 'wu', 0, 0, 0, 2), ('S', 'tab', 1), ('S', 'wu', 0, 1, 0, 2), ('S', 'wg', 1, 0, 2), ('S', 'wu', 1, 0, 0, 2), ('S', 'wu', 1, 1, 0, 2), ('S', 'wds'), ('S', 'wd')]
-STEPS = [('gs', 0, 1024), ('g0', 0, 1024), ('pw', 0), ('ps', 0), ('g1', 0, 256), ('g1', 256, 512), ('g1', 512, 1024), ('cast', 0, 0, 0), ('cast', 0, 0, 1), ('cast', 0, 1, 0), ('cast', 0, 1, 1), ('qw', 0, 0, 2), ('gate', 0, 0, 0), ('gate', 0, 0, 1), ('up', 0, 0, 0), ('up', 0, 0, 1), ('gate', 0, 1, 0), ('gate', 0, 1, 1), ('gt', 0, 512), ('gt', 512, 1024), ('up', 0, 1, 0), ('up', 0, 1, 1), ('gate', 0, 2, 0), ('gate', 0, 2, 1), ('cast', 1, 0, 0), ('cast', 1, 0, 1), ('pw', 1), ('ps', 1), ('up', 0, 2, 0), ('gate', 0, 3, 0), ('gate', 0, 3, 1), ('up', 0, 2, 1), ('cast', 1, 1, 0), ('cast', 1, 1, 1), ('qw', 1, 0, 1), ('up', 0, 3, 0), ('gate', 1, 0, 0), ('gate', 1, 0, 1), ('qw', 1, 1, 2), ('up', 0, 3, 1), ('qh', 0, 0, 512), ('gate', 1, 1, 0), ('up', 1, 0, 0), ('gate', 1, 1, 1), ('up', 1, 0, 1), ('qh', 0, 512, 1024), ('gate', 1, 2, 0), ('up', 1, 1, 0), ('qh', 1, 0, 256), ('gate', 1, 2, 1), ('up', 1, 1, 1), ('gate', 1, 3, 0), ('down', 0, 256), ('up', 1, 2, 0), ('qh', 1, 256, 512), ('gate', 1, 3, 1), ('up', 1, 2, 1), ('down', 256, 512), ('up', 1, 3, 0), ('qh', 1, 512, 768), ('up', 1, 3, 1), ('qh', 1, 768, 896), ('down', 512, 768), ('qh', 1, 896, 1024), ('down', 768, 896), ('down', 896, 1024)]
+GATE_BANKS = 5
+UP_BANKS = 3
 
 
 def tile_list_gmlpt_gelu_tsL_kernel(tc, tab_words, tab_scales, wg_words, wg_scales, wu, wd_words, wd_scales, ts, offs, out):
@@ -33,19 +27,8 @@ def tile_list_gmlpt_gelu_tsL_kernel(tc, tab_words, tab_scales, wg_words, wg_scal
         keep = ctx.enter_context(tc.tile_pool(name="keep", bufs=1))
         shared = ctx.enter_context(tc.tile_pool(name="shared", bufs=1))
         place = {"wu_raw00": 0, "wu_raw01": 8192, "wu_raw10": 16384, "wu_raw11": 24576, "wu_bf0": 32768, "wu_bf1": 40960, "tab_w0": 49152, "tab_w1": 57344}
-        used = {}
-
-        def late_tile(shape, dtype, nbytes, name):
-            host = OVER.get(name)
-            if host is None:
-                return keep.tile(shape, dtype, name=name, align_bytes=64)
-            at = place[host] + used.get(host, 0)
-            used[host] = used.get(host, 0) + nbytes
-            assert used[host] <= 8192
-            return shared.tile(shape, dtype, name=name, offset=at, align_bytes=64)
-
-        ps_g = ctx.enter_context(tc.psum_pool(name="ps_g", bufs=BANKS[0]))
-        ps_u = ctx.enter_context(tc.psum_pool(name="ps_u", bufs=BANKS[1]))
+        ps_g = ctx.enter_context(tc.psum_pool(name="ps_g", bufs=GATE_BANKS))
+        ps_u = ctx.enter_context(tc.psum_pool(name="ps_u", bufs=UP_BANKS))
 
         offsets = keep.tile([P, J // 16], U16, name="offsets")
 
@@ -55,9 +38,9 @@ def tile_list_gmlpt_gelu_tsL_kernel(tc, tab_words, tab_scales, wg_words, wg_scal
         for plane in (tab_s, wg_s_raw, wd_s):
             nc.vector.memset(plane[:].bitcast(I32), 0)
 
-        def load_scales(queue, plane, src, c0, c1):
+        def load_scales(queue, plane, src):
             for q in range(4):
-                queue.dma_start(plane[32 * q : 32 * q + 8, c0:c1].bitcast(I32), src[:, 4 * q : 4 * q + 4, c0:c1].bitcast(I32))
+                queue.dma_start(plane[32 * q : 32 * q + 8, :].bitcast(I32), src[:, 4 * q : 4 * q + 4, :].bitcast(I32))
 
         tab_w = [shared.tile([P, T], U32, name="tab_w%d" % a, offset=place["tab_w%d" % a], align_bytes=64) for a in range(2)]
         wg_raw = [keep.tile([P, 2, 512], I32, name="wg_raw%d" % b, align_bytes=64) for b in range(2)]
@@ -66,44 +49,32 @@ def tile_list_gmlpt_gelu_tsL_kernel(tc, tab_words, tab_scales, wg_words, wg_scal
         ts_all = keep.tile([P, T], F32, name="ts_all", align_bytes=64)
         wg_src = wg_words.rearrange("a p r i -> p a (r i)")
 
-        def load_tab(queue, a):
-            queue.dma_start(tab_w[a][:].bitcast(I32), tab_words[a].rearrange("p t i -> p (t i)").bitcast(I32))
-
-        def load_wg(queue, b, a0, a1):
-            queue.dma_start(wg_raw[b][:, a0:a1, :], wg_src[:, a0:a1, 2048 * b : 2048 * (b + 1)].bitcast(I32))
-
-        def load_wu(queue, b, a, h0, h1):
-            if True:
-                src = wu[512 * a : 512 * (a + 1), 512 * b + 256 * h0 : 512 * b + 256 * h1]
-                queue.dma_start(wu_raw[b, a][:, :, 256 * h0 : 256 * h1], src.rearrange("(p i) c -> p i c", i=4))
-
         ts_row = keep.tile([P, 16], F32, name="ts_row", align_bytes=64)
 
-        queues = {"S": nc.sync, "A": nc.scalar, "G": nc.gpsimd}
+        def load_tab(a):
+            nc.sync.dma_start(tab_w[a][:].bitcast(I32), tab_words[a].rearrange("p t i -> p (t i)").bitcast(I32))
 
-        def load(queue, kind, *x):
-            queue = queues[queue]
-            if kind == "offs":
-                nc.sync.dma_start(offsets[:], offs)
-            elif kind == "ts":
-                queue.dma_start(ts_row[:], ts[0].rearrange("(p c) -> p c", c=16))
-            elif kind == "wd":
-                queue.dma_start(wd_w[:].bitcast(I32), wd_words.rearrange("a p n i -> p a (n i)").bitcast(I32))
-            elif kind == "tabs":
-                load_scales(queue, tab_s, tab_scales, 0, T)
-            elif kind == "wgs":
-                load_scales(queue, wg_s_raw, wg_scales, *(x or (0, R)))
-            elif kind == "wds":
-                load_scales(queue, wd_s, wd_scales, 0, N)
-            elif kind == "tab":
-                load_tab(queue, *x)
-            elif kind == "wg":
-                load_wg(queue, *x)
-            else:
-                load_wu(queue, *x)
+        def load_wg(b):
+            nc.sync.dma_start(wg_raw[b][:], wg_src[:, :, 2048 * b : 2048 * (b + 1)].bitcast(I32))
 
-        for item in LOADS:
-            load(*item)
+        def load_wu(b, a):
+            src = wu[512 * a : 512 * (a + 1), 512 * b : 512 * (b + 1)]
+            nc.sync.dma_start(wu_raw[b, a][:], src.rearrange("(p i) c -> p i c", i=4))
+
+        load_wg(0)
+        load_scales(nc.sync, tab_s, tab_scales)
+        nc.sync.dma_start(ts_row[:], ts[0].rearrange("(p c) -> p c", c=16))
+        nc.sync.dma_start(offsets[:], offs)
+        load_tab(0)
+        load_scales(nc.gpsimd, wg_s_raw, wg_scales)
+        load_wu(0, 0)
+        load_tab(1)
+        load_wu(0, 1)
+        load_wg(1)
+        load_wu(1, 0)
+        load_wu(1, 1)
+        load_scales(nc.sync, wd_s, wd_scales)
+        nc.sync.dma_start(wd_w[:].bitcast(I32), wd_words.rearrange("a p n i -> p a (n i)").bitcast(I32))
 
         warm = keep.tile([P, 8], F32, name="warm")
         nc.vector.memset(warm[:], 0.0)
@@ -119,24 +90,28 @@ def tile_list_gmlpt_gelu_tsL_kernel(tc, tab_words, tab_scales, wg_words, wg_scal
 
         v_w = [keep.tile([P, J], U32, name="v_w%d" % a, align_bytes=64) for a in range(2)]
         v_s = keep.tile([P, J], U8, name="v_s", align_bytes=64)
-        ts_g = {}
+        ts_g = [
+            keep.tile([P, 512], F32, name="ts_g0", align_bytes=64),
+            shared.tile([P, 512], F32, name="ts_g1", offset=place["wu_bf0"], align_bytes=64),
+        ]
 
         def gather(dst, window, j0, j1):
             nc.vector.tensor_copy(dst[:, j0:j1], window[:].indirect(offsets[:, j0 // 16 : j1 // 16]))
 
-        wg_w = {}
-        wg_s = {}
+        def gather_ts(half):
+            nc.vector.tensor_copy(ts_g[half][:], ts_all[:].indirect(offsets[:, 32 * half : 32 * (half + 1)]))
 
-        def permute_wg(b):
-            wg_w[b] = late_tile([P, 2, 4, P], U32, 4096, "wg_w%d" % b)
-            (nc.vector if PERM[b] == "V" else nc.gpsimd).tensor_copy(
+        wg_w = [keep.tile([P, 2, 4, P], U32, name="wg_w%d" % b, align_bytes=64) for b in range(2)]
+        wg_s = [shared.tile([P, 4, P], U8, name="wg_s%d" % b, offset=place["tab_w0"] + 512 * b, align_bytes=64) for b in range(2)]
+
+        def deal_wg(b):
+            nc.vector.tensor_copy(
                 wg_w[b][:].bitcast(I32).rearrange("p a t m -> p a m t"),
                 wg_raw[b][:].rearrange("p a (m t) -> p a m t", t=4),
             )
 
-        def permute_scales(b):
-            wg_s[b] = late_tile([P, 4, P], U8, 512, "wg_s%d" % b)
-            (nc.vector if PERM[2 + b] == "V" else nc.gpsimd).tensor_copy(wg_s[b][:], wg_s_raw[:, 512 * b : 512 * (b + 1)].rearrange("p (m t) -> p t m", t=4))
+        def deal_scales(b):
+            nc.vector.tensor_copy(wg_s[b][:], wg_s_raw[:, 512 * b : 512 * (b + 1)].rearrange("p (m t) -> p t m", t=4))
 
         wu_bf = [shared.tile([P, 2, 4, P, 4], BF16, name="wu_bf%d" % b, offset=place["wu_bf%d" % b], align_bytes=64) for b in range(2)]
         wu_w = [keep.tile([P, 2, 512], U32, name="wu_w%d" % b, align_bytes=64) for b in range(2)]
@@ -145,17 +120,10 @@ def tile_list_gmlpt_gelu_tsL_kernel(tc, tab_words, tab_scales, wg_words, wg_scal
         def cast_wu(b, a, h):
             dst = wu_bf[b][:, a, 2 * h : 2 * (h + 1), :, :].rearrange("p t m i -> p m i t")
             src = wu_raw[b, a][:].rearrange("p i (m t) -> p m i t", t=4)[:, :, :, 2 * h : 2 * (h + 1)]
-            who = CAST[4 * b + 2 * a + h]
-            if who in "sv":
-                who = {"s": "S", "v": "V"}[who]
-                dst = wu_bf[b][:, a, :, 64 * h : 64 * (h + 1), :].rearrange("p t m i -> p m i t")
-                src = wu_raw[b, a][:, :, 256 * h : 256 * (h + 1)].rearrange("p i (m t) -> p m i t", t=4)
-            if who == "S":
-                nc.scalar.copy(dst, src)
-            elif who == "V":
+            if (b, a) == (0, 1):
                 nc.vector.tensor_copy(dst, src)
             else:
-                nc.gpsimd.tensor_scalar(dst, src, 1.0, 0.0, MULT, ADD)
+                nc.scalar.copy(dst, src)
 
         def quantize_wu(b, a0, a1):
             nc.vector.quantize_mx(
@@ -165,55 +133,54 @@ def tile_list_gmlpt_gelu_tsL_kernel(tc, tab_words, tab_scales, wg_words, wg_scal
             )
 
         g = {}
-
-        def g_tile(b, c):
-            if (b, c) not in g:
-                g[b, c] = late_tile([P, 2, 256, 2], F32, 4096, "g%d%d" % (b, c))
-            return g[b, c]
+        for b in range(2):
+            for c in range(4):
+                if b == 1 and c < 2:
+                    g[b, c] = shared.tile([P, 2, 256, 2], F32, name="g1%d" % c, offset=place["wu_raw1%d" % c], align_bytes=64)
+                else:
+                    g[b, c] = keep.tile([P, 2, 256, 2], F32, name="g%d%d" % (b, c), align_bytes=64)
 
         def gate(b, c, u):
             cols = slice(256 * c, 256 * (c + 1))
-            if True:
-                bank = ps_g.tile([P, 2, 256], F32, name="ga")
-                for e in range(2):
-                    t = 2 * u + e
-                    for a in range(2):
-                        nc.tensor.matmul_mx(
-                            bank[:, e, :],
-                            lhsT=wg_w[b][:, a, t, :].bitcast(FP8X4),
-                            lhsT_scale=wg_s[b][4 * a : P, t, :],
-                            rhs=v_w[a][:, cols].bitcast(FP8X4),
-                            rhs_scale=v_s[4 * a : P, cols],
-                            start=(a == 0),
-                            stop=(a == 1),
-                        )
-                nc.scalar.activation(g_tile(b, c)[:, u, :, :], bank[:].rearrange("p e j -> p j e"), GELU)
+            bank = ps_g.tile([P, 2, 256], F32, name="ga")
+            for e in range(2):
+                t = 2 * u + e
+                for a in range(2):
+                    nc.tensor.matmul_mx(
+                        bank[:, e, :],
+                        lhsT=wg_w[b][:, a, t, :].bitcast(FP8X4),
+                        lhsT_scale=wg_s[b][4 * a : P, t, :],
+                        rhs=v_w[a][:, cols].bitcast(FP8X4),
+                        rhs_scale=v_s[4 * a : P, cols],
+                        start=(a == 0),
+                        stop=(a == 1),
+                    )
+            nc.scalar.activation(g[b, c][:, u, :, :], bank[:].rearrange("p e j -> p j e"), GELU)
 
         h_bf = [keep.tile([P, J, 4], BF16, name="h_bf%d" % b, align_bytes=64) for b in range(2)]
         h_w = [keep.tile([P, J], U32, name="h_w%d" % b, align_bytes=64) for b in range(2)]
         h_s = [keep.tile([P, J], U8, name="h_s%d" % b, align_bytes=64) for b in range(2)]
 
         def up(b, c, d):
-            if True:
-                cols = slice(256 * c + P * d, 256 * c + P * (d + 1))
-                bank = ps_u.tile([P, 4, P], F32, name="ub")
-                for t in range(4):
-                    for a in range(2):
-                        nc.tensor.matmul_mx(
-                            bank[:, t, :],
-                            lhsT=wu_w[b][:, a, P * t : P * (t + 1)].bitcast(FP8X4),
-                            lhsT_scale=wu_s[b][:, a, P * t : P * (t + 1)],
-                            rhs=v_w[a][:, cols].bitcast(FP8X4),
-                            rhs_scale=v_s[4 * a : P, cols],
-                            start=(a == 0),
-                            stop=(a == 1),
-                        )
-                nc.vector.tensor_tensor(
-                    h_bf[b][:, cols, :].rearrange("p j (u e) -> p j u e", u=2),
-                    bank[:].rearrange("p (u e) j -> p j u e", u=2),
-                    g[b, c][:, :, P * d : P * (d + 1), :].rearrange("p u j e -> p j u e"),
-                    MULT,
-                )
+            cols = slice(256 * c + P * d, 256 * c + P * (d + 1))
+            bank = ps_u.tile([P, 4, P], F32, name="ub")
+            for t in range(4):
+                for a in range(2):
+                    nc.tensor.matmul_mx(
+                        bank[:, t, :],
+                        lhsT=wu_w[b][:, a, P * t : P * (t + 1)].bitcast(FP8X4),
+                        lhsT_scale=wu_s[b][:, a, P * t : P * (t + 1)],
+                        rhs=v_w[a][:, cols].bitcast(FP8X4),
+                        rhs_scale=v_s[4 * a : P, cols],
+                        start=(a == 0),
+                        stop=(a == 1),
+                    )
+            nc.vector.tensor_tensor(
+                h_bf[b][:, cols, :].rearrange("p j (u e) -> p j u e", u=2),
+                bank[:].rearrange("p (u e) j -> p j u e", u=2),
+                g[b, c][:, :, P * d : P * (d + 1), :].rearrange("p u j e -> p j u e"),
+                MULT,
+            )
 
         def quantize_h(b, j0, j1):
             nc.vector.quantize_mx(h_w[b][:, j0:j1].bitcast(FP8X4), h_s[b][:, j0:j1], h_bf[b][:, j0:j1, :].rearrange("p j t -> p (j t)"))
@@ -221,20 +188,20 @@ def tile_list_gmlpt_gelu_tsL_kernel(tc, tab_words, tab_scales, wg_words, wg_scal
         def down(j0, j1):
             w = j1 - j0
             bank = ps_g.tile([P, 2, w], F32, name="ga")
-            for n in range(2):
-                for b in range(2):
+            for b in range(2):
+                for n in range(2):
                     nc.tensor.matmul_mx(
                         bank[:, n, :],
                         lhsT=wd_w[:, b, P * n : P * (n + 1)].bitcast(FP8X4),
                         lhsT_scale=wd_s[4 * b : P, P * n : P * (n + 1)],
                         rhs=h_w[b][:, j0:j1].bitcast(FP8X4),
                         rhs_scale=h_s[b][:, j0:j1],
-                        start=(b == 0),
-                        stop=(b == 1),
+                        start=(b == 0 and n == 0),
+                        stop=(b == 1 and n == 1),
                     )
             res = keep.tile([P, 2, w], F32, name="res%d" % j0)
-            factor = ts_g[j0][0][:, ts_g[j0][1] : ts_g[j0][1] + w].unsqueeze(1).to_broadcast([P, 2, w])
-            if j0 < GOUT:
+            factor = ts_g[j0 // 512][:, j0 % 512 : j0 % 512 + w].unsqueeze(1).to_broadcast([P, 2, w])
+            if j0 < 512:
                 y_sb = keep.tile([P, 2, w], F32, name="y_sb%d" % j0)
                 nc.scalar.copy(y_sb[:], bank[:])
                 nc.gpsimd.tensor_tensor(res[:], y_sb[:], factor, MULT)
@@ -242,35 +209,49 @@ def tile_list_gmlpt_gelu_tsL_kernel(tc, tab_words, tab_scales, wg_words, wg_scal
                 nc.vector.tensor_tensor(res[:], bank[:], factor, MULT)
             nc.sync.dma_start(out[:, j0:j1].rearrange("(n p) j -> p n j", p=P), res[:])
 
-        def step(kind, *x):
-            if kind == "gs":
-                gather(v_s, tab_s, *x)
-            elif kind == "g0":
-                gather(v_w[0], tab_w[0], *x)
-            elif kind == "g1":
-                gather(v_w[1], tab_w[1], *x)
-            elif kind == "gt":
-                j0, j1 = x
-                picked = late_tile([P, j1 - j0], F32, 4 * (j1 - j0), "ts_g%d" % j0)
-                nc.vector.tensor_copy(picked[:], ts_all[:].indirect(offsets[:, j0 // 16 : j1 // 16]))
-                for j in range(j0, j1, P):
-                    ts_g[j] = (picked, j - j0)
-            elif kind == "pw":
-                permute_wg(*x)
-            elif kind == "ps":
-                permute_scales(*x)
-            elif kind == "cast":
-                cast_wu(*x)
-            elif kind == "qw":
-                quantize_wu(*x)
-            elif kind == "gate":
-                gate(*x)
-            elif kind == "up":
-                up(*x)
-            elif kind == "qh":
-                quantize_h(*x)
-            else:
-                down(*x)
-
-        for item in STEPS:
-            step(*item)
+        gather(v_s, tab_s, 0, J)
+        gather(v_w[0], tab_w[0], 0, J)
+        deal_wg(0)
+        deal_scales(0)
+        for j0, j1 in ((0, 256), (256, 512), (512, J)):
+            gather(v_w[1], tab_w[1], j0, j1)
+        for a in range(2):
+            for h in range(2):
+                cast_wu(0, a, h)
+        quantize_wu(0, 0, 2)
+        for half in range(2):
+            gather_ts(half)
+        deal_wg(1)
+        deal_scales(1)
+        for u in range(2):
+            gate(0, 0, u)
+        for c in range(4):
+            if c < 3:
+                for u in range(2):
+                    gate(0, c + 1, u)
+            for d in range(2):
+                up(0, c, d)
+            if c in (1, 2):
+                for h in range(2):
+                    cast_wu(1, c - 1, h)
+        for a in range(2):
+            quantize_wu(1, a, a + 1)
+        for c in range(2):
+            for u in range(2):
+                gate(1, c, u)
+        for c in range(4):
+            for d in range(2):
+                if c < 2:
+                    gate(1, c + 2, d)
+                if c == 0:
+                    quantize_h(0, 512 * d, 512 * (d + 1))
+                elif d == 0 and c > 1:
+                    down(256 * (c - 2), 256 * (c - 1))
+                up(1, c, d)
+                if c > 0 and d == 0:
+                    quantize_h(1, 256 * (c - 1), 256 * c)
+        quantize_h(1, 768, 896)
+        down(512, 768)
+        quantize_h(1, 896, J)
+        down(768, 896)
+        down(896, J)

@@ -17,8 +17,9 @@ GELU = mybir.ActivationFunctionType.Gelu_apprx_tanh
 MULT = mybir.AluOpType.mult
 
 P = 128
-GATE_BANKS = 5
-UP_BANKS = 3
+GATE_BANK = [[0, 1, 2, 3, 4, 5, 6, 7], [3, 4, 5, 6, 0, 3, 4, 5]]
+UP_BANK = [[0, 1, 2, 7, 1, 2, 7, 1], [2, 7, 1, 2, 7, 1, 2, 7]]
+DOWN_BANK = {0: 6, 256: 0, 512: 3, 768: 4, 896: 5}
 
 
 def tile_list_gmlpt_gelu_tsL_kernel(tc, tab_words, tab_scales, wg_words, wg_scales, wu, wd_words, wd_scales, ts, offs, out):
@@ -26,14 +27,16 @@ def tile_list_gmlpt_gelu_tsL_kernel(tc, tab_words, tab_scales, wg_words, wg_scal
     with ExitStack() as ctx:
         keep = ctx.enter_context(tc.tile_pool(name="keep", bufs=1))
         shared = ctx.enter_context(tc.tile_pool(name="shared", bufs=1))
-        place = {"wu_raw00": 0, "wu_raw01": 8192, "wu_raw10": 16384, "wu_raw11": 24576, "wu_bf0": 32768, "wu_bf1": 40960, "tab_w0": 49152, "tab_w1": 57344}
-        ps_g = ctx.enter_context(tc.psum_pool(name="ps_g", bufs=GATE_BANKS))
-        ps_u = ctx.enter_context(tc.psum_pool(name="ps_u", bufs=UP_BANKS))
+        place = {"wu_raw00": 0, "wu_raw01": 8192, "wu_raw10": 16384, "wu_raw11": 24576, "wu_bf0": 32768, "wu_bf1": 40960, "tab_w0": 49152, "tab_w1": 57344, "wg_s_raw": 65536, "wg_raw0": 66560, "wg_raw1": 70656}
+        psum = ctx.enter_context(tc.psum_pool(name="psum", bufs=1))
+
+        def in_bank(number, shape):
+            return psum.tile(shape, F32, name="bank%d" % number)
 
         offsets = keep.tile([P, J // 16], U16, name="offsets")
 
         tab_s = keep.tile([P, T], U8, name="tab_s", align_bytes=64)
-        wg_s_raw = keep.tile([P, R], U8, name="wg_s_raw", align_bytes=64)
+        wg_s_raw = shared.tile([P, R], U8, name="wg_s_raw", offset=place["wg_s_raw"], align_bytes=64)
         wd_s = keep.tile([P, N], U8, name="wd_s", align_bytes=64)
         for plane in (tab_s, wg_s_raw, wd_s):
             nc.vector.memset(plane[:].bitcast(I32), 0)
@@ -43,7 +46,7 @@ def tile_list_gmlpt_gelu_tsL_kernel(tc, tab_words, tab_scales, wg_words, wg_scal
                 queue.dma_start(plane[32 * q : 32 * q + 8, :].bitcast(I32), src[:, 4 * q : 4 * q + 4, :].bitcast(I32))
 
         tab_w = [shared.tile([P, T], U32, name="tab_w%d" % a, offset=place["tab_w%d" % a], align_bytes=64) for a in range(2)]
-        wg_raw = [keep.tile([P, 2, 512], I32, name="wg_raw%d" % b, align_bytes=64) for b in range(2)]
+        wg_raw = [shared.tile([P, 2, 512], I32, name="wg_raw%d" % b, offset=place["wg_raw%d" % b], align_bytes=64) for b in range(2)]
         wu_raw = {(b, a): shared.tile([P, 4, 512], F32, name="wu_raw%d%d" % (b, a), offset=place["wu_raw%d%d" % (b, a)], align_bytes=64) for b in range(2) for a in range(2)}
         wd_w = keep.tile([P, 2, N], U32, name="wd_w", align_bytes=64)
         ts_all = keep.tile([P, T], F32, name="ts_all", align_bytes=64)
@@ -61,16 +64,16 @@ def tile_list_gmlpt_gelu_tsL_kernel(tc, tab_words, tab_scales, wg_words, wg_scal
             src = wu[512 * a : 512 * (a + 1), 512 * b : 512 * (b + 1)]
             nc.sync.dma_start(wu_raw[b, a][:], src.rearrange("(p i) c -> p i c", i=4))
 
-        load_wg(0)
-        load_scales(nc.sync, tab_s, tab_scales)
-        nc.sync.dma_start(ts_row[:], ts[0].rearrange("(p c) -> p c", c=16))
         nc.sync.dma_start(offsets[:], offs)
+        nc.sync.dma_start(ts_row[:], ts[0].rearrange("(p c) -> p c", c=16))
+        load_scales(nc.sync, tab_s, tab_scales)
+        load_wg(0)
+        load_scales(nc.sync, wg_s_raw, wg_scales)
         load_tab(0)
-        load_scales(nc.gpsimd, wg_s_raw, wg_scales)
         load_wu(0, 0)
         load_tab(1)
-        load_wu(0, 1)
         load_wg(1)
+        load_wu(0, 1)
         load_wu(1, 0)
         load_wu(1, 1)
         load_scales(nc.sync, wd_s, wd_scales)
@@ -83,26 +86,20 @@ def tile_list_gmlpt_gelu_tsL_kernel(tc, tab_words, tab_scales, wg_words, wg_scal
         ident = keep.tile([P, P], F32, name="ident", align_bytes=64)
         make_identity(nc, ident[:])
         for c0 in range(0, 16, 4):
-            bank = ps_g.tile([P, 4, P], F32, name="ga")
+            bank = in_bank(4 + c0 // 4, [P, 4, P])
             for c in range(4):
                 nc.tensor.transpose(bank[:, c, :], ts_row[:, c0 + c : c0 + c + 1].to_broadcast([P, P]), ident[:])
             nc.scalar.copy(ts_all[:].rearrange("q (p c) -> q p c", c=16)[:, :, c0 : c0 + 4], bank[:].rearrange("q c p -> q p c"))
 
         v_w = [keep.tile([P, J], U32, name="v_w%d" % a, align_bytes=64) for a in range(2)]
         v_s = keep.tile([P, J], U8, name="v_s", align_bytes=64)
-        ts_g = [
-            keep.tile([P, 512], F32, name="ts_g0", align_bytes=64),
-            shared.tile([P, 512], F32, name="ts_g1", offset=place["wu_bf0"], align_bytes=64),
-        ]
+        ts_g = shared.tile([P, J], F32, name="ts_g", offset=place["tab_w0"], align_bytes=64)
 
         def gather(dst, window, j0, j1):
             nc.vector.tensor_copy(dst[:, j0:j1], window[:].indirect(offsets[:, j0 // 16 : j1 // 16]))
 
-        def gather_ts(half):
-            nc.vector.tensor_copy(ts_g[half][:], ts_all[:].indirect(offsets[:, 32 * half : 32 * (half + 1)]))
-
         wg_w = [keep.tile([P, 2, 4, P], U32, name="wg_w%d" % b, align_bytes=64) for b in range(2)]
-        wg_s = [shared.tile([P, 4, P], U8, name="wg_s%d" % b, offset=place["tab_w0"] + 512 * b, align_bytes=64) for b in range(2)]
+        wg_s = keep.tile([P, 2, 4, P], U8, name="wg_s", align_bytes=64)
 
         def deal_wg(b):
             nc.vector.tensor_copy(
@@ -110,11 +107,14 @@ def tile_list_gmlpt_gelu_tsL_kernel(tc, tab_words, tab_scales, wg_words, wg_scal
                 wg_raw[b][:].rearrange("p a (m t) -> p a m t", t=4),
             )
 
-        def deal_scales(b):
-            nc.vector.tensor_copy(wg_s[b][:], wg_s_raw[:, 512 * b : 512 * (b + 1)].rearrange("p (m t) -> p t m", t=4))
+        def deal_scales():
+            nc.vector.tensor_copy(wg_s[:], wg_s_raw[:].rearrange("p (b m t) -> p b t m", b=2, t=4))
 
         wu_bf = [shared.tile([P, 2, 4, P, 4], BF16, name="wu_bf%d" % b, offset=place["wu_bf%d" % b], align_bytes=64) for b in range(2)]
-        wu_w = [keep.tile([P, 2, 512], U32, name="wu_w%d" % b, align_bytes=64) for b in range(2)]
+        wu_w = [
+            shared.tile([P, 2, 512], U32, name="wu_w0", offset=place["tab_w1"], align_bytes=64),
+            keep.tile([P, 2, 512], U32, name="wu_w1", align_bytes=64),
+        ]
         wu_s = [keep.tile([P, 2, 512], U8, name="wu_s%d" % b, align_bytes=64) for b in range(2)]
 
         def cast_wu(b, a, h):
@@ -140,22 +140,30 @@ def tile_list_gmlpt_gelu_tsL_kernel(tc, tab_words, tab_scales, wg_words, wg_scal
                 else:
                     g[b, c] = keep.tile([P, 2, 256, 2], F32, name="g%d%d" % (b, c), align_bytes=64)
 
-        def gate(b, c, u):
+        gate_bank = {}
+
+        def gate_pass(b, c, u, a):
             cols = slice(256 * c, 256 * (c + 1))
-            bank = ps_g.tile([P, 2, 256], F32, name="ga")
+            if a == 0:
+                gate_bank[b, c, u] = in_bank(GATE_BANK[b][2 * c + u], [P, 2, 256])
+            bank = gate_bank[b, c, u]
             for e in range(2):
                 t = 2 * u + e
-                for a in range(2):
-                    nc.tensor.matmul_mx(
-                        bank[:, e, :],
-                        lhsT=wg_w[b][:, a, t, :].bitcast(FP8X4),
-                        lhsT_scale=wg_s[b][4 * a : P, t, :],
-                        rhs=v_w[a][:, cols].bitcast(FP8X4),
-                        rhs_scale=v_s[4 * a : P, cols],
-                        start=(a == 0),
-                        stop=(a == 1),
-                    )
-            nc.scalar.activation(g[b, c][:, u, :, :], bank[:].rearrange("p e j -> p j e"), GELU)
+                nc.tensor.matmul_mx(
+                    bank[:, e, :],
+                    lhsT=wg_w[b][:, a, t, :].bitcast(FP8X4),
+                    lhsT_scale=wg_s[4 * a : P, b, t, :],
+                    rhs=v_w[a][:, cols].bitcast(FP8X4),
+                    rhs_scale=v_s[4 * a : P, cols],
+                    start=(a == 0 and e == 0),
+                    stop=(a == 1 and e == 1),
+                )
+            if a == 1:
+                nc.scalar.activation(g[b, c][:, u, :, :], bank[:].rearrange("p e j -> p j e"), GELU)
+
+        def gate(b, c, u):
+            for a in range(2):
+                gate_pass(b, c, u, a)
 
         h_bf = [keep.tile([P, J, 4], BF16, name="h_bf%d" % b, align_bytes=64) for b in range(2)]
         h_w = [keep.tile([P, J], U32, name="h_w%d" % b, align_bytes=64) for b in range(2)]
@@ -163,17 +171,18 @@ def tile_list_gmlpt_gelu_tsL_kernel(tc, tab_words, tab_scales, wg_words, wg_scal
 
         def up(b, c, d):
             cols = slice(256 * c + P * d, 256 * c + P * (d + 1))
-            bank = ps_u.tile([P, 4, P], F32, name="ub")
-            for t in range(4):
-                for a in range(2):
+            bank = in_bank(UP_BANK[b][2 * c + d], [P, 4, P])
+            passes = (0, 1) if 2 * c + d < 3 else (1, 0)
+            for a in passes:
+                for t in range(4):
                     nc.tensor.matmul_mx(
                         bank[:, t, :],
                         lhsT=wu_w[b][:, a, P * t : P * (t + 1)].bitcast(FP8X4),
                         lhsT_scale=wu_s[b][:, a, P * t : P * (t + 1)],
                         rhs=v_w[a][:, cols].bitcast(FP8X4),
                         rhs_scale=v_s[4 * a : P, cols],
-                        start=(a == 0),
-                        stop=(a == 1),
+                        start=(a == passes[0] and t == 0),
+                        stop=(a == passes[1] and t == 3),
                     )
             nc.vector.tensor_tensor(
                 h_bf[b][:, cols, :].rearrange("p j (u e) -> p j u e", u=2),
@@ -187,7 +196,7 @@ def tile_list_gmlpt_gelu_tsL_kernel(tc, tab_words, tab_scales, wg_words, wg_scal
 
         def down(j0, j1):
             w = j1 - j0
-            bank = ps_g.tile([P, 2, w], F32, name="ga")
+            bank = in_bank(DOWN_BANK[j0], [P, 2, w])
             for b in range(2):
                 for n in range(2):
                     nc.tensor.matmul_mx(
@@ -200,7 +209,7 @@ def tile_list_gmlpt_gelu_tsL_kernel(tc, tab_words, tab_scales, wg_words, wg_scal
                         stop=(b == 1 and n == 1),
                     )
             res = keep.tile([P, 2, w], F32, name="res%d" % j0)
-            factor = ts_g[j0 // 512][:, j0 % 512 : j0 % 512 + w].unsqueeze(1).to_broadcast([P, 2, w])
+            factor = ts_g[:, j0:j1].unsqueeze(1).to_broadcast([P, 2, w])
             if j0 < 512:
                 y_sb = keep.tile([P, 2, w], F32, name="y_sb%d" % j0)
                 nc.scalar.copy(y_sb[:], bank[:])
@@ -210,25 +219,27 @@ def tile_list_gmlpt_gelu_tsL_kernel(tc, tab_words, tab_scales, wg_words, wg_scal
             nc.sync.dma_start(out[:, j0:j1].rearrange("(n p) j -> p n j", p=P), res[:])
 
         gather(v_s, tab_s, 0, J)
-        gather(v_w[0], tab_w[0], 0, J)
         deal_wg(0)
-        deal_scales(0)
+        deal_scales()
+        for j0, j1 in ((0, 256), (256, J)):
+            gather(v_w[0], tab_w[0], j0, j1)
+        for c in range(4):
+            for u in range(2):
+                gate_pass(0, c, u, 0)
+        gather(ts_g, ts_all, 0, J)
+        for h in range(2):
+            cast_wu(0, 0, h)
         for j0, j1 in ((0, 256), (256, 512), (512, J)):
             gather(v_w[1], tab_w[1], j0, j1)
-        for a in range(2):
-            for h in range(2):
-                cast_wu(0, a, h)
-        quantize_wu(0, 0, 2)
-        for half in range(2):
-            gather_ts(half)
-        deal_wg(1)
-        deal_scales(1)
-        for u in range(2):
-            gate(0, 0, u)
         for c in range(4):
-            if c < 3:
-                for u in range(2):
-                    gate(0, c + 1, u)
+            for u in range(2):
+                gate_pass(0, c, u, 1)
+        deal_wg(1)
+        quantize_wu(0, 0, 1)
+        for h in range(2):
+            cast_wu(0, 1, h)
+        quantize_wu(0, 1, 2)
+        for c in range(4):
             for d in range(2):
                 up(0, c, d)
             if c in (1, 2):

@@ -15,11 +15,12 @@ U8 = mybir.dt.uint8
 FP8X4 = mybir.dt.float8_e4m3fn_x4
 GELU = mybir.ActivationFunctionType.Gelu_apprx_tanh
 MULT = mybir.AluOpType.mult
+ADD = mybir.AluOpType.add
 
 P = 128
-GATE_BANK = [[0, 1, 2, 3, 4, 5, 6, 7], [3, 4, 5, 6, 0, 3, 4, 5]]
-UP_BANK = [[0, 1, 2, 7, 1, 2, 7, 1], [2, 7, 1, 2, 7, 1, 2, 7]]
-DOWN_BANK = {0: 6, 256: 0, 512: 3, 768: 4, 896: 5}
+GATE_BANK = [[0, 1, 2, 3, 4, 5, 6, 7], [3, 4, 5, 6, 0, 1, 2, 7]]
+UP_BANK = [[0, 1, 2, 7, 3, 4, 5, 6], [3, 4, 5, 6, 3, 4, 5, 6]]
+DOWN_BANK = {0: 0, 256: 1, 512: 2, 768: 7, 896: 0}
 
 
 def tile_list_gmlpt_gelu_tsL_kernel(tc, tab_words, tab_scales, wg_words, wg_scales, wu, wd_words, wd_scales, ts, offs, out):
@@ -27,7 +28,7 @@ def tile_list_gmlpt_gelu_tsL_kernel(tc, tab_words, tab_scales, wg_words, wg_scal
     with ExitStack() as ctx:
         keep = ctx.enter_context(tc.tile_pool(name="keep", bufs=1))
         shared = ctx.enter_context(tc.tile_pool(name="shared", bufs=1))
-        place = {"wu_raw00": 0, "wu_raw01": 8192, "wu_raw10": 16384, "wu_raw11": 24576, "wu_bf0": 32768, "wu_bf1": 40960, "tab_w0": 49152, "tab_w1": 57344, "wg_s_raw": 65536, "wg_raw0": 66560, "wg_raw1": 70656}
+        place = {"wu_raw00": 0, "wu_raw01": 8192, "wu_raw10": 16384, "wu_raw11": 24576, "wu_bf0": 32768, "wu_bf1": 40960, "tab_w1": 49152, "tab_w0": 57344, "ts_g": 62464, "wg_s_raw": 65536, "wg_raw0": 69632, "wg_raw1": 73728, "g02": 77824}
         psum = ctx.enter_context(tc.psum_pool(name="psum", bufs=1))
 
         def in_bank(number, shape):
@@ -38,7 +39,8 @@ def tile_list_gmlpt_gelu_tsL_kernel(tc, tab_words, tab_scales, wg_words, wg_scal
         tab_s = keep.tile([P, T], U8, name="tab_s", align_bytes=64)
         wg_s_raw = shared.tile([P, R], U8, name="wg_s_raw", offset=place["wg_s_raw"], align_bytes=64)
         wd_s = keep.tile([P, N], U8, name="wd_s", align_bytes=64)
-        for plane in (tab_s, wg_s_raw, wd_s):
+        nc.gpsimd.memset(wg_s_raw[:].bitcast(I32), 0)
+        for plane in (tab_s, wd_s):
             nc.vector.memset(plane[:].bitcast(I32), 0)
 
         def load_scales(queue, plane, src):
@@ -47,9 +49,14 @@ def tile_list_gmlpt_gelu_tsL_kernel(tc, tab_words, tab_scales, wg_words, wg_scal
 
         tab_w = [shared.tile([P, T], U32, name="tab_w%d" % a, offset=place["tab_w%d" % a], align_bytes=64) for a in range(2)]
         wg_raw = [shared.tile([P, 2, 512], I32, name="wg_raw%d" % b, offset=place["wg_raw%d" % b], align_bytes=64) for b in range(2)]
-        wu_raw = {(b, a): shared.tile([P, 4, 512], F32, name="wu_raw%d%d" % (b, a), offset=place["wu_raw%d%d" % (b, a)], align_bytes=64) for b in range(2) for a in range(2)}
+        wu_raw = {(b, 0): shared.tile([P, 4, 512], F32, name="wu_raw%d0" % b, offset=place["wu_raw%d0" % b], align_bytes=64) for b in range(2)}
+        wu_half = {
+            (b, h): shared.tile([P, 4, 256], F32, name="wu_half%d%d" % (b, h), offset=place["wu_raw%d1" % b] + 4096 * h, align_bytes=64)
+            for b in range(2)
+            for h in range(2)
+        }
         wd_w = keep.tile([P, 2, N], U32, name="wd_w", align_bytes=64)
-        ts_all = keep.tile([P, T], F32, name="ts_all", align_bytes=64)
+        ts_all = shared.tile([P, T], F32, name="ts_all", offset=place["wu_bf1"], align_bytes=64)
         wg_src = wg_words.rearrange("a p r i -> p a (r i)")
 
         ts_row = keep.tile([P, 16], F32, name="ts_row", align_bytes=64)
@@ -62,14 +69,19 @@ def tile_list_gmlpt_gelu_tsL_kernel(tc, tab_words, tab_scales, wg_words, wg_scal
 
         def load_wu(b, a):
             src = wu[512 * a : 512 * (a + 1), 512 * b : 512 * (b + 1)]
-            nc.sync.dma_start(wu_raw[b, a][:], src.rearrange("(p i) c -> p i c", i=4))
+            src = src.rearrange("(p i) c -> p i c", i=4)
+            if a == 0:
+                nc.sync.dma_start(wu_raw[b, a][:], src)
+            else:
+                for h in range(2):
+                    nc.sync.dma_start(wu_half[b, h][:], src[:, :, 256 * h : 256 * (h + 1)])
 
-        nc.sync.dma_start(offsets[:], offs)
-        nc.sync.dma_start(ts_row[:], ts[0].rearrange("(p c) -> p c", c=16))
-        load_scales(nc.sync, tab_s, tab_scales)
         load_wg(0)
-        load_scales(nc.sync, wg_s_raw, wg_scales)
+        load_scales(nc.sync, tab_s, tab_scales)
+        nc.sync.dma_start(ts_row[:], ts[0].rearrange("(p c) -> p c", c=16))
+        nc.sync.dma_start(offsets[:], offs)
         load_tab(0)
+        load_scales(nc.sync, wg_s_raw, wg_scales)
         load_wu(0, 0)
         load_tab(1)
         load_wg(1)
@@ -91,12 +103,21 @@ def tile_list_gmlpt_gelu_tsL_kernel(tc, tab_words, tab_scales, wg_words, wg_scal
                 nc.tensor.transpose(bank[:, c, :], ts_row[:, c0 + c : c0 + c + 1].to_broadcast([P, P]), ident[:])
             nc.scalar.copy(ts_all[:].rearrange("q (p c) -> q p c", c=16)[:, :, c0 : c0 + 4], bank[:].rearrange("q c p -> q p c"))
 
-        v_w = [keep.tile([P, J], U32, name="v_w%d" % a, align_bytes=64) for a in range(2)]
+        v_first = keep.tile([P, 256], U32, name="v_first", align_bytes=64)
+        v_rest = shared.tile([P, J - 256], U32, name="v_rest", offset=place["wg_s_raw"], align_bytes=64)
+        v_w1 = keep.tile([P, J], U32, name="v_w1", align_bytes=64)
+
+        def table_words(a, j0, j1):
+            if a == 1:
+                return v_w1[:, j0:j1]
+            return v_first[:, j0:j1] if j0 < 256 else v_rest[:, j0 - 256 : j1 - 256]
+
         v_s = keep.tile([P, J], U8, name="v_s", align_bytes=64)
-        ts_g = shared.tile([P, J], F32, name="ts_g", offset=place["tab_w0"], align_bytes=64)
+        ts_g = shared.tile([P, 768], F32, name="ts_g", offset=place["tab_w0"], align_bytes=64)
+        ts_last = shared.tile([P, 256], F32, name="ts_last", offset=place["wu_bf0"] + 4096, align_bytes=64)
 
         def gather(dst, window, j0, j1):
-            nc.vector.tensor_copy(dst[:, j0:j1], window[:].indirect(offsets[:, j0 // 16 : j1 // 16]))
+            nc.vector.tensor_copy(dst, window[:].indirect(offsets[:, j0 // 16 : j1 // 16]))
 
         wg_w = [keep.tile([P, 2, 4, P], U32, name="wg_w%d" % b, align_bytes=64) for b in range(2)]
         wg_s = keep.tile([P, 2, 4, P], U8, name="wg_s", align_bytes=64)
@@ -113,15 +134,23 @@ def tile_list_gmlpt_gelu_tsL_kernel(tc, tab_words, tab_scales, wg_words, wg_scal
         wu_bf = [shared.tile([P, 2, 4, P, 4], BF16, name="wu_bf%d" % b, offset=place["wu_bf%d" % b], align_bytes=64) for b in range(2)]
         wu_w = [
             shared.tile([P, 2, 512], U32, name="wu_w0", offset=place["tab_w1"], align_bytes=64),
-            keep.tile([P, 2, 512], U32, name="wu_w1", align_bytes=64),
+            shared.tile([P, 2, 512], U32, name="wu_w1", offset=place["g02"], align_bytes=64),
         ]
         wu_s = [keep.tile([P, 2, 512], U8, name="wu_s%d" % b, align_bytes=64) for b in range(2)]
 
         def cast_wu(b, a, h):
-            dst = wu_bf[b][:, a, 2 * h : 2 * (h + 1), :, :].rearrange("p t m i -> p m i t")
-            src = wu_raw[b, a][:].rearrange("p i (m t) -> p m i t", t=4)[:, :, :, 2 * h : 2 * (h + 1)]
+            if a == 0:
+                dst = wu_bf[b][:, a, 2 * h : 2 * (h + 1), :, :].rearrange("p t m i -> p m i t")
+                src = wu_raw[b, a][:].rearrange("p i (m t) -> p m i t", t=4)[:, :, :, 2 * h : 2 * (h + 1)]
+            else:
+                dst = wu_bf[b][:, a, :, 64 * h : 64 * (h + 1), :].rearrange("p t m i -> p m i t")
+                src = wu_half[b, h][:].rearrange("p i (m t) -> p m i t", t=4)
             if (b, a) == (0, 1):
                 nc.vector.tensor_copy(dst, src)
+            elif (b, a) == (1, 0):
+                for m0 in (0, 64):
+                    rows = slice(m0, m0 + 64)
+                    nc.gpsimd.tensor_scalar(dst[:, rows].rearrange("p m i t -> p m t i"), src[:, rows].rearrange("p m i t -> p m t i"), 1.0, 0.0, MULT, ADD)
             else:
                 nc.scalar.copy(dst, src)
 
@@ -135,8 +164,10 @@ def tile_list_gmlpt_gelu_tsL_kernel(tc, tab_words, tab_scales, wg_words, wg_scal
         g = {}
         for b in range(2):
             for c in range(4):
-                if b == 1 and c < 2:
-                    g[b, c] = shared.tile([P, 2, 256, 2], F32, name="g1%d" % c, offset=place["wu_raw1%d" % c], align_bytes=64)
+                if (b, c) == (1, 2):
+                    g[b, c] = shared.tile([P, 2, 256, 2], F32, name="g12", offset=place["wu_raw11"] + 4096, align_bytes=64)
+                elif (b, c) == (0, 2):
+                    g[b, c] = shared.tile([P, 2, 256, 2], F32, name="g02", offset=place["g02"], align_bytes=64)
                 else:
                     g[b, c] = keep.tile([P, 2, 256, 2], F32, name="g%d%d" % (b, c), align_bytes=64)
 
@@ -153,7 +184,7 @@ def tile_list_gmlpt_gelu_tsL_kernel(tc, tab_words, tab_scales, wg_words, wg_scal
                     bank[:, e, :],
                     lhsT=wg_w[b][:, a, t, :].bitcast(FP8X4),
                     lhsT_scale=wg_s[4 * a : P, b, t, :],
-                    rhs=v_w[a][:, cols].bitcast(FP8X4),
+                    rhs=table_words(a, cols.start, cols.stop).bitcast(FP8X4),
                     rhs_scale=v_s[4 * a : P, cols],
                     start=(a == 0 and e == 0),
                     stop=(a == 1 and e == 1),
@@ -179,7 +210,7 @@ def tile_list_gmlpt_gelu_tsL_kernel(tc, tab_words, tab_scales, wg_words, wg_scal
                         bank[:, t, :],
                         lhsT=wu_w[b][:, a, P * t : P * (t + 1)].bitcast(FP8X4),
                         lhsT_scale=wu_s[b][:, a, P * t : P * (t + 1)],
-                        rhs=v_w[a][:, cols].bitcast(FP8X4),
+                        rhs=table_words(a, cols.start, cols.stop).bitcast(FP8X4),
                         rhs_scale=v_s[4 * a : P, cols],
                         start=(a == passes[0] and t == 0),
                         stop=(a == passes[1] and t == 3),
@@ -209,7 +240,7 @@ def tile_list_gmlpt_gelu_tsL_kernel(tc, tab_words, tab_scales, wg_words, wg_scal
                         stop=(b == 1 and n == 1),
                     )
             res = keep.tile([P, 2, w], F32, name="res%d" % j0)
-            factor = ts_g[:, j0:j1].unsqueeze(1).to_broadcast([P, 2, w])
+            factor = (ts_g[:, j0:j1] if j0 < 768 else ts_last[:, j0 - 768 : j1 - 768]).unsqueeze(1).to_broadcast([P, 2, w])
             if j0 < 512:
                 y_sb = keep.tile([P, 2, w], F32, name="y_sb%d" % j0)
                 nc.scalar.copy(y_sb[:], bank[:])
@@ -218,19 +249,20 @@ def tile_list_gmlpt_gelu_tsL_kernel(tc, tab_words, tab_scales, wg_words, wg_scal
                 nc.vector.tensor_tensor(res[:], bank[:], factor, MULT)
             nc.sync.dma_start(out[:, j0:j1].rearrange("(n p) j -> p n j", p=P), res[:])
 
-        gather(v_s, tab_s, 0, J)
+        gather(v_s[:], tab_s, 0, J)
         deal_wg(0)
+        gather(v_first[:], tab_w[0], 0, 256)
         deal_scales()
-        for j0, j1 in ((0, 256), (256, J)):
-            gather(v_w[0], tab_w[0], j0, j1)
+        for j0, j1 in ((256, 512), (512, J)):
+            gather(table_words(0, j0, j1), tab_w[0], j0, j1)
         for c in range(4):
             for u in range(2):
                 gate_pass(0, c, u, 0)
-        gather(ts_g, ts_all, 0, J)
+        gather(ts_g[:], ts_all, 0, 768)
         for h in range(2):
             cast_wu(0, 0, h)
         for j0, j1 in ((0, 256), (256, 512), (512, J)):
-            gather(v_w[1], tab_w[1], j0, j1)
+            gather(table_words(1, j0, j1), tab_w[1], j0, j1)
         for c in range(4):
             for u in range(2):
                 gate_pass(0, c, u, 1)
@@ -239,21 +271,23 @@ def tile_list_gmlpt_gelu_tsL_kernel(tc, tab_words, tab_scales, wg_words, wg_scal
         for h in range(2):
             cast_wu(0, 1, h)
         quantize_wu(0, 1, 2)
-        for c in range(4):
-            for d in range(2):
-                up(0, c, d)
-            if c in (1, 2):
-                for h in range(2):
-                    cast_wu(1, c - 1, h)
-        for a in range(2):
-            quantize_wu(1, a, a + 1)
+        gather(ts_last[:], ts_all, 768, J)
         for c in range(2):
             for u in range(2):
                 gate(1, c, u)
         for c in range(4):
             for d in range(2):
-                if c < 2:
-                    gate(1, c + 2, d)
+                up(0, c, d)
+        for a in range(2):
+            for h in range(2):
+                cast_wu(1, a, h)
+        for c in range(2, 4):
+            for u in range(2):
+                gate(1, c, u)
+        for a in range(2):
+            quantize_wu(1, a, a + 1)
+        for c in range(4):
+            for d in range(2):
                 if c == 0:
                     quantize_h(0, 512 * d, 512 * (d + 1))
                 elif d == 0 and c > 1:

@@ -28,7 +28,7 @@ def tile_list_gmlpt_gelu_tsL_kernel(tc, tab_words, tab_scales, wg_words, wg_scal
     with ExitStack() as ctx:
         keep = ctx.enter_context(tc.tile_pool(name="keep", bufs=1))
         shared = ctx.enter_context(tc.tile_pool(name="shared", bufs=1))
-        place = {"wu_raw00": 0, "wu_raw01": 8192, "wu_raw10": 16384, "wu_raw11": 24576, "wu_bf0": 32768, "wu_bf1": 40960, "tab_w1": 49152, "tab_w0": 57344, "ts_g": 62464, "wg_s_raw": 65536, "wg_raw0": 69632, "wg_raw1": 73728, "g02": 77824}
+        place = {"wu_raw00": 0, "wu_raw01": 8192, "wu_raw10": 16384, "wu_raw11": 24576, "wu_bf0": 32768, "wu_bf1": 40960 + 40960 + 6144, "ts_all": 40960 + 40960, "tab_w1": 49152, "tab_w0": 57344, "ts_g": 62464, "wg_s_raw": 65536, "wg_raw0": 69632, "wg_raw1": 73728, "g02": 77824}
         psum = ctx.enter_context(tc.psum_pool(name="psum", bufs=1))
 
         def in_bank(number, shape):
@@ -49,14 +49,10 @@ def tile_list_gmlpt_gelu_tsL_kernel(tc, tab_words, tab_scales, wg_words, wg_scal
 
         tab_w = [shared.tile([P, T], U32, name="tab_w%d" % a, offset=place["tab_w%d" % a], align_bytes=64) for a in range(2)]
         wg_raw = [shared.tile([P, 2, 512], I32, name="wg_raw%d" % b, offset=place["wg_raw%d" % b], align_bytes=64) for b in range(2)]
-        wu_raw = {(b, 0): shared.tile([P, 4, 512], F32, name="wu_raw%d0" % b, offset=place["wu_raw%d0" % b], align_bytes=64) for b in range(2)}
-        wu_half = {
-            (b, h): shared.tile([P, 4, 256], F32, name="wu_half%d%d" % (b, h), offset=place["wu_raw%d1" % b] + 4096 * h, align_bytes=64)
-            for b in range(2)
-            for h in range(2)
-        }
+        wu_raw = {(b, a): shared.tile([P, 4, 512], F32, name="wu_raw%d%d" % (b, a), offset=place["wu_raw%d%d" % (b, a)], align_bytes=64) for b, a in ((0, 0), (1, 0), (1, 1))}
+        wu_half = {(0, h): shared.tile([P, 4, 256], F32, name="wu_half%d" % h, offset=place["wu_raw01"] + 4096 * h, align_bytes=64) for h in range(2)}
         wd_w = keep.tile([P, 2, N], U32, name="wd_w", align_bytes=64)
-        ts_all = shared.tile([P, T], F32, name="ts_all", offset=place["wu_bf1"], align_bytes=64)
+        ts_all = shared.tile([P, T], F32, name="ts_all", offset=place["ts_all"], align_bytes=64)
         wg_src = wg_words.rearrange("a p r i -> p a (r i)")
 
         ts_row = keep.tile([P, 16], F32, name="ts_row", align_bytes=64)
@@ -70,7 +66,7 @@ def tile_list_gmlpt_gelu_tsL_kernel(tc, tab_words, tab_scales, wg_words, wg_scal
         def load_wu(b, a):
             src = wu[512 * a : 512 * (a + 1), 512 * b : 512 * (b + 1)]
             src = src.rearrange("(p i) c -> p i c", i=4)
-            if a == 0:
+            if (b, a) != (0, 1):
                 nc.sync.dma_start(wu_raw[b, a][:], src)
             else:
                 for h in range(2):
@@ -103,14 +99,14 @@ def tile_list_gmlpt_gelu_tsL_kernel(tc, tab_words, tab_scales, wg_words, wg_scal
                 nc.tensor.transpose(bank[:, c, :], ts_row[:, c0 + c : c0 + c + 1].to_broadcast([P, P]), ident[:])
             nc.scalar.copy(ts_all[:].rearrange("q (p c) -> q p c", c=16)[:, :, c0 : c0 + 4], bank[:].rearrange("q c p -> q p c"))
 
-        v_first = keep.tile([P, 256], U32, name="v_first", align_bytes=64)
-        v_rest = shared.tile([P, J - 256], U32, name="v_rest", offset=place["wg_s_raw"], align_bytes=64)
+        v_first = keep.tile([P, 512], U32, name="v_first", align_bytes=64)
+        v_rest = shared.tile([P, J - 512], U32, name="v_rest", offset=place["wg_s_raw"], align_bytes=64)
         v_w1 = keep.tile([P, J], U32, name="v_w1", align_bytes=64)
 
         def table_words(a, j0, j1):
             if a == 1:
                 return v_w1[:, j0:j1]
-            return v_first[:, j0:j1] if j0 < 256 else v_rest[:, j0 - 256 : j1 - 256]
+            return v_first[:, j0:j1] if j0 < 512 else v_rest[:, j0 - 512 : j1 - 512]
 
         v_s = keep.tile([P, J], U8, name="v_s", align_bytes=64)
         ts_g = shared.tile([P, 768], F32, name="ts_g", offset=place["tab_w0"], align_bytes=64)
@@ -139,15 +135,15 @@ def tile_list_gmlpt_gelu_tsL_kernel(tc, tab_words, tab_scales, wg_words, wg_scal
         wu_s = [keep.tile([P, 2, 512], U8, name="wu_s%d" % b, align_bytes=64) for b in range(2)]
 
         def cast_wu(b, a, h):
-            if a == 0:
+            if (b, a) != (0, 1):
                 dst = wu_bf[b][:, a, 2 * h : 2 * (h + 1), :, :].rearrange("p t m i -> p m i t")
                 src = wu_raw[b, a][:].rearrange("p i (m t) -> p m i t", t=4)[:, :, :, 2 * h : 2 * (h + 1)]
             else:
-                dst = wu_bf[b][:, a, :, 64 * h : 64 * (h + 1), :].rearrange("p t m i -> p m i t")
-                src = wu_half[b, h][:].rearrange("p i (m t) -> p m i t", t=4)
+                dst = wu_bf[b][:, a, :, 64 * h : 64 * (h + 1), :].rearrange("p (u e) m i -> p u m i e", u=2)
+                src = wu_half[b, h][:].rearrange("p i (m u e) -> p u m i e", u=2, e=2)
             if (b, a) == (0, 1):
                 nc.vector.tensor_copy(dst, src)
-            elif (b, a) == (1, 0):
+            elif (b, a, h) == (1, 0, 0):
                 for m0 in (0, 64):
                     rows = slice(m0, m0 + 64)
                     nc.gpsimd.tensor_scalar(dst[:, rows].rearrange("p m i t -> p m t i"), src[:, rows].rearrange("p m i t -> p m t i"), 1.0, 0.0, MULT, ADD)
@@ -251,10 +247,9 @@ def tile_list_gmlpt_gelu_tsL_kernel(tc, tab_words, tab_scales, wg_words, wg_scal
 
         gather(v_s[:], tab_s, 0, J)
         deal_wg(0)
-        gather(v_first[:], tab_w[0], 0, 256)
+        gather(v_first[:], tab_w[0], 0, 512)
         deal_scales()
-        for j0, j1 in ((256, 512), (512, J)):
-            gather(table_words(0, j0, j1), tab_w[0], j0, j1)
+        gather(v_rest[:], tab_w[0], 512, J)
         for c in range(4):
             for u in range(2):
                 gate_pass(0, c, u, 0)

@@ -28,7 +28,7 @@ def tile_list_gmlpt_gelu_tsL_kernel(tc, tab_words, tab_scales, wg_words, wg_scal
     with ExitStack() as ctx:
         keep = ctx.enter_context(tc.tile_pool(name="keep", bufs=1))
         shared = ctx.enter_context(tc.tile_pool(name="shared", bufs=1))
-        place = {"wu_raw00": 0, "wu_raw01": 8192, "wu_raw10": 16384, "wu_raw11": 24576, "wu_bf0": 32768, "wu_bf1": 40960 + 40960 + 6144, "ts_all": 40960 + 40960, "tab_w1": 49152, "tab_w0": 57344, "ts_g": 62464, "wg_s_raw": 65536, "wg_raw0": 69632, "wg_raw1": 73728, "g02": 77824}
+        place = {"wu_raw00": 0, "wu_raw01": 8192, "wu_raw10": 16384, "wu_raw11": 24576, "wu_bf0": 32768, "wu_bf1": 40960 + 40960 + 6144, "ts_all": 40960 + 40960, "tab_w1": 49152, "tab_w0": 57344, "ts_g": 62464, "wg_s_raw": 101376, "v_rest": 101888, "ts_early": 98816, "wg_raw0": 69632, "wg_raw1": 73728, "g02": 77824}
         psum = ctx.enter_context(tc.psum_pool(name="psum", bufs=1))
 
         def in_bank(number, shape):
@@ -39,16 +39,17 @@ def tile_list_gmlpt_gelu_tsL_kernel(tc, tab_words, tab_scales, wg_words, wg_scal
         tab_s = keep.tile([P, T], U8, name="tab_s", align_bytes=64)
         wg_s_raw = shared.tile([P, R], U8, name="wg_s_raw", offset=place["wg_s_raw"], align_bytes=64)
         wd_s = keep.tile([P, N], U8, name="wd_s", align_bytes=64)
-        nc.gpsimd.memset(wg_s_raw[:].bitcast(I32), 0)
-        for plane in (tab_s, wd_s):
-            nc.vector.memset(plane[:].bitcast(I32), 0)
+        for plane in (tab_s, wg_s_raw):
+            nc.gpsimd.memset(plane[:].bitcast(I32), 0)
+        nc.vector.memset(wd_s[:].bitcast(I32), 0)
 
         def load_scales(queue, plane, src):
             for q in range(4):
                 queue.dma_start(plane[32 * q : 32 * q + 8, :].bitcast(I32), src[:, 4 * q : 4 * q + 4, :].bitcast(I32))
 
         tab_w = [shared.tile([P, T], U32, name="tab_w%d" % a, offset=place["tab_w%d" % a], align_bytes=64) for a in range(2)]
-        wg_raw = [shared.tile([P, 2, 512], I32, name="wg_raw%d" % b, offset=place["wg_raw%d" % b], align_bytes=64) for b in range(2)]
+        wg_raw0 = [shared.tile([P, 512], I32, name="wg_raw0%d" % a, offset=place["wg_raw0"] + 2048 * a, align_bytes=64) for a in range(2)]
+        wg_raw1 = shared.tile([P, 2, 512], I32, name="wg_raw1", offset=place["wg_raw1"], align_bytes=64)
         wu_raw = {(b, a): shared.tile([P, 4, 512], F32, name="wu_raw%d%d" % (b, a), offset=place["wu_raw%d%d" % (b, a)], align_bytes=64) for b, a in ((0, 0), (1, 0), (1, 1))}
         wu_half = {(0, h): shared.tile([P, 4, 256], F32, name="wu_half%d" % h, offset=place["wu_raw01"] + 4096 * h, align_bytes=64) for h in range(2)}
         wd_w = keep.tile([P, 2, N], U32, name="wd_w", align_bytes=64)
@@ -60,8 +61,11 @@ def tile_list_gmlpt_gelu_tsL_kernel(tc, tab_words, tab_scales, wg_words, wg_scal
         def load_tab(a):
             nc.sync.dma_start(tab_w[a][:].bitcast(I32), tab_words[a].rearrange("p t i -> p (t i)").bitcast(I32))
 
-        def load_wg(b):
-            nc.sync.dma_start(wg_raw[b][:], wg_src[:, :, 2048 * b : 2048 * (b + 1)].bitcast(I32))
+        def load_wg0(a):
+            nc.sync.dma_start(wg_raw0[a][:], wg_src[:, a, 0:2048].bitcast(I32))
+
+        def load_wg1():
+            nc.sync.dma_start(wg_raw1[:], wg_src[:, :, 2048:4096].bitcast(I32))
 
         def load_wu(b, a):
             src = wu[512 * a : 512 * (a + 1), 512 * b : 512 * (b + 1)]
@@ -72,15 +76,16 @@ def tile_list_gmlpt_gelu_tsL_kernel(tc, tab_words, tab_scales, wg_words, wg_scal
                 for h in range(2):
                     nc.sync.dma_start(wu_half[b, h][:], src[:, :, 256 * h : 256 * (h + 1)])
 
-        load_wg(0)
+        load_wg0(0)
         load_scales(nc.sync, tab_s, tab_scales)
         nc.sync.dma_start(ts_row[:], ts[0].rearrange("(p c) -> p c", c=16))
         nc.sync.dma_start(offsets[:], offs)
         load_tab(0)
         load_scales(nc.sync, wg_s_raw, wg_scales)
+        load_wg0(1)
         load_wu(0, 0)
         load_tab(1)
-        load_wg(1)
+        load_wg1()
         load_wu(0, 1)
         load_wu(1, 0)
         load_wu(1, 1)
@@ -100,7 +105,7 @@ def tile_list_gmlpt_gelu_tsL_kernel(tc, tab_words, tab_scales, wg_words, wg_scal
             nc.scalar.copy(ts_all[:].rearrange("q (p c) -> q p c", c=16)[:, :, c0 : c0 + 4], bank[:].rearrange("q c p -> q p c"))
 
         v_first = keep.tile([P, 512], U32, name="v_first", align_bytes=64)
-        v_rest = shared.tile([P, J - 512], U32, name="v_rest", offset=place["wg_s_raw"], align_bytes=64)
+        v_rest = shared.tile([P, J - 512], U32, name="v_rest", offset=place["v_rest"], align_bytes=64)
         v_w1 = keep.tile([P, J], U32, name="v_w1", align_bytes=64)
 
         def table_words(a, j0, j1):
@@ -109,8 +114,8 @@ def tile_list_gmlpt_gelu_tsL_kernel(tc, tab_words, tab_scales, wg_words, wg_scal
             return v_first[:, j0:j1] if j0 < 512 else v_rest[:, j0 - 512 : j1 - 512]
 
         v_s = keep.tile([P, J], U8, name="v_s", align_bytes=64)
-        ts_g = shared.tile([P, 768], F32, name="ts_g", offset=place["tab_w0"], align_bytes=64)
-        ts_last = shared.tile([P, 256], F32, name="ts_last", offset=place["wu_bf0"] + 4096, align_bytes=64)
+        ts_g = shared.tile([P, 768], F32, name="ts_g", offset=place["ts_early"], align_bytes=64)
+        ts_last = shared.tile([P, 256], F32, name="ts_last", offset=place["wu_raw01"] + 4096, align_bytes=64)
 
         def gather(dst, window, j0, j1):
             nc.vector.tensor_copy(dst, window[:].indirect(offsets[:, j0 // 16 : j1 // 16]))
@@ -118,10 +123,16 @@ def tile_list_gmlpt_gelu_tsL_kernel(tc, tab_words, tab_scales, wg_words, wg_scal
         wg_w = [keep.tile([P, 2, 4, P], U32, name="wg_w%d" % b, align_bytes=64) for b in range(2)]
         wg_s = keep.tile([P, 2, 4, P], U8, name="wg_s", align_bytes=64)
 
-        def deal_wg(b):
+        def deal_wg0(a):
             nc.vector.tensor_copy(
-                wg_w[b][:].bitcast(I32).rearrange("p a t m -> p a m t"),
-                wg_raw[b][:].rearrange("p a (m t) -> p a m t", t=4),
+                wg_w[0][:, a].bitcast(I32).rearrange("p (u e) m -> p u m e", u=2),
+                wg_raw0[a][:].rearrange("p (m u e) -> p u m e", u=2, e=2),
+            )
+
+        def deal_wg1():
+            nc.vector.tensor_copy(
+                wg_w[1][:].bitcast(I32).rearrange("p a (u e) m -> p a u m e", u=2),
+                wg_raw1[:].rearrange("p a (m u e) -> p a u m e", u=2, e=2),
             )
 
         def deal_scales():
@@ -221,9 +232,12 @@ def tile_list_gmlpt_gelu_tsL_kernel(tc, tab_words, tab_scales, wg_words, wg_scal
         def quantize_h(b, j0, j1):
             nc.vector.quantize_mx(h_w[b][:, j0:j1].bitcast(FP8X4), h_s[b][:, j0:j1], h_bf[b][:, j0:j1, :].rearrange("p j t -> p (j t)"))
 
-        def down(j0, j1):
+        down_bank = {}
+
+        def down_passes(j0, j1):
             w = j1 - j0
             bank = in_bank(DOWN_BANK[j0], [P, 2, w])
+            down_bank[j0] = bank
             for b in range(2):
                 for n in range(2):
                     nc.tensor.matmul_mx(
@@ -235,6 +249,10 @@ def tile_list_gmlpt_gelu_tsL_kernel(tc, tab_words, tab_scales, wg_words, wg_scal
                         start=(b == 0 and n == 0),
                         stop=(b == 1 and n == 1),
                     )
+
+        def finish(j0, j1):
+            w = j1 - j0
+            bank = down_bank[j0]
             res = keep.tile([P, 2, w], F32, name="res%d" % j0)
             factor = (ts_g[:, j0:j1] if j0 < 768 else ts_last[:, j0 - 768 : j1 - 768]).unsqueeze(1).to_broadcast([P, 2, w])
             if j0 < 512:
@@ -245,10 +263,15 @@ def tile_list_gmlpt_gelu_tsL_kernel(tc, tab_words, tab_scales, wg_words, wg_scal
                 nc.vector.tensor_tensor(res[:], bank[:], factor, MULT)
             nc.sync.dma_start(out[:, j0:j1].rearrange("(n p) j -> p n j", p=P), res[:])
 
+        def down(j0, j1):
+            down_passes(j0, j1)
+            finish(j0, j1)
+
         gather(v_s[:], tab_s, 0, J)
-        deal_wg(0)
+        deal_wg0(0)
         gather(v_first[:], tab_w[0], 0, 512)
         deal_scales()
+        deal_wg0(1)
         gather(v_rest[:], tab_w[0], 512, J)
         for c in range(4):
             for u in range(2):
@@ -261,7 +284,7 @@ def tile_list_gmlpt_gelu_tsL_kernel(tc, tab_words, tab_scales, wg_words, wg_scal
         for c in range(4):
             for u in range(2):
                 gate_pass(0, c, u, 1)
-        deal_wg(1)
+        deal_wg1()
         quantize_wu(0, 0, 1)
         for h in range(2):
             cast_wu(0, 1, h)
@@ -290,7 +313,8 @@ def tile_list_gmlpt_gelu_tsL_kernel(tc, tab_words, tab_scales, wg_words, wg_scal
                 up(1, c, d)
                 if c > 0 and d == 0:
                     quantize_h(1, 256 * (c - 1), 256 * c)
-        quantize_h(1, 768, 896)
+                if (c, d) == (3, 0):
+                    quantize_h(1, 768, 896)
         down(512, 768)
         quantize_h(1, 896, J)
         down(768, 896)

@@ -130,10 +130,11 @@ def tile_list_gmlpt_gelu_tsL_kernel(tc, tab_words, tab_scales, wg_words, wg_scal
             )
 
         def deal_wg1():
-            nc.vector.tensor_copy(
-                wg_w[1][:].bitcast(I32).rearrange("p a (u e) m -> p a u m e", u=2),
-                wg_raw1[:].rearrange("p a (m u e) -> p a u m e", u=2, e=2),
-            )
+            for a in range(2):
+                nc.vector.tensor_copy(
+                    wg_w[1][:, a].bitcast(I32).rearrange("p (u e) m -> p u m e", u=2),
+                    wg_raw1[:, a].rearrange("p (m u e) -> p u m e", u=2, e=2),
+                )
 
         def deal_scales():
             nc.vector.tensor_copy(wg_s[:], wg_s_raw[:].rearrange("p (b m t) -> p b t m", b=2, t=4))
@@ -160,6 +161,18 @@ def tile_list_gmlpt_gelu_tsL_kernel(tc, tab_words, tab_scales, wg_words, wg_scal
                     nc.gpsimd.tensor_scalar(dst[:, rows].rearrange("p m i t -> p m t i"), src[:, rows].rearrange("p m i t -> p m t i"), 1.0, 0.0, MULT, ADD)
             else:
                 nc.scalar.copy(dst, src)
+
+        def cast_last_piece(u):
+            dst = wu_bf[0][:, 1, 2 * u : 2 * (u + 1), 64:128, :].rearrange("p e m i -> p m i e")
+            src = wu_half[0, 1][:].rearrange("p i (m t) -> p m i t", t=4)[:, :, :, 2 * u : 2 * (u + 1)]
+            nc.vector.tensor_copy(dst, src)
+
+        def quantize_slots(u):
+            nc.vector.quantize_mx(
+                wu_w[0][:, 1, 256 * u : 256 * (u + 1)].bitcast(FP8X4),
+                wu_s[0][:, 1, 256 * u : 256 * (u + 1)],
+                wu_bf[0][:, 1, 2 * u : 2 * (u + 1), :, :].rearrange("p t m i -> p (t m i)"),
+            )
 
         def quantize_wu(b, a0, a1):
             nc.vector.quantize_mx(
@@ -279,16 +292,18 @@ def tile_list_gmlpt_gelu_tsL_kernel(tc, tab_words, tab_scales, wg_words, wg_scal
         gather(ts_g[:], ts_all, 0, 768)
         for h in range(2):
             cast_wu(0, 0, h)
-        for j0, j1 in ((0, 256), (256, 512), (512, J)):
+        for j0, j1 in ((0, 256), (256, 512), (512, 768), (768, J)):
             gather(table_words(1, j0, j1), tab_w[1], j0, j1)
         for c in range(4):
             for u in range(2):
                 gate_pass(0, c, u, 1)
         deal_wg1()
         quantize_wu(0, 0, 1)
-        for h in range(2):
-            cast_wu(0, 1, h)
-        quantize_wu(0, 1, 2)
+        cast_wu(0, 1, 0)
+        for u in range(2):
+            cast_last_piece(u)
+        for u in range(2):
+            quantize_slots(u)
         gather(ts_last[:], ts_all, 768, J)
         for c in range(2):
             for u in range(2):

@@ -18,9 +18,42 @@ MULT = mybir.AluOpType.mult
 ADD = mybir.AluOpType.add
 
 P = 128
+BAND = 512
+CHUNK = 256
+KIB = 1024
+
+FIRST_ENTRIES = 512
+TS_EARLY = 768
+EARLY_UP_TILES = 3
+GPSIMD_COLUMNS = 512
+
 GATE_BANK = [[0, 1, 2, 3, 4, 5, 6, 7], [3, 4, 5, 6, 0, 1, 2, 7]]
 UP_BANK = [[0, 1, 2, 7, 3, 4, 5, 6], [3, 4, 5, 6, 3, 4, 5, 6]]
 DOWN_BANK = {0: 0, 256: 1, 512: 2, 768: 7, 896: 0}
+
+PLACE = {
+    "wu_raw00": 0,
+    "wu_raw01": 8 * KIB,
+    "wu_raw10": 16 * KIB,
+    "wu_raw11": 24 * KIB,
+    "wu_bf0": 32 * KIB,
+    "tab_w1": 48 * KIB,
+    "tab_w0": 56 * KIB,
+    "wg_raw0": 68 * KIB,
+    "wg_raw1": 72 * KIB,
+    "g02": 76 * KIB,
+    "ts_all": 80 * KIB,
+    "wg_s_raw": 99 * KIB,
+}
+TENANT = {
+    "v_rest": PLACE["wg_s_raw"] + R // 2,
+    "ts_early": PLACE["wg_s_raw"] + R // 2 - 4 * TS_EARLY,
+    "wu_w0": PLACE["tab_w1"],
+    "ts_late": PLACE["wu_raw01"] + 4 * KIB,
+    "wu_bf1": PLACE["ts_all"] + 6 * KIB,
+    "wu_w1": PLACE["g02"],
+    "g12": PLACE["wu_raw11"] + 4 * KIB,
+}
 
 
 def tile_list_gmlpt_gelu_tsL_kernel(tc, tab_words, tab_scales, wg_words, wg_scales, wu, wd_words, wd_scales, ts, offs, out):
@@ -28,8 +61,10 @@ def tile_list_gmlpt_gelu_tsL_kernel(tc, tab_words, tab_scales, wg_words, wg_scal
     with ExitStack() as ctx:
         keep = ctx.enter_context(tc.tile_pool(name="keep", bufs=1))
         shared = ctx.enter_context(tc.tile_pool(name="shared", bufs=1))
-        place = {"wu_raw00": 0, "wu_raw01": 8192, "wu_raw10": 16384, "wu_raw11": 24576, "wu_bf0": 32768, "wu_bf1": 40960 + 40960 + 6144, "ts_all": 40960 + 40960, "tab_w1": 49152, "tab_w0": 57344, "ts_g": 62464, "wg_s_raw": 101376, "v_rest": 101888, "ts_early": 98816, "wg_raw0": 69632, "wg_raw1": 73728, "g02": 77824}
         psum = ctx.enter_context(tc.psum_pool(name="psum", bufs=1))
+
+        def placed(shape, dtype, name, offset):
+            return shared.tile(shape, dtype, name=name, offset=offset, align_bytes=64)
 
         def in_bank(number, shape):
             return psum.tile(shape, F32, name="bank%d" % number)
@@ -37,59 +72,51 @@ def tile_list_gmlpt_gelu_tsL_kernel(tc, tab_words, tab_scales, wg_words, wg_scal
         offsets = keep.tile([P, J // 16], U16, name="offsets")
 
         tab_s = keep.tile([P, T], U8, name="tab_s", align_bytes=64)
-        wg_s_raw = shared.tile([P, R], U8, name="wg_s_raw", offset=place["wg_s_raw"], align_bytes=64)
+        wg_s_raw = placed([P, R], U8, "wg_s_raw", PLACE["wg_s_raw"])
         wd_s = keep.tile([P, N], U8, name="wd_s", align_bytes=64)
-        for plane in (tab_s, wg_s_raw):
-            nc.gpsimd.memset(plane[:].bitcast(I32), 0)
+        for scale_tile in (tab_s, wg_s_raw):
+            nc.gpsimd.memset(scale_tile[:].bitcast(I32), 0)
         nc.vector.memset(wd_s[:].bitcast(I32), 0)
 
-        def load_scales(queue, plane, src):
-            for q in range(4):
-                queue.dma_start(plane[32 * q : 32 * q + 8, :].bitcast(I32), src[:, 4 * q : 4 * q + 4, :].bitcast(I32))
-
-        tab_w = [shared.tile([P, T], U32, name="tab_w%d" % a, offset=place["tab_w%d" % a], align_bytes=64) for a in range(2)]
-        wg_raw0 = [shared.tile([P, 512], I32, name="wg_raw0%d" % a, offset=place["wg_raw0"] + 2048 * a, align_bytes=64) for a in range(2)]
-        wg_raw1 = shared.tile([P, 2, 512], I32, name="wg_raw1", offset=place["wg_raw1"], align_bytes=64)
-        wu_raw = {(b, a): shared.tile([P, 4, 512], F32, name="wu_raw%d%d" % (b, a), offset=place["wu_raw%d%d" % (b, a)], align_bytes=64) for b, a in ((0, 0), (1, 0), (1, 1))}
-        wu_half = {(0, h): shared.tile([P, 4, 256], F32, name="wu_half%d" % h, offset=place["wu_raw01"] + 4096 * h, align_bytes=64) for h in range(2)}
+        tab_w = [placed([P, T], U32, "tab_w%d" % a, PLACE["tab_w%d" % a]) for a in range(2)]
+        wg_raw0 = [placed([P, BAND], I32, "wg_raw0%d" % a, PLACE["wg_raw0"] + 4 * BAND * a) for a in range(2)]
+        wg_raw1 = placed([P, 2, BAND], I32, "wg_raw1", PLACE["wg_raw1"])
+        wu_raw = {(b, a): placed([P, 4, BAND], F32, "wu_raw%d%d" % (b, a), PLACE["wu_raw%d%d" % (b, a)]) for b, a in ((0, 0), (1, 0), (1, 1))}
+        wu_half = [placed([P, 4, BAND // 2], F32, "wu_half%d" % half, PLACE["wu_raw01"] + 4 * KIB * half) for half in range(2)]
         wd_w = keep.tile([P, 2, N], U32, name="wd_w", align_bytes=64)
-        ts_all = shared.tile([P, T], F32, name="ts_all", offset=place["ts_all"], align_bytes=64)
-        wg_src = wg_words.rearrange("a p r i -> p a (r i)")
+        ts_all = placed([P, T], F32, "ts_all", PLACE["ts_all"])
+        ts_row = keep.tile([P, T // P], F32, name="ts_row", align_bytes=64)
 
-        ts_row = keep.tile([P, 16], F32, name="ts_row", align_bytes=64)
+        def load_scales(scale_tile, src):
+            for q in range(4):
+                nc.sync.dma_start(scale_tile[32 * q : 32 * q + 8, :].bitcast(I32), src[:, 4 * q : 4 * q + 4, :].bitcast(I32))
 
         def load_tab(a):
             nc.sync.dma_start(tab_w[a][:].bitcast(I32), tab_words[a].rearrange("p t i -> p (t i)").bitcast(I32))
 
+        wg_src = wg_words.rearrange("a p r i -> p a (r i)")
+
         def load_wg0(a):
-            nc.sync.dma_start(wg_raw0[a][:], wg_src[:, a, 0:2048].bitcast(I32))
+            nc.sync.dma_start(wg_raw0[a][:], wg_src[:, a, 0 : 4 * BAND].bitcast(I32))
 
-        def load_wg1():
-            nc.sync.dma_start(wg_raw1[:], wg_src[:, :, 2048:4096].bitcast(I32))
+        def wu_src(b, a):
+            return wu[BAND * a : BAND * (a + 1), BAND * b : BAND * (b + 1)].rearrange("(p i) c -> p i c", i=4)
 
-        def load_wu(b, a):
-            src = wu[512 * a : 512 * (a + 1), 512 * b : 512 * (b + 1)]
-            src = src.rearrange("(p i) c -> p i c", i=4)
-            if (b, a) != (0, 1):
-                nc.sync.dma_start(wu_raw[b, a][:], src)
-            else:
-                for h in range(2):
-                    nc.sync.dma_start(wu_half[b, h][:], src[:, :, 256 * h : 256 * (h + 1)])
-
-        load_wg0(0)
-        load_scales(nc.sync, tab_s, tab_scales)
-        nc.sync.dma_start(ts_row[:], ts[0].rearrange("(p c) -> p c", c=16))
         nc.sync.dma_start(offsets[:], offs)
+        load_wg0(0)
+        load_scales(tab_s, tab_scales)
+        nc.sync.dma_start(ts_row[:], ts[0].rearrange("(p c) -> p c", c=T // P))
         load_tab(0)
-        load_scales(nc.sync, wg_s_raw, wg_scales)
+        load_scales(wg_s_raw, wg_scales)
         load_wg0(1)
-        load_wu(0, 0)
+        nc.sync.dma_start(wu_raw[0, 0][:], wu_src(0, 0))
         load_tab(1)
-        load_wg1()
-        load_wu(0, 1)
-        load_wu(1, 0)
-        load_wu(1, 1)
-        load_scales(nc.sync, wd_s, wd_scales)
+        nc.sync.dma_start(wg_raw1[:], wg_src[:, :, 4 * BAND : 8 * BAND].bitcast(I32))
+        for half in range(2):
+            nc.sync.dma_start(wu_half[half][:], wu_src(0, 1)[:, :, BAND // 2 * half : BAND // 2 * (half + 1)])
+        for a in range(2):
+            nc.sync.dma_start(wu_raw[1, a][:], wu_src(1, a))
+        load_scales(wd_s, wd_scales)
         nc.sync.dma_start(wd_w[:].bitcast(I32), wd_words.rearrange("a p n i -> p a (n i)").bitcast(I32))
 
         warm = keep.tile([P, 8], F32, name="warm")
@@ -98,24 +125,26 @@ def tile_list_gmlpt_gelu_tsL_kernel(tc, tab_words, tab_scales, wg_words, wg_scal
 
         ident = keep.tile([P, P], F32, name="ident", align_bytes=64)
         make_identity(nc, ident[:])
-        for c0 in range(0, 16, 4):
+        for c0 in range(0, T // P, 4):
             bank = in_bank(4 + c0 // 4, [P, 4, P])
             for c in range(4):
                 nc.tensor.transpose(bank[:, c, :], ts_row[:, c0 + c : c0 + c + 1].to_broadcast([P, P]), ident[:])
-            nc.scalar.copy(ts_all[:].rearrange("q (p c) -> q p c", c=16)[:, :, c0 : c0 + 4], bank[:].rearrange("q c p -> q p c"))
+            nc.scalar.copy(ts_all[:].rearrange("q (p c) -> q p c", c=T // P)[:, :, c0 : c0 + 4], bank[:].rearrange("q c p -> q p c"))
 
-        v_first = keep.tile([P, 512], U32, name="v_first", align_bytes=64)
-        v_rest = shared.tile([P, J - 512], U32, name="v_rest", offset=place["v_rest"], align_bytes=64)
+        v_first = keep.tile([P, FIRST_ENTRIES], U32, name="v_first", align_bytes=64)
+        v_rest = placed([P, J - FIRST_ENTRIES], U32, "v_rest", TENANT["v_rest"])
         v_w1 = keep.tile([P, J], U32, name="v_w1", align_bytes=64)
+        v_s = keep.tile([P, J], U8, name="v_s", align_bytes=64)
+        ts_early = placed([P, TS_EARLY], F32, "ts_early", TENANT["ts_early"])
+        ts_late = placed([P, J - TS_EARLY], F32, "ts_late", TENANT["ts_late"])
 
         def table_words(a, j0, j1):
             if a == 1:
                 return v_w1[:, j0:j1]
-            return v_first[:, j0:j1] if j0 < 512 else v_rest[:, j0 - 512 : j1 - 512]
+            return v_first[:, j0:j1] if j0 < FIRST_ENTRIES else v_rest[:, j0 - FIRST_ENTRIES : j1 - FIRST_ENTRIES]
 
-        v_s = keep.tile([P, J], U8, name="v_s", align_bytes=64)
-        ts_g = shared.tile([P, 768], F32, name="ts_g", offset=place["ts_early"], align_bytes=64)
-        ts_last = shared.tile([P, 256], F32, name="ts_last", offset=place["wu_raw01"] + 4096, align_bytes=64)
+        def listed_ts(j0, j1):
+            return ts_early[:, j0:j1] if j0 < TS_EARLY else ts_late[:, j0 - TS_EARLY : j1 - TS_EARLY]
 
         def gather(dst, window, j0, j1):
             nc.vector.tensor_copy(dst, window[:].indirect(offsets[:, j0 // 16 : j1 // 16]))
@@ -123,80 +152,69 @@ def tile_list_gmlpt_gelu_tsL_kernel(tc, tab_words, tab_scales, wg_words, wg_scal
         wg_w = [keep.tile([P, 2, 4, P], U32, name="wg_w%d" % b, align_bytes=64) for b in range(2)]
         wg_s = keep.tile([P, 2, 4, P], U8, name="wg_s", align_bytes=64)
 
-        def deal_wg0(a):
+        def deal_wg(b, a):
+            src = wg_raw0[a][:] if b == 0 else wg_raw1[:, a]
             nc.vector.tensor_copy(
-                wg_w[0][:, a].bitcast(I32).rearrange("p (u e) m -> p u m e", u=2),
-                wg_raw0[a][:].rearrange("p (m u e) -> p u m e", u=2, e=2),
+                wg_w[b][:, a].bitcast(I32).rearrange("p (u e) m -> p u m e", u=2),
+                src.rearrange("p (m u e) -> p u m e", u=2, e=2),
             )
-
-        def deal_wg1():
-            for a in range(2):
-                nc.vector.tensor_copy(
-                    wg_w[1][:, a].bitcast(I32).rearrange("p (u e) m -> p u m e", u=2),
-                    wg_raw1[:, a].rearrange("p (m u e) -> p u m e", u=2, e=2),
-                )
 
         def deal_scales():
             nc.vector.tensor_copy(wg_s[:], wg_s_raw[:].rearrange("p (b m t) -> p b t m", b=2, t=4))
 
-        wu_bf = [shared.tile([P, 2, 4, P, 4], BF16, name="wu_bf%d" % b, offset=place["wu_bf%d" % b], align_bytes=64) for b in range(2)]
-        wu_w = [
-            shared.tile([P, 2, 512], U32, name="wu_w0", offset=place["tab_w1"], align_bytes=64),
-            shared.tile([P, 2, 512], U32, name="wu_w1", offset=place["g02"], align_bytes=64),
-        ]
-        wu_s = [keep.tile([P, 2, 512], U8, name="wu_s%d" % b, align_bytes=64) for b in range(2)]
+        wu_bf = [placed([P, 2, 4, P, 4], BF16, "wu_bf0", PLACE["wu_bf0"]), placed([P, 2, 4, P, 4], BF16, "wu_bf1", TENANT["wu_bf1"])]
+        wu_w = [placed([P, 2, BAND], U32, "wu_w%d" % b, TENANT["wu_w%d" % b]) for b in range(2)]
+        wu_s = [keep.tile([P, 2, BAND], U8, name="wu_s%d" % b, align_bytes=64) for b in range(2)]
 
-        def cast_wu(b, a, h):
-            if (b, a) != (0, 1):
-                dst = wu_bf[b][:, a, 2 * h : 2 * (h + 1), :, :].rearrange("p t m i -> p m i t")
-                src = wu_raw[b, a][:].rearrange("p i (m t) -> p m i t", t=4)[:, :, :, 2 * h : 2 * (h + 1)]
-            else:
-                dst = wu_bf[b][:, a, :, 64 * h : 64 * (h + 1), :].rearrange("p (u e) m i -> p u m i e", u=2)
-                src = wu_half[b, h][:].rearrange("p i (m u e) -> p u m i e", u=2, e=2)
-            if (b, a) == (0, 1):
-                nc.vector.tensor_copy(dst, src)
-            elif (b, a, h) == (1, 0, 0):
-                for m0 in (0, 64):
-                    rows = slice(m0, m0 + 64)
-                    nc.gpsimd.tensor_scalar(dst[:, rows].rearrange("p m i t -> p m t i"), src[:, rows].rearrange("p m i t -> p m t i"), 1.0, 0.0, MULT, ADD)
-            else:
-                nc.scalar.copy(dst, src)
-
-        def cast_last_piece(u):
-            dst = wu_bf[0][:, 1, 2 * u : 2 * (u + 1), 64:128, :].rearrange("p e m i -> p m i e")
-            src = wu_half[0, 1][:].rearrange("p i (m t) -> p m i t", t=4)[:, :, :, 2 * u : 2 * (u + 1)]
-            nc.vector.tensor_copy(dst, src)
-
-        def quantize_slots(u):
-            nc.vector.quantize_mx(
-                wu_w[0][:, 1, 256 * u : 256 * (u + 1)].bitcast(FP8X4),
-                wu_s[0][:, 1, 256 * u : 256 * (u + 1)],
-                wu_bf[0][:, 1, 2 * u : 2 * (u + 1), :, :].rearrange("p t m i -> p (t m i)"),
+        def slot_pair_views(b, a, u, src, places):
+            slots = slice(2 * u, 2 * (u + 1))
+            return (
+                wu_bf[b][:, a, slots, places, :].rearrange("p t m i -> p m i t"),
+                src[:].rearrange("p i (m t) -> p m i t", t=4)[:, :, :, slots],
             )
 
-        def quantize_wu(b, a0, a1):
+        def round_on_scalar(b, a, u):
+            nc.scalar.copy(*slot_pair_views(b, a, u, wu_raw[b, a], slice(0, P)))
+
+        def round_on_gpsimd(b, a, u):
+            dst, src = slot_pair_views(b, a, u, wu_raw[b, a], slice(0, P))
+            for m0 in (0, P // 2):
+                places = slice(m0, m0 + P // 2)
+                nc.gpsimd.tensor_scalar(dst[:, places].rearrange("p m i t -> p m t i"), src[:, places].rearrange("p m i t -> p m t i"), 1.0, 0.0, MULT, ADD)
+
+        def round_first_half():
+            nc.vector.tensor_copy(
+                wu_bf[0][:, 1, :, 0 : P // 2, :].rearrange("p (u e) m i -> p u m i e", u=2),
+                wu_half[0][:].rearrange("p i (m u e) -> p u m i e", u=2, e=2),
+            )
+
+        def round_second_half(u):
+            nc.vector.tensor_copy(*slot_pair_views(0, 1, u, wu_half[1], slice(P // 2, P)))
+
+        def quantize_wu(b, a, t0, t1):
             nc.vector.quantize_mx(
-                wu_w[b][:, a0:a1, :].rearrange("p a c -> p (a c)").bitcast(FP8X4),
-                wu_s[b][:, a0:a1, :].rearrange("p a c -> p (a c)"),
-                wu_bf[b][:, a0:a1, :, :, :].rearrange("p a t m i -> p (a t m i)"),
+                wu_w[b][:, a, P * t0 : P * t1].bitcast(FP8X4),
+                wu_s[b][:, a, P * t0 : P * t1],
+                wu_bf[b][:, a, t0:t1, :, :].rearrange("p t m i -> p (t m i)"),
             )
 
         g = {}
         for b in range(2):
             for c in range(4):
-                if (b, c) == (1, 2):
-                    g[b, c] = shared.tile([P, 2, 256, 2], F32, name="g12", offset=place["wu_raw11"] + 4096, align_bytes=64)
-                elif (b, c) == (0, 2):
-                    g[b, c] = shared.tile([P, 2, 256, 2], F32, name="g02", offset=place["g02"], align_bytes=64)
+                name = "g%d%d" % (b, c)
+                if name in TENANT:
+                    g[b, c] = placed([P, 2, CHUNK, 2], F32, name, TENANT[name])
+                elif name in PLACE:
+                    g[b, c] = placed([P, 2, CHUNK, 2], F32, name, PLACE[name])
                 else:
-                    g[b, c] = keep.tile([P, 2, 256, 2], F32, name="g%d%d" % (b, c), align_bytes=64)
+                    g[b, c] = keep.tile([P, 2, CHUNK, 2], F32, name=name, align_bytes=64)
 
         gate_bank = {}
 
         def gate_pass(b, c, u, a):
-            cols = slice(256 * c, 256 * (c + 1))
+            j0, j1 = CHUNK * c, CHUNK * (c + 1)
             if a == 0:
-                gate_bank[b, c, u] = in_bank(GATE_BANK[b][2 * c + u], [P, 2, 256])
+                gate_bank[b, c, u] = in_bank(GATE_BANK[b][2 * c + u], [P, 2, CHUNK])
             bank = gate_bank[b, c, u]
             for e in range(2):
                 t = 2 * u + e
@@ -204,8 +222,8 @@ def tile_list_gmlpt_gelu_tsL_kernel(tc, tab_words, tab_scales, wg_words, wg_scal
                     bank[:, e, :],
                     lhsT=wg_w[b][:, a, t, :].bitcast(FP8X4),
                     lhsT_scale=wg_s[4 * a : P, b, t, :],
-                    rhs=table_words(a, cols.start, cols.stop).bitcast(FP8X4),
-                    rhs_scale=v_s[4 * a : P, cols],
+                    rhs=table_words(a, j0, j1).bitcast(FP8X4),
+                    rhs_scale=v_s[4 * a : P, j0:j1],
                     start=(a == 0 and e == 0),
                     stop=(a == 1 and e == 1),
                 )
@@ -221,22 +239,22 @@ def tile_list_gmlpt_gelu_tsL_kernel(tc, tab_words, tab_scales, wg_words, wg_scal
         h_s = [keep.tile([P, J], U8, name="h_s%d" % b, align_bytes=64) for b in range(2)]
 
         def up(b, c, d):
-            cols = slice(256 * c + P * d, 256 * c + P * (d + 1))
+            j0, j1 = CHUNK * c + P * d, CHUNK * c + P * (d + 1)
             bank = in_bank(UP_BANK[b][2 * c + d], [P, 4, P])
-            passes = (0, 1) if 2 * c + d < 3 else (1, 0)
+            passes = (0, 1) if 2 * c + d < EARLY_UP_TILES else (1, 0)
             for a in passes:
                 for t in range(4):
                     nc.tensor.matmul_mx(
                         bank[:, t, :],
                         lhsT=wu_w[b][:, a, P * t : P * (t + 1)].bitcast(FP8X4),
                         lhsT_scale=wu_s[b][:, a, P * t : P * (t + 1)],
-                        rhs=table_words(a, cols.start, cols.stop).bitcast(FP8X4),
-                        rhs_scale=v_s[4 * a : P, cols],
+                        rhs=table_words(a, j0, j1).bitcast(FP8X4),
+                        rhs_scale=v_s[4 * a : P, j0:j1],
                         start=(a == passes[0] and t == 0),
                         stop=(a == passes[1] and t == 3),
                     )
             nc.vector.tensor_tensor(
-                h_bf[b][:, cols, :].rearrange("p j (u e) -> p j u e", u=2),
+                h_bf[b][:, j0:j1, :].rearrange("p j (u e) -> p j u e", u=2),
                 bank[:].rearrange("p (u e) j -> p j u e", u=2),
                 g[b, c][:, :, P * d : P * (d + 1), :].rearrange("p u j e -> p j u e"),
                 MULT,
@@ -245,12 +263,9 @@ def tile_list_gmlpt_gelu_tsL_kernel(tc, tab_words, tab_scales, wg_words, wg_scal
         def quantize_h(b, j0, j1):
             nc.vector.quantize_mx(h_w[b][:, j0:j1].bitcast(FP8X4), h_s[b][:, j0:j1], h_bf[b][:, j0:j1, :].rearrange("p j t -> p (j t)"))
 
-        down_bank = {}
-
-        def down_passes(j0, j1):
-            w = j1 - j0
-            bank = in_bank(DOWN_BANK[j0], [P, 2, w])
-            down_bank[j0] = bank
+        def down(j0, j1):
+            width = j1 - j0
+            bank = in_bank(DOWN_BANK[j0], [P, 2, width])
             for b in range(2):
                 for n in range(2):
                     nc.tensor.matmul_mx(
@@ -262,75 +277,72 @@ def tile_list_gmlpt_gelu_tsL_kernel(tc, tab_words, tab_scales, wg_words, wg_scal
                         start=(b == 0 and n == 0),
                         stop=(b == 1 and n == 1),
                     )
-
-        def finish(j0, j1):
-            w = j1 - j0
-            bank = down_bank[j0]
-            res = keep.tile([P, 2, w], F32, name="res%d" % j0)
-            factor = (ts_g[:, j0:j1] if j0 < 768 else ts_last[:, j0 - 768 : j1 - 768]).unsqueeze(1).to_broadcast([P, 2, w])
-            if j0 < 512:
-                y_sb = keep.tile([P, 2, w], F32, name="y_sb%d" % j0)
+            res = keep.tile([P, 2, width], F32, name="res%d" % j0)
+            factor = listed_ts(j0, j1).unsqueeze(1).to_broadcast([P, 2, width])
+            if j0 < GPSIMD_COLUMNS:
+                y_sb = keep.tile([P, 2, width], F32, name="y_sb%d" % j0)
                 nc.scalar.copy(y_sb[:], bank[:])
                 nc.gpsimd.tensor_tensor(res[:], y_sb[:], factor, MULT)
             else:
                 nc.vector.tensor_tensor(res[:], bank[:], factor, MULT)
             nc.sync.dma_start(out[:, j0:j1].rearrange("(n p) j -> p n j", p=P), res[:])
 
-        def down(j0, j1):
-            down_passes(j0, j1)
-            finish(j0, j1)
-
         gather(v_s[:], tab_s, 0, J)
-        deal_wg0(0)
-        gather(v_first[:], tab_w[0], 0, 512)
+        deal_wg(0, 0)
+        gather(v_first[:], tab_w[0], 0, FIRST_ENTRIES)
         deal_scales()
-        deal_wg0(1)
-        gather(v_rest[:], tab_w[0], 512, J)
+        deal_wg(0, 1)
+        gather(v_rest[:], tab_w[0], FIRST_ENTRIES, J)
         for c in range(4):
             for u in range(2):
                 gate_pass(0, c, u, 0)
-        gather(ts_g[:], ts_all, 0, 768)
-        for h in range(2):
-            cast_wu(0, 0, h)
-        for j0, j1 in ((0, 256), (256, 512), (512, 768), (768, J)):
-            gather(table_words(1, j0, j1), tab_w[1], j0, j1)
+        gather(ts_early[:], ts_all, 0, TS_EARLY)
+        for u in range(2):
+            round_on_scalar(0, 0, u)
+
+        for c in range(4):
+            gather(table_words(1, CHUNK * c, CHUNK * (c + 1)), tab_w[1], CHUNK * c, CHUNK * (c + 1))
         for c in range(4):
             for u in range(2):
                 gate_pass(0, c, u, 1)
-        deal_wg1()
-        quantize_wu(0, 0, 1)
-        cast_wu(0, 1, 0)
+
+        for a in range(2):
+            deal_wg(1, a)
+        quantize_wu(0, 0, 0, 4)
+        round_first_half()
         for u in range(2):
-            cast_last_piece(u)
+            round_second_half(u)
         for u in range(2):
-            quantize_slots(u)
-        gather(ts_last[:], ts_all, 768, J)
+            quantize_wu(0, 1, 2 * u, 2 * (u + 1))
+        gather(ts_late[:], ts_all, TS_EARLY, J)
+
         for c in range(2):
             for u in range(2):
                 gate(1, c, u)
         for c in range(4):
             for d in range(2):
                 up(0, c, d)
-        for a in range(2):
-            for h in range(2):
-                cast_wu(1, a, h)
+        round_on_gpsimd(1, 0, 0)
+        round_on_scalar(1, 0, 1)
+        for u in range(2):
+            round_on_scalar(1, 1, u)
         for c in range(2, 4):
             for u in range(2):
                 gate(1, c, u)
         for a in range(2):
-            quantize_wu(1, a, a + 1)
+            quantize_wu(1, a, 0, 4)
+
+        quantize_h(0, 0, J)
         for c in range(4):
-            for d in range(2):
-                if c == 0:
-                    quantize_h(0, 512 * d, 512 * (d + 1))
-                elif d == 0 and c > 1:
-                    down(256 * (c - 2), 256 * (c - 1))
-                up(1, c, d)
-                if c > 0 and d == 0:
-                    quantize_h(1, 256 * (c - 1), 256 * c)
-                if (c, d) == (3, 0):
-                    quantize_h(1, 768, 896)
-        down(512, 768)
-        quantize_h(1, 896, J)
-        down(768, 896)
-        down(896, J)
+            if c > 1:
+                down(CHUNK * (c - 2), CHUNK * (c - 1))
+            up(1, c, 0)
+            if c > 0:
+                quantize_h(1, CHUNK * (c - 1), CHUNK * c)
+            if c == 3:
+                quantize_h(1, J - CHUNK, J - P)
+            up(1, c, 1)
+        down(J - 2 * CHUNK, J - CHUNK)
+        quantize_h(1, J - P, J)
+        down(J - CHUNK, J - P)
+        down(J - P, J)

@@ -19,41 +19,16 @@ ADD = mybir.AluOpType.add
 
 P = 128
 BAND = 512
+HALF = BAND // 2
 CHUNK = 256
 KIB = 1024
-
-FIRST_ENTRIES = 512
-TS_EARLY = 768
-EARLY_UP_TILES = 3
 GPSIMD_COLUMNS = 512
 
-GATE_BANK = [[0, 1, 2, 3, 4, 5, 6, 7], [3, 4, 5, 6, 0, 1, 2, 7]]
-UP_BANK = [[0, 1, 2, 7, 3, 4, 5, 6], [3, 4, 5, 6, 3, 4, 5, 6]]
-DOWN_BANK = {0: 0, 256: 1, 512: 2, 768: 7, 896: 0}
-
-PLACE = {
-    "wu_raw00": 0,
-    "wu_raw01": 8 * KIB,
-    "wu_raw10": 16 * KIB,
-    "wu_raw11": 24 * KIB,
-    "wu_bf0": 32 * KIB,
-    "tab_w1": 48 * KIB,
-    "tab_w0": 56 * KIB,
-    "wg_raw0": 68 * KIB,
-    "wg_raw1": 72 * KIB,
-    "g02": 76 * KIB,
-    "ts_all": 80 * KIB,
-    "wg_s_raw": 99 * KIB,
-}
-TENANT = {
-    "v_rest": PLACE["wg_s_raw"] + R // 2,
-    "ts_early": PLACE["wg_s_raw"] + R // 2 - 4 * TS_EARLY,
-    "wu_w0": PLACE["tab_w1"],
-    "ts_late": PLACE["wu_raw01"] + 4 * KIB,
-    "wu_bf1": PLACE["ts_all"] + 6 * KIB,
-    "wu_w1": PLACE["g02"],
-    "g12": PLACE["wu_raw11"] + 4 * KIB,
-}
+EARLY_GATES = 5
+EARLY_UP_TILES = 2
+GATE_BANK = [[0, 1, 2, 3, 4, 5, 6, 7], [0, 1, 2, 3, 4, 0, 1, 2]]
+UP_BANK = [[5, 6, 7, 0, 1, 2, 3, 4], [5, 6, 7, 3, 5, 6, 7, 3]]
+DOWN_BANK = {0: 4, 256: 0, 512: 1, 768: 2, 896: 4}
 
 
 def tile_list_gmlpt_gelu_tsL_kernel(tc, tab_words, tab_scales, wg_words, wg_scales, wu, wd_words, wd_scales, ts, offs, out):
@@ -63,6 +38,9 @@ def tile_list_gmlpt_gelu_tsL_kernel(tc, tab_words, tab_scales, wg_words, wg_scal
         shared = ctx.enter_context(tc.tile_pool(name="shared", bufs=1))
         psum = ctx.enter_context(tc.psum_pool(name="psum", bufs=1))
 
+        def held(shape, dtype, name):
+            return keep.tile(shape, dtype, name=name, align_bytes=64)
+
         def placed(shape, dtype, name, offset):
             return shared.tile(shape, dtype, name=name, offset=offset, align_bytes=64)
 
@@ -70,22 +48,20 @@ def tile_list_gmlpt_gelu_tsL_kernel(tc, tab_words, tab_scales, wg_words, wg_scal
             return psum.tile(shape, F32, name="bank%d" % number)
 
         offsets = keep.tile([P, J // 16], U16, name="offsets")
-
-        tab_s = keep.tile([P, T], U8, name="tab_s", align_bytes=64)
-        wg_s_raw = placed([P, R], U8, "wg_s_raw", PLACE["wg_s_raw"])
-        wd_s = keep.tile([P, N], U8, name="wd_s", align_bytes=64)
+        tab_s = held([P, T], U8, "tab_s")
+        wg_s_raw = placed([P, R], U8, "wg_s_raw", 20 * KIB)
+        wd_s = held([P, N], U8, "wd_s")
         for scale_tile in (tab_s, wg_s_raw):
             nc.gpsimd.memset(scale_tile[:].bitcast(I32), 0)
         nc.vector.memset(wd_s[:].bitcast(I32), 0)
 
-        tab_w = [placed([P, T], U32, "tab_w%d" % a, PLACE["tab_w%d" % a]) for a in range(2)]
-        wg_raw0 = [placed([P, BAND], I32, "wg_raw0%d" % a, PLACE["wg_raw0"] + 4 * BAND * a) for a in range(2)]
-        wg_raw1 = placed([P, 2, BAND], I32, "wg_raw1", PLACE["wg_raw1"])
-        wu_raw = {(b, a): placed([P, 4, BAND], F32, "wu_raw%d%d" % (b, a), PLACE["wu_raw%d%d" % (b, a)]) for b, a in ((0, 0), (1, 0), (1, 1))}
-        wu_half = [placed([P, 4, BAND // 2], F32, "wu_half%d" % half, PLACE["wu_raw01"] + 4 * KIB * half) for half in range(2)]
-        wd_w = keep.tile([P, 2, N], U32, name="wd_w", align_bytes=64)
-        ts_all = placed([P, T], F32, "ts_all", PLACE["ts_all"])
-        ts_row = keep.tile([P, T // P], F32, name="ts_row", align_bytes=64)
+        tab_w = [held([P, T], U32, "tab_w%d" % a) for a in range(2)]
+        wg_raw0 = [held([P, BAND], U32, "wg_raw0%d" % a) for a in range(2)]
+        wg_raw1 = [placed([P, BAND], U32, "wg_raw1%d" % a, (2 + 13 * a) * KIB) for a in range(2)]
+        wu_half = {(b, a, x): held([P, 4, HALF], F32, "wu_half%d%d%d" % (b, a, x)) for b in range(2) for a in range(2) for x in range(2)}
+        wd_w = held([P, 2, N], U32, "wd_w")
+        ts_all = held([P, T], F32, "ts_all")
+        ts_row = held([P, T // P], F32, "ts_row")
 
         def load_scales(scale_tile, src):
             for q in range(4):
@@ -96,26 +72,26 @@ def tile_list_gmlpt_gelu_tsL_kernel(tc, tab_words, tab_scales, wg_words, wg_scal
 
         wg_src = wg_words.rearrange("a p r i -> p a (r i)")
 
-        def load_wg0(a):
-            nc.sync.dma_start(wg_raw0[a][:], wg_src[:, a, 0 : 4 * BAND].bitcast(I32))
+        def load_wg(b, a):
+            nc.sync.dma_start((wg_raw0, wg_raw1)[b][a][:].bitcast(I32), wg_src[:, a, 4 * BAND * b : 4 * BAND * (b + 1)].bitcast(I32))
 
         def wu_src(b, a):
             return wu[BAND * a : BAND * (a + 1), BAND * b : BAND * (b + 1)].rearrange("(p i) c -> p i c", i=4)
 
         nc.sync.dma_start(offsets[:], offs)
-        load_wg0(0)
+        load_wg(0, 0)
         load_scales(tab_s, tab_scales)
         nc.sync.dma_start(ts_row[:], ts[0].rearrange("(p c) -> p c", c=T // P))
         load_tab(0)
         load_scales(wg_s_raw, wg_scales)
-        load_wg0(1)
-        nc.sync.dma_start(wu_raw[0, 0][:], wu_src(0, 0))
+        load_wg(0, 1)
         load_tab(1)
-        nc.sync.dma_start(wg_raw1[:], wg_src[:, :, 4 * BAND : 8 * BAND].bitcast(I32))
-        for half in range(2):
-            nc.sync.dma_start(wu_half[half][:], wu_src(0, 1)[:, :, BAND // 2 * half : BAND // 2 * (half + 1)])
         for a in range(2):
-            nc.sync.dma_start(wu_raw[1, a][:], wu_src(1, a))
+            load_wg(1, a)
+        for b in range(2):
+            for a in range(2):
+                for x in range(2):
+                    nc.sync.dma_start(wu_half[b, a, x][:], wu_src(b, a)[:, :, HALF * x : HALF * (x + 1)])
         load_scales(wd_s, wd_scales)
         nc.sync.dma_start(wd_w[:].bitcast(I32), wd_words.rearrange("a p n i -> p a (n i)").bitcast(I32))
 
@@ -123,7 +99,7 @@ def tile_list_gmlpt_gelu_tsL_kernel(tc, tab_words, tab_scales, wg_words, wg_scal
         nc.vector.memset(warm[:], 0.0)
         nc.scalar.activation(warm[:, 0:1], warm[:, 1:2], GELU)
 
-        ident = keep.tile([P, P], F32, name="ident", align_bytes=64)
+        ident = held([P, P], F32, "ident")
         make_identity(nc, ident[:])
         for c0 in range(0, T // P, 4):
             bank = in_bank(4 + c0 // 4, [P, 4, P])
@@ -131,65 +107,48 @@ def tile_list_gmlpt_gelu_tsL_kernel(tc, tab_words, tab_scales, wg_words, wg_scal
                 nc.tensor.transpose(bank[:, c, :], ts_row[:, c0 + c : c0 + c + 1].to_broadcast([P, P]), ident[:])
             nc.scalar.copy(ts_all[:].rearrange("q (p c) -> q p c", c=T // P)[:, :, c0 : c0 + 4], bank[:].rearrange("q c p -> q p c"))
 
-        v_first = keep.tile([P, FIRST_ENTRIES], U32, name="v_first", align_bytes=64)
-        v_rest = placed([P, J - FIRST_ENTRIES], U32, "v_rest", TENANT["v_rest"])
-        v_w1 = keep.tile([P, J], U32, name="v_w1", align_bytes=64)
-        v_s = keep.tile([P, J], U8, name="v_s", align_bytes=64)
-        ts_early = placed([P, TS_EARLY], F32, "ts_early", TENANT["ts_early"])
-        ts_late = placed([P, J - TS_EARLY], F32, "ts_late", TENANT["ts_late"])
+        v_w = [[held([P, J // 2], U32, "v_w%d%d" % (a, x)) if (a, x) != (0, 1) else placed([P, J // 2], U32, "v_w01", 20 * KIB) for x in range(2)] for a in range(2)]
+        v_s = held([P, J], U8, "v_s")
+        ts_g = placed([P, J], F32, "ts_g", 0)
 
         def table_words(a, j0, j1):
-            if a == 1:
-                return v_w1[:, j0:j1]
-            return v_first[:, j0:j1] if j0 < FIRST_ENTRIES else v_rest[:, j0 - FIRST_ENTRIES : j1 - FIRST_ENTRIES]
-
-        def listed_ts(j0, j1):
-            return ts_early[:, j0:j1] if j0 < TS_EARLY else ts_late[:, j0 - TS_EARLY : j1 - TS_EARLY]
+            x = j0 // (J // 2)
+            return v_w[a][x][:, j0 - x * J // 2 : j1 - x * J // 2]
 
         def gather(dst, window, j0, j1):
             nc.vector.tensor_copy(dst, window[:].indirect(offsets[:, j0 // 16 : j1 // 16]))
 
-        wg_w = [keep.tile([P, 2, 4, P], U32, name="wg_w%d" % b, align_bytes=64) for b in range(2)]
-        wg_s = keep.tile([P, 2, 4, P], U8, name="wg_s", align_bytes=64)
+        wg_w = [held([P, 2, 4, P], U32, "wg_w%d" % b) for b in range(2)]
+        wg_s = held([P, 2, 4, P], U8, "wg_s")
 
-        def deal_wg(b, a):
-            src = wg_raw0[a][:] if b == 0 else wg_raw1[:, a]
-            nc.vector.tensor_copy(
-                wg_w[b][:, a].bitcast(I32).rearrange("p (u e) m -> p u m e", u=2),
-                src.rearrange("p (m u e) -> p u m e", u=2, e=2),
-            )
-
-        def deal_scales():
-            nc.vector.tensor_copy(wg_s[:], wg_s_raw[:].rearrange("p (b m t) -> p b t m", b=2, t=4))
-
-        wu_bf = [placed([P, 2, 4, P, 4], BF16, "wu_bf0", PLACE["wu_bf0"]), placed([P, 2, 4, P, 4], BF16, "wu_bf1", TENANT["wu_bf1"])]
-        wu_w = [placed([P, 2, BAND], U32, "wu_w%d" % b, TENANT["wu_w%d" % b]) for b in range(2)]
-        wu_s = [keep.tile([P, 2, BAND], U8, name="wu_s%d" % b, align_bytes=64) for b in range(2)]
-
-        def slot_pair_views(b, a, u, src, places):
-            slots = slice(2 * u, 2 * (u + 1))
+        def deal_views(b, a, dtype):
+            src = (wg_raw0, wg_raw1)[b][a][:]
             return (
-                wu_bf[b][:, a, slots, places, :].rearrange("p t m i -> p m i t"),
-                src[:].rearrange("p i (m t) -> p m i t", t=4)[:, :, :, slots],
+                wg_w[b][:, a].bitcast(dtype).rearrange("p (u e) m -> p u m e", u=2),
+                src.bitcast(dtype).rearrange("p (m u e) -> p u m e", u=2, e=2),
             )
 
-        def round_on_scalar(b, a, u):
-            nc.scalar.copy(*slot_pair_views(b, a, u, wu_raw[b, a], slice(0, P)))
+        wu_bf = [placed([P, 2, 4, P, 4], BF16, "wu_bf%d" % b, 24 * KIB) for b in range(2)]
+        wu_w = [held([P, 2, BAND], U32, "wu_w0"), placed([P, 2, BAND], U32, "wu_w1", 4 * KIB)]
+        wu_s = [held([P, 2, BAND], U8, "wu_s%d" % b) for b in range(2)]
 
-        def round_on_gpsimd(b, a, u):
-            dst, src = slot_pair_views(b, a, u, wu_raw[b, a], slice(0, P))
-            for m0 in (0, P // 2):
-                places = slice(m0, m0 + P // 2)
-                nc.gpsimd.tensor_scalar(dst[:, places].rearrange("p m i t -> p m t i"), src[:, places].rearrange("p m i t -> p m t i"), 1.0, 0.0, MULT, ADD)
-
-        def round_first_half():
-            nc.vector.tensor_copy(
-                wu_bf[0][:, 1, :, 0 : P // 2, :].rearrange("p (u e) m i -> p u m i e", u=2),
-                wu_half[0][:].rearrange("p i (m u e) -> p u m i e", u=2, e=2),
+        def round_views(b, a, u, x, order):
+            slots = slice(2 * u, 2 * (u + 1))
+            places = slice(P // 2 * x, P // 2 * (x + 1))
+            src = wu_half[b, a, x][:]
+            return (
+                wu_bf[b][:, a, slots, places, :].rearrange("p t m i -> " + order),
+                src.rearrange("p i (m t) -> p t m i", t=4)[:, slots].rearrange("p t m i -> " + order),
             )
 
-        def round_second_half(u):
-            nc.vector.tensor_copy(*slot_pair_views(0, 1, u, wu_half[1], slice(P // 2, P)))
+        def round_on_gpsimd(b, a, u, x):
+            nc.gpsimd.tensor_scalar(*round_views(b, a, u, x, "p m t i"), 1.0, 0.0, MULT, ADD)
+
+        def round_on_scalar(b, a, u, x):
+            nc.scalar.copy(*round_views(b, a, u, x, "p m i t"))
+
+        def round_on_vector(b, a, u, x):
+            nc.vector.tensor_copy(*round_views(b, a, u, x, "p m i t"))
 
         def quantize_wu(b, a, t0, t1):
             nc.vector.quantize_mx(
@@ -198,17 +157,12 @@ def tile_list_gmlpt_gelu_tsL_kernel(tc, tab_words, tab_scales, wg_words, wg_scal
                 wu_bf[b][:, a, t0:t1, :, :].rearrange("p t m i -> p (t m i)"),
             )
 
-        g = {}
-        for b in range(2):
-            for c in range(4):
-                name = "g%d%d" % (b, c)
-                if name in TENANT:
-                    g[b, c] = placed([P, 2, CHUNK, 2], F32, name, TENANT[name])
-                elif name in PLACE:
-                    g[b, c] = placed([P, 2, CHUNK, 2], F32, name, PLACE[name])
-                else:
-                    g[b, c] = keep.tile([P, 2, CHUNK, 2], F32, name=name, align_bytes=64)
-
+        g_first = placed([P, 3, 2, CHUNK, 2], F32, "g_first", 4 * KIB)
+        g_last = placed([P, 2, CHUNK, 2], F32, "g_last", 16 * KIB)
+        g = {(0, c): g_first[:, c] for c in range(3)}
+        g[0, 3] = g_last[:]
+        for c in range(4):
+            g[1, c] = held([P, 2, CHUNK, 2], F32, "g1%d" % c)[:]
         gate_bank = {}
 
         def gate_pass(b, c, u, a):
@@ -227,21 +181,19 @@ def tile_list_gmlpt_gelu_tsL_kernel(tc, tab_words, tab_scales, wg_words, wg_scal
                     start=(a == 0 and e == 0),
                     stop=(a == 1 and e == 1),
                 )
-            if a == 1:
-                nc.scalar.activation(g[b, c][:, u, :, :], bank[:].rearrange("p e j -> p j e"), GELU)
 
-        def gate(b, c, u):
-            for a in range(2):
-                gate_pass(b, c, u, a)
+        def gelu(b, c, u):
+            nc.scalar.activation(g[b, c][:, u, :, :], gate_bank[b, c, u][:].rearrange("p e j -> p j e"), GELU)
 
-        h_bf = [keep.tile([P, J, 4], BF16, name="h_bf%d" % b, align_bytes=64) for b in range(2)]
-        h_w = [keep.tile([P, J], U32, name="h_w%d" % b, align_bytes=64) for b in range(2)]
-        h_s = [keep.tile([P, J], U8, name="h_s%d" % b, align_bytes=64) for b in range(2)]
+        h_bf = [held([P, J, 4], BF16, "h_bf%d" % b) for b in range(2)]
+        h_w = [held([P, J], U32, "h_w%d" % b) for b in range(2)]
+        h_s = [held([P, J], U8, "h_s%d" % b) for b in range(2)]
 
-        def up(b, c, d):
-            j0, j1 = CHUNK * c + P * d, CHUNK * c + P * (d + 1)
-            bank = in_bank(UP_BANK[b][2 * c + d], [P, 4, P])
-            passes = (0, 1) if 2 * c + d < EARLY_UP_TILES else (1, 0)
+        def up(b, i):
+            c, d = divmod(i, 2)
+            j0, j1 = P * i, P * (i + 1)
+            bank = in_bank(UP_BANK[b][i], [P, 4, P])
+            passes = (0, 1) if i < EARLY_UP_TILES else (1, 0)
             for a in passes:
                 for t in range(4):
                     nc.tensor.matmul_mx(
@@ -278,7 +230,7 @@ def tile_list_gmlpt_gelu_tsL_kernel(tc, tab_words, tab_scales, wg_words, wg_scal
                         stop=(b == 1 and n == 1),
                     )
             res = keep.tile([P, 2, width], F32, name="res%d" % j0)
-            factor = listed_ts(j0, j1).unsqueeze(1).to_broadcast([P, 2, width])
+            factor = ts_g[:, j0:j1].unsqueeze(1).to_broadcast([P, 2, width])
             if j0 < GPSIMD_COLUMNS:
                 y_sb = keep.tile([P, 2, width], F32, name="y_sb%d" % j0)
                 nc.scalar.copy(y_sb[:], bank[:])
@@ -287,61 +239,70 @@ def tile_list_gmlpt_gelu_tsL_kernel(tc, tab_words, tab_scales, wg_words, wg_scal
                 nc.vector.tensor_tensor(res[:], bank[:], factor, MULT)
             nc.sync.dma_start(out[:, j0:j1].rearrange("(n p) j -> p n j", p=P), res[:])
 
+        nc.vector.tensor_copy(*deal_views(0, 0, I32))
         gather(v_s[:], tab_s, 0, J)
-        deal_wg(0, 0)
-        gather(v_first[:], tab_w[0], 0, FIRST_ENTRIES)
-        deal_scales()
-        deal_wg(0, 1)
-        gather(v_rest[:], tab_w[0], FIRST_ENTRIES, J)
+        gather(v_w[0][0][:], tab_w[0], 0, J // 2)
+        nc.vector.tensor_copy(wg_s[:], wg_s_raw[:].rearrange("p (b m t) -> p b t m", b=2, t=4))
+        nc.vector.tensor_copy(*deal_views(0, 1, I32))
+        gather(v_w[0][1][:], tab_w[0], J // 2, J)
         for c in range(4):
             for u in range(2):
                 gate_pass(0, c, u, 0)
-        gather(ts_early[:], ts_all, 0, TS_EARLY)
-        for u in range(2):
-            round_on_scalar(0, 0, u)
-
         for c in range(4):
             gather(table_words(1, CHUNK * c, CHUNK * (c + 1)), tab_w[1], CHUNK * c, CHUNK * (c + 1))
+        for a in range(2):
+            nc.scalar.copy(*deal_views(1, a, U32))
         for c in range(4):
             for u in range(2):
                 gate_pass(0, c, u, 1)
+                gelu(0, c, u)
+        gather(ts_g[:], ts_all, 0, J)
 
-        for a in range(2):
-            deal_wg(1, a)
-        quantize_wu(0, 0, 0, 4)
-        round_first_half()
+        for u, x in ((0, 0), (1, 0), (0, 1)):
+            round_on_gpsimd(0, 0, u, x)
+        round_on_vector(0, 0, 1, 1)
         for u in range(2):
-            round_second_half(u)
+            round_on_vector(0, 1, u, 0)
+        quantize_wu(0, 0, 0, 4)
+        for u in range(2):
+            round_on_vector(0, 1, u, 1)
         for u in range(2):
             quantize_wu(0, 1, 2 * u, 2 * (u + 1))
-        gather(ts_late[:], ts_all, TS_EARLY, J)
 
-        for c in range(2):
-            for u in range(2):
-                gate(1, c, u)
-        for c in range(4):
-            for d in range(2):
-                up(0, c, d)
-        round_on_gpsimd(1, 0, 0)
-        round_on_scalar(1, 0, 1)
-        for u in range(2):
-            round_on_scalar(1, 1, u)
-        for c in range(2, 4):
-            for u in range(2):
-                gate(1, c, u)
-        for a in range(2):
-            quantize_wu(1, a, 0, 4)
+        def gate(i):
+            c, u = divmod(i, 2)
+            for a in range(2):
+                gate_pass(1, c, u, a)
 
-        quantize_h(0, 0, J)
+        for i in range(EARLY_GATES):
+            gate(i)
+            gelu(1, *divmod(i, 2))
+        for x in range(2):
+            for u in range(2):
+                round_on_gpsimd(1, 0, u, x)
+        for x in range(2):
+            round_on_scalar(1, 1, 1, x)
+            round_on_gpsimd(1, 1, 0, x)
+        for i in range(8):
+            up(0, i)
+            if i == 6:
+                for a in range(2):
+                    quantize_wu(1, a, 0, 4)
+        for i in range(EARLY_GATES, 8):
+            gate(i)
+            gelu(1, *divmod(i, 2))
+
+        for x in range(2):
+            quantize_h(0, J // 2 * x, J // 2 * (x + 1))
         for c in range(4):
             if c > 1:
                 down(CHUNK * (c - 2), CHUNK * (c - 1))
-            up(1, c, 0)
+            up(1, 2 * c)
             if c > 0:
                 quantize_h(1, CHUNK * (c - 1), CHUNK * c)
             if c == 3:
                 quantize_h(1, J - CHUNK, J - P)
-            up(1, c, 1)
+            up(1, 2 * c + 1)
         down(J - 2 * CHUNK, J - CHUNK)
         quantize_h(1, J - P, J)
         down(J - CHUNK, J - P)

@@ -49,16 +49,17 @@ def tile_list_gmlpt_gelu_tsL_kernel(tc, tab_words, tab_scales, wg_words, wg_scal
 
         offsets = keep.tile([P, J // 16], U16, name="offsets")
         tab_s = held([P, T], U8, "tab_s")
-        wg_s_raw = placed([P, R], U8, "wg_s_raw", 20 * KIB)
+        wg_s_raw = placed([P, R], U8, "wg_s_raw", 62 * KIB - R // 2)
         wd_s = held([P, N], U8, "wd_s")
         for scale_tile in (tab_s, wg_s_raw):
             nc.gpsimd.memset(scale_tile[:].bitcast(I32), 0)
         nc.vector.memset(wd_s[:].bitcast(I32), 0)
 
-        tab_w = [held([P, T], U32, "tab_w%d" % a) for a in range(2)]
+        tab_w = [held([P, T], U32, "tab_w0"), placed([P, T], U32, "tab_w1", 40 * KIB)]
         wg_raw0 = [held([P, BAND], U32, "wg_raw0%d" % a) for a in range(2)]
-        wg_raw1 = [placed([P, BAND], U32, "wg_raw1%d" % a, (2 + 13 * a) * KIB) for a in range(2)]
-        wu_half = {(b, a, x): held([P, 4, HALF], F32, "wu_half%d%d%d" % (b, a, x)) for b in range(2) for a in range(2) for x in range(2)}
+        wg_raw1 = placed([P, 2, BAND], U32, "wg_raw1", 0)
+        wu_half = {(a, x): placed([P, 4, HALF], F32, "wu_half%d%d" % (a, x), (64 + 8 * a + 4 * x) * KIB) for a in range(2) for x in range(2)}
+        wu_raw1 = [held([P, 4, BAND], F32, "wu_raw1%d" % a) for a in range(2)]
         wd_w = held([P, 2, N], U32, "wd_w")
         ts_all = held([P, T], F32, "ts_all")
         ts_row = held([P, T // P], F32, "ts_row")
@@ -72,26 +73,30 @@ def tile_list_gmlpt_gelu_tsL_kernel(tc, tab_words, tab_scales, wg_words, wg_scal
 
         wg_src = wg_words.rearrange("a p r i -> p a (r i)")
 
-        def load_wg(b, a):
-            nc.sync.dma_start((wg_raw0, wg_raw1)[b][a][:].bitcast(I32), wg_src[:, a, 4 * BAND * b : 4 * BAND * (b + 1)].bitcast(I32))
+        def load_wg0(a):
+            nc.sync.dma_start(wg_raw0[a][:].bitcast(I32), wg_src[:, a, 0 : 4 * BAND].bitcast(I32))
+
+        def load_half(a, x):
+            nc.sync.dma_start(wu_half[a, x][:], wu_src(0, a)[:, :, HALF * x : HALF * (x + 1)])
 
         def wu_src(b, a):
             return wu[BAND * a : BAND * (a + 1), BAND * b : BAND * (b + 1)].rearrange("(p i) c -> p i c", i=4)
 
         nc.sync.dma_start(offsets[:], offs)
-        load_wg(0, 0)
+        load_wg0(0)
         load_scales(tab_s, tab_scales)
         nc.sync.dma_start(ts_row[:], ts[0].rearrange("(p c) -> p c", c=T // P))
         load_tab(0)
         load_scales(wg_s_raw, wg_scales)
-        load_wg(0, 1)
+        load_wg0(1)
+        load_half(0, 0)
         load_tab(1)
+        load_half(0, 1)
+        nc.sync.dma_start(wg_raw1[:].bitcast(I32), wg_src[:, :, 4 * BAND : 8 * BAND].bitcast(I32))
+        for x in range(2):
+            load_half(1, x)
         for a in range(2):
-            load_wg(1, a)
-        for b in range(2):
-            for a in range(2):
-                for x in range(2):
-                    nc.sync.dma_start(wu_half[b, a, x][:], wu_src(b, a)[:, :, HALF * x : HALF * (x + 1)])
+            nc.sync.dma_start(wu_raw1[a][:], wu_src(1, a))
         load_scales(wd_s, wd_scales)
         nc.sync.dma_start(wd_w[:].bitcast(I32), wd_words.rearrange("a p n i -> p a (n i)").bitcast(I32))
 
@@ -107,9 +112,18 @@ def tile_list_gmlpt_gelu_tsL_kernel(tc, tab_words, tab_scales, wg_words, wg_scal
                 nc.tensor.transpose(bank[:, c, :], ts_row[:, c0 + c : c0 + c + 1].to_broadcast([P, P]), ident[:])
             nc.scalar.copy(ts_all[:].rearrange("q (p c) -> q p c", c=T // P)[:, :, c0 : c0 + 4], bank[:].rearrange("q c p -> q p c"))
 
-        v_w = [[held([P, J // 2], U32, "v_w%d%d" % (a, x)) if (a, x) != (0, 1) else placed([P, J // 2], U32, "v_w01", 20 * KIB) for x in range(2)] for a in range(2)]
+        v_w = [[held([P, J // 2], U32, "v_w%d%d" % (a, x)) if (a, x) != (0, 1) else placed([P, J // 2], U32, "v_w01", 62 * KIB) for x in range(2)] for a in range(2)]
         v_s = held([P, J], U8, "v_s")
-        ts_g = placed([P, J], F32, "ts_g", 0)
+        ts_part = [
+            placed([P, J // 2], F32, "ts_early", 60 * KIB),
+            placed([P, CHUNK], F32, "ts_mid", 24 * KIB),
+            placed([P, CHUNK], F32, "ts_late", 76 * KIB),
+        ]
+
+        def listed_ts(j0, j1):
+            part, first = (0, 0) if j0 < 512 else (1, 512) if j0 < 768 else (2, 768)
+            return ts_part[part][:, j0 - first : j1 - first]
+
 
         def table_words(a, j0, j1):
             x = j0 // (J // 2)
@@ -122,22 +136,22 @@ def tile_list_gmlpt_gelu_tsL_kernel(tc, tab_words, tab_scales, wg_words, wg_scal
         wg_s = held([P, 2, 4, P], U8, "wg_s")
 
         def deal_views(b, a, dtype):
-            src = (wg_raw0, wg_raw1)[b][a][:]
+            src = wg_raw0[a][:] if b == 0 else wg_raw1[:, a]
             return (
                 wg_w[b][:, a].bitcast(dtype).rearrange("p (u e) m -> p u m e", u=2),
                 src.bitcast(dtype).rearrange("p (m u e) -> p u m e", u=2, e=2),
             )
 
-        wu_bf = [placed([P, 2, 4, P, 4], BF16, "wu_bf%d" % b, 24 * KIB) for b in range(2)]
-        wu_w = [held([P, 2, BAND], U32, "wu_w0"), placed([P, 2, BAND], U32, "wu_w1", 4 * KIB)]
+        wu_bf = {(b, a): placed([P, 4, P, 4], BF16, "wu_bf%d%d" % (b, a), [[24, 28], [31, 27]][b][a] * KIB) for b in range(2) for a in range(2)}
+        wu_w = [placed([P, 2, BAND], U32, "wu_w0", 40 * KIB), placed([P, 2, BAND], U32, "wu_w1", 4 * KIB)]
         wu_s = [held([P, 2, BAND], U8, "wu_s%d" % b) for b in range(2)]
 
         def round_views(b, a, u, x, order):
             slots = slice(2 * u, 2 * (u + 1))
-            places = slice(P // 2 * x, P // 2 * (x + 1))
-            src = wu_half[b, a, x][:]
+            places = slice(P // 2 * x[0], P // 2 * x[1])
+            src = wu_half[a, x[0]][:] if b == 0 else wu_raw1[a][:, :, HALF * x[0] : HALF * x[1]]
             return (
-                wu_bf[b][:, a, slots, places, :].rearrange("p t m i -> " + order),
+                wu_bf[b, a][:, slots, places, :].rearrange("p t m i -> " + order),
                 src.rearrange("p i (m t) -> p t m i", t=4)[:, slots].rearrange("p t m i -> " + order),
             )
 
@@ -154,7 +168,7 @@ def tile_list_gmlpt_gelu_tsL_kernel(tc, tab_words, tab_scales, wg_words, wg_scal
             nc.vector.quantize_mx(
                 wu_w[b][:, a, P * t0 : P * t1].bitcast(FP8X4),
                 wu_s[b][:, a, P * t0 : P * t1],
-                wu_bf[b][:, a, t0:t1, :, :].rearrange("p t m i -> p (t m i)"),
+                wu_bf[b, a][:, t0:t1, :, :].rearrange("p t m i -> p (t m i)"),
             )
 
         g_first = placed([P, 3, 2, CHUNK, 2], F32, "g_first", 4 * KIB)
@@ -186,7 +200,13 @@ def tile_list_gmlpt_gelu_tsL_kernel(tc, tab_words, tab_scales, wg_words, wg_scal
             nc.scalar.activation(g[b, c][:, u, :, :], gate_bank[b, c, u][:].rearrange("p e j -> p j e"), GELU)
 
         h_bf = [held([P, J, 4], BF16, "h_bf%d" % b) for b in range(2)]
-        h_w = [held([P, J], U32, "h_w%d" % b) for b in range(2)]
+        h_w0 = [held([P, J // 2], U32, "h_w00"), placed([P, J // 2], U32, "h_w01", 27 * KIB)]
+        h_w1 = held([P, J], U32, "h_w1")
+
+        def h_words(b, j0, j1):
+            x = j0 // (J // 2)
+            return h_w1[:, j0:j1] if b == 1 else h_w0[x][:, j0 - x * J // 2 : j1 - x * J // 2]
+
         h_s = [held([P, J], U8, "h_s%d" % b) for b in range(2)]
 
         def up(b, i):
@@ -213,7 +233,7 @@ def tile_list_gmlpt_gelu_tsL_kernel(tc, tab_words, tab_scales, wg_words, wg_scal
             )
 
         def quantize_h(b, j0, j1):
-            nc.vector.quantize_mx(h_w[b][:, j0:j1].bitcast(FP8X4), h_s[b][:, j0:j1], h_bf[b][:, j0:j1, :].rearrange("p j t -> p (j t)"))
+            nc.vector.quantize_mx(h_words(b, j0, j1).bitcast(FP8X4), h_s[b][:, j0:j1], h_bf[b][:, j0:j1, :].rearrange("p j t -> p (j t)"))
 
         def down(j0, j1):
             width = j1 - j0
@@ -224,13 +244,13 @@ def tile_list_gmlpt_gelu_tsL_kernel(tc, tab_words, tab_scales, wg_words, wg_scal
                         bank[:, n, :],
                         lhsT=wd_w[:, b, P * n : P * (n + 1)].bitcast(FP8X4),
                         lhsT_scale=wd_s[4 * b : P, P * n : P * (n + 1)],
-                        rhs=h_w[b][:, j0:j1].bitcast(FP8X4),
+                        rhs=h_words(b, j0, j1).bitcast(FP8X4),
                         rhs_scale=h_s[b][:, j0:j1],
                         start=(b == 0 and n == 0),
                         stop=(b == 1 and n == 1),
                     )
             res = keep.tile([P, 2, width], F32, name="res%d" % j0)
-            factor = ts_g[:, j0:j1].unsqueeze(1).to_broadcast([P, 2, width])
+            factor = listed_ts(j0, j1).unsqueeze(1).to_broadcast([P, 2, width])
             if j0 < GPSIMD_COLUMNS:
                 y_sb = keep.tile([P, 2, width], F32, name="y_sb%d" % j0)
                 nc.scalar.copy(y_sb[:], bank[:])
@@ -245,29 +265,32 @@ def tile_list_gmlpt_gelu_tsL_kernel(tc, tab_words, tab_scales, wg_words, wg_scal
         nc.vector.tensor_copy(wg_s[:], wg_s_raw[:].rearrange("p (b m t) -> p b t m", b=2, t=4))
         nc.vector.tensor_copy(*deal_views(0, 1, I32))
         gather(v_w[0][1][:], tab_w[0], J // 2, J)
+        gather(ts_part[0][:], ts_all, 0, 512)
+        for u in range(2):
+            round_on_scalar(0, 0, u, (0, 1))
         for c in range(4):
             for u in range(2):
                 gate_pass(0, c, u, 0)
         for c in range(4):
             gather(table_words(1, CHUNK * c, CHUNK * (c + 1)), tab_w[1], CHUNK * c, CHUNK * (c + 1))
+        for u in range(2):
+            round_on_gpsimd(0, 0, u, (1, 2))
         for a in range(2):
-            nc.scalar.copy(*deal_views(1, a, U32))
+            nc.vector.tensor_copy(*deal_views(1, a, I32))
         for c in range(4):
             for u in range(2):
                 gate_pass(0, c, u, 1)
                 gelu(0, c, u)
-        gather(ts_g[:], ts_all, 0, J)
 
-        for u, x in ((0, 0), (1, 0), (0, 1)):
-            round_on_gpsimd(0, 0, u, x)
-        round_on_vector(0, 0, 1, 1)
-        for u in range(2):
-            round_on_vector(0, 1, u, 0)
         quantize_wu(0, 0, 0, 4)
-        for u in range(2):
-            round_on_vector(0, 1, u, 1)
+        for x in range(2):
+            for u in range(2):
+                round_on_vector(0, 1, u, (x, x + 1))
+            if x == 0:
+                gather(ts_part[1][:], ts_all, 512, 768)
         for u in range(2):
             quantize_wu(0, 1, 2 * u, 2 * (u + 1))
+        gather(ts_part[2][:], ts_all, 768, J)
 
         def gate(i):
             c, u = divmod(i, 2)
@@ -277,17 +300,15 @@ def tile_list_gmlpt_gelu_tsL_kernel(tc, tab_words, tab_scales, wg_words, wg_scal
         for i in range(EARLY_GATES):
             gate(i)
             gelu(1, *divmod(i, 2))
-        for x in range(2):
-            for u in range(2):
-                round_on_gpsimd(1, 0, u, x)
-        for x in range(2):
-            round_on_scalar(1, 1, 1, x)
-            round_on_gpsimd(1, 1, 0, x)
+        for a, x in ((0, 0), (0, 1), (1, 0)):
+            round_on_gpsimd(1, a, 0, (x, x + 1))
+        for a in range(2):
+            round_on_scalar(1, a, 1, (0, 2))
+        round_on_scalar(1, 1, 0, (1, 2))
         for i in range(8):
             up(0, i)
-            if i == 6:
-                for a in range(2):
-                    quantize_wu(1, a, 0, 4)
+            if i >= 6:
+                quantize_wu(1, i - 6, 0, 4)
         for i in range(EARLY_GATES, 8):
             gate(i)
             gelu(1, *divmod(i, 2))

@@ -24,11 +24,12 @@ CHUNK = 256
 KIB = 1024
 GPSIMD_COLUMNS = 512
 
-EARLY_GATES = 5
+TS_EARLY = 768
+EARLY_GATES = 4
 EARLY_UP_TILES = 2
-GATE_BANK = [[0, 1, 2, 3, 4, 5, 6, 7], [0, 1, 2, 3, 4, 0, 1, 2]]
-UP_BANK = [[5, 6, 7, 0, 1, 2, 3, 4], [5, 6, 7, 3, 5, 6, 7, 3]]
-DOWN_BANK = {0: 4, 256: 0, 512: 1, 768: 2, 896: 4}
+GATE_BANK = [[0, 1, 2, 3, 4, 5, 6, 7], [0, 1, 2, 3, 6, 7, 0, 1]]
+UP_BANK = [[4, 5, 6, 7, 0, 1, 4, 5], [4, 5, 2, 3, 4, 5, 2, 3]]
+DOWN_BANK = {0: 6, 256: 7, 512: 0, 768: 1, 896: 6}
 
 
 def tile_list_gmlpt_gelu_tsL_kernel(tc, tab_words, tab_scales, wg_words, wg_scales, wu, wd_words, wd_scales, ts, offs, out):
@@ -59,7 +60,7 @@ def tile_list_gmlpt_gelu_tsL_kernel(tc, tab_words, tab_scales, wg_words, wg_scal
         wg_raw0 = [held([P, BAND], U32, "wg_raw0%d" % a) for a in range(2)]
         wg_raw1 = placed([P, 2, BAND], U32, "wg_raw1", 0)
         wu_half = {(a, x): placed([P, 4, HALF], F32, "wu_half%d%d" % (a, x), (64 + 8 * a + 4 * x) * KIB) for a in range(2) for x in range(2)}
-        wu_raw1 = [held([P, 4, BAND], F32, "wu_raw1%d" % a) for a in range(2)]
+        wu_raw1 = [placed([P, 4, BAND], F32, "wu_raw1%d" % a, (80 + 8 * a) * KIB) for a in range(2)]
         wd_w = held([P, 2, N], U32, "wd_w")
         ts_all = held([P, T], F32, "ts_all")
         ts_row = held([P, T // P], F32, "ts_row")
@@ -114,15 +115,11 @@ def tile_list_gmlpt_gelu_tsL_kernel(tc, tab_words, tab_scales, wg_words, wg_scal
 
         v_w = [[held([P, J // 2], U32, "v_w%d%d" % (a, x)) if (a, x) != (0, 1) else placed([P, J // 2], U32, "v_w01", 62 * KIB) for x in range(2)] for a in range(2)]
         v_s = held([P, J], U8, "v_s")
-        ts_part = [
-            placed([P, J // 2], F32, "ts_early", 60 * KIB),
-            placed([P, CHUNK], F32, "ts_mid", 24 * KIB),
-            placed([P, CHUNK], F32, "ts_late", 76 * KIB),
-        ]
+        ts_early = placed([P, TS_EARLY], F32, "ts_early", 62 * KIB - 4 * TS_EARLY)
+        ts_late = placed([P, J - TS_EARLY], F32, "ts_late", 76 * KIB)
 
         def listed_ts(j0, j1):
-            part, first = (0, 0) if j0 < 512 else (1, 512) if j0 < 768 else (2, 768)
-            return ts_part[part][:, j0 - first : j1 - first]
+            return ts_early[:, j0:j1] if j0 < TS_EARLY else ts_late[:, j0 - TS_EARLY : j1 - TS_EARLY]
 
 
         def table_words(a, j0, j1):
@@ -143,7 +140,7 @@ def tile_list_gmlpt_gelu_tsL_kernel(tc, tab_words, tab_scales, wg_words, wg_scal
             )
 
         wu_bf = {(b, a): placed([P, 4, P, 4], BF16, "wu_bf%d%d" % (b, a), [[24, 28], [31, 27]][b][a] * KIB) for b in range(2) for a in range(2)}
-        wu_w = [placed([P, 2, BAND], U32, "wu_w0", 40 * KIB), placed([P, 2, BAND], U32, "wu_w1", 4 * KIB)]
+        wu_w = [placed([P, 2, BAND], U32, "wu_w0", 0), placed([P, 2, BAND], U32, "wu_w1", 4 * KIB)]
         wu_s = [held([P, 2, BAND], U8, "wu_s%d" % b) for b in range(2)]
 
         def round_views(b, a, u, x, order):
@@ -164,6 +161,12 @@ def tile_list_gmlpt_gelu_tsL_kernel(tc, tab_words, tab_scales, wg_words, wg_scal
         def round_on_vector(b, a, u, x):
             nc.vector.tensor_copy(*round_views(b, a, u, x, "p m i t"))
 
+        def round_half_on_vector(a, x):
+            nc.vector.tensor_copy(
+                wu_bf[0, a][:, :, P // 2 * x : P // 2 * (x + 1), :].rearrange("p (u e) m i -> p u m i e", u=2),
+                wu_half[a, x][:].rearrange("p i (m u e) -> p u m i e", u=2, e=2),
+            )
+
         def quantize_wu(b, a, t0, t1):
             nc.vector.quantize_mx(
                 wu_w[b][:, a, P * t0 : P * t1].bitcast(FP8X4),
@@ -176,7 +179,7 @@ def tile_list_gmlpt_gelu_tsL_kernel(tc, tab_words, tab_scales, wg_words, wg_scal
         g = {(0, c): g_first[:, c] for c in range(3)}
         g[0, 3] = g_last[:]
         for c in range(4):
-            g[1, c] = held([P, 2, CHUNK, 2], F32, "g1%d" % c)[:]
+            g[1, c] = (held([P, 2, CHUNK, 2], F32, "g1%d" % c) if c != 1 else placed([P, 2, CHUNK, 2], F32, "g11", 88 * KIB))[:]
         gate_bank = {}
 
         def gate_pass(b, c, u, a):
@@ -200,12 +203,7 @@ def tile_list_gmlpt_gelu_tsL_kernel(tc, tab_words, tab_scales, wg_words, wg_scal
             nc.scalar.activation(g[b, c][:, u, :, :], gate_bank[b, c, u][:].rearrange("p e j -> p j e"), GELU)
 
         h_bf = [held([P, J, 4], BF16, "h_bf%d" % b) for b in range(2)]
-        h_w0 = [held([P, J // 2], U32, "h_w00"), placed([P, J // 2], U32, "h_w01", 27 * KIB)]
-        h_w1 = held([P, J], U32, "h_w1")
-
-        def h_words(b, j0, j1):
-            x = j0 // (J // 2)
-            return h_w1[:, j0:j1] if b == 1 else h_w0[x][:, j0 - x * J // 2 : j1 - x * J // 2]
+        h_w = [placed([P, J], U32, "h_w0", 27 * KIB), held([P, J], U32, "h_w1")]
 
         h_s = [held([P, J], U8, "h_s%d" % b) for b in range(2)]
 
@@ -233,7 +231,7 @@ def tile_list_gmlpt_gelu_tsL_kernel(tc, tab_words, tab_scales, wg_words, wg_scal
             )
 
         def quantize_h(b, j0, j1):
-            nc.vector.quantize_mx(h_words(b, j0, j1).bitcast(FP8X4), h_s[b][:, j0:j1], h_bf[b][:, j0:j1, :].rearrange("p j t -> p (j t)"))
+            nc.vector.quantize_mx(h_w[b][:, j0:j1].bitcast(FP8X4), h_s[b][:, j0:j1], h_bf[b][:, j0:j1, :].rearrange("p j t -> p (j t)"))
 
         def down(j0, j1):
             width = j1 - j0
@@ -244,7 +242,7 @@ def tile_list_gmlpt_gelu_tsL_kernel(tc, tab_words, tab_scales, wg_words, wg_scal
                         bank[:, n, :],
                         lhsT=wd_w[:, b, P * n : P * (n + 1)].bitcast(FP8X4),
                         lhsT_scale=wd_s[4 * b : P, P * n : P * (n + 1)],
-                        rhs=h_words(b, j0, j1).bitcast(FP8X4),
+                        rhs=h_w[b][:, j0:j1].bitcast(FP8X4),
                         rhs_scale=h_s[b][:, j0:j1],
                         start=(b == 0 and n == 0),
                         stop=(b == 1 and n == 1),
@@ -265,7 +263,7 @@ def tile_list_gmlpt_gelu_tsL_kernel(tc, tab_words, tab_scales, wg_words, wg_scal
         nc.vector.tensor_copy(wg_s[:], wg_s_raw[:].rearrange("p (b m t) -> p b t m", b=2, t=4))
         nc.vector.tensor_copy(*deal_views(0, 1, I32))
         gather(v_w[0][1][:], tab_w[0], J // 2, J)
-        gather(ts_part[0][:], ts_all, 0, 512)
+        gather(ts_early[:], ts_all, 0, TS_EARLY)
         for u in range(2):
             round_on_scalar(0, 0, u, (0, 1))
         for c in range(4):
@@ -273,8 +271,8 @@ def tile_list_gmlpt_gelu_tsL_kernel(tc, tab_words, tab_scales, wg_words, wg_scal
                 gate_pass(0, c, u, 0)
         for c in range(4):
             gather(table_words(1, CHUNK * c, CHUNK * (c + 1)), tab_w[1], CHUNK * c, CHUNK * (c + 1))
-        for u in range(2):
-            round_on_gpsimd(0, 0, u, (1, 2))
+        round_on_scalar(0, 0, 1, (1, 2))
+        round_on_vector(0, 0, 0, (1, 2))
         for a in range(2):
             nc.vector.tensor_copy(*deal_views(1, a, I32))
         for c in range(4):
@@ -283,14 +281,12 @@ def tile_list_gmlpt_gelu_tsL_kernel(tc, tab_words, tab_scales, wg_words, wg_scal
                 gelu(0, c, u)
 
         quantize_wu(0, 0, 0, 4)
-        for x in range(2):
-            for u in range(2):
-                round_on_vector(0, 1, u, (x, x + 1))
-            if x == 0:
-                gather(ts_part[1][:], ts_all, 512, 768)
+        round_half_on_vector(1, 0)
+        for u in range(2):
+            round_on_vector(0, 1, u, (1, 2))
         for u in range(2):
             quantize_wu(0, 1, 2 * u, 2 * (u + 1))
-        gather(ts_part[2][:], ts_all, 768, J)
+        gather(ts_late[:], ts_all, TS_EARLY, J)
 
         def gate(i):
             c, u = divmod(i, 2)
@@ -299,22 +295,23 @@ def tile_list_gmlpt_gelu_tsL_kernel(tc, tab_words, tab_scales, wg_words, wg_scal
 
         for i in range(EARLY_GATES):
             gate(i)
-            gelu(1, *divmod(i, 2))
-        for a, x in ((0, 0), (0, 1), (1, 0)):
-            round_on_gpsimd(1, a, 0, (x, x + 1))
+            if i < 2:
+                gelu(1, 0, i)
         for a in range(2):
+            round_on_gpsimd(1, a, 0, (0, 1))
             round_on_scalar(1, a, 1, (0, 2))
-        round_on_scalar(1, 1, 0, (1, 2))
+            round_on_scalar(1, a, 0, (1, 2))
+        for u in range(2):
+            gelu(1, 1, u)
         for i in range(8):
             up(0, i)
-            if i >= 6:
-                quantize_wu(1, i - 6, 0, 4)
+        for a in range(2):
+            quantize_wu(1, a, 0, 4)
         for i in range(EARLY_GATES, 8):
             gate(i)
             gelu(1, *divmod(i, 2))
 
-        for x in range(2):
-            quantize_h(0, J // 2 * x, J // 2 * (x + 1))
+        quantize_h(0, 0, J)
         for c in range(4):
             if c > 1:
                 down(CHUNK * (c - 2), CHUNK * (c - 1))

@@ -58,8 +58,9 @@ def tile_list_gmlpt_gelu_tsL_kernel(tc, tab_words, tab_scales, wg_words, wg_scal
 
         tab_w = [held([P, T], U32, "tab_w0"), placed([P, T], U32, "tab_w1", 40 * KIB)]
         wg_raw0 = [held([P, BAND], U32, "wg_raw0%d" % a) for a in range(2)]
-        wg_raw1 = placed([P, 2, BAND], U32, "wg_raw1", 0)
-        wu_half = {(a, x): placed([P, 4, HALF], F32, "wu_half%d%d" % (a, x), (64 + 8 * a + 4 * x) * KIB) for a in range(2) for x in range(2)}
+        wg_raw1 = held([P, 2, BAND], U32, "wg_raw1")
+        wu_raw00 = held([P, 4, BAND], F32, "wu_raw00")
+        wu_half = {(a, x): placed([P, 4, HALF], F32, "wu_half%d%d" % (a, x), (64 + 8 * a + 4 * x) * KIB) for a in (1,) for x in range(2)}
         wu_raw1 = [placed([P, 4, BAND], F32, "wu_raw1%d" % a, (80 + 8 * a) * KIB) for a in range(2)]
         wd_w = held([P, 2, N], U32, "wd_w")
         ts_all = held([P, T], F32, "ts_all")
@@ -90,10 +91,9 @@ def tile_list_gmlpt_gelu_tsL_kernel(tc, tab_words, tab_scales, wg_words, wg_scal
         load_tab(0)
         load_scales(wg_s_raw, wg_scales)
         load_wg0(1)
-        load_half(0, 0)
-        load_tab(1)
-        load_half(0, 1)
         nc.sync.dma_start(wg_raw1[:].bitcast(I32), wg_src[:, :, 4 * BAND : 8 * BAND].bitcast(I32))
+        load_tab(1)
+        nc.sync.dma_start(wu_raw00[:], wu_src(0, 0))
         for x in range(2):
             load_half(1, x)
         for a in range(2):
@@ -140,13 +140,13 @@ def tile_list_gmlpt_gelu_tsL_kernel(tc, tab_words, tab_scales, wg_words, wg_scal
             )
 
         wu_bf = {(b, a): placed([P, 4, P, 4], BF16, "wu_bf%d%d" % (b, a), [[24, 28], [31, 27]][b][a] * KIB) for b in range(2) for a in range(2)}
-        wu_w = [placed([P, 2, BAND], U32, "wu_w0", 0), placed([P, 2, BAND], U32, "wu_w1", 4 * KIB)]
+        wu_w = [held([P, 2, BAND], U32, "wu_w0"), placed([P, 2, BAND], U32, "wu_w1", 4 * KIB)]
         wu_s = [held([P, 2, BAND], U8, "wu_s%d" % b) for b in range(2)]
 
         def round_views(b, a, u, x, order):
             slots = slice(2 * u, 2 * (u + 1))
             places = slice(P // 2 * x[0], P // 2 * x[1])
-            src = wu_half[a, x[0]][:] if b == 0 else wu_raw1[a][:, :, HALF * x[0] : HALF * x[1]]
+            src = wu_half[a, x[0]][:] if (b, a) == (0, 1) else (wu_raw1[a] if b else wu_raw00)[:, :, HALF * x[0] : HALF * x[1]]
             return (
                 wu_bf[b, a][:, slots, places, :].rearrange("p t m i -> " + order),
                 src.rearrange("p i (m t) -> p t m i", t=4)[:, slots].rearrange("p t m i -> " + order),
@@ -264,24 +264,22 @@ def tile_list_gmlpt_gelu_tsL_kernel(tc, tab_words, tab_scales, wg_words, wg_scal
         nc.vector.tensor_copy(*deal_views(0, 1, I32))
         gather(v_w[0][1][:], tab_w[0], J // 2, J)
         gather(ts_early[:], ts_all, 0, TS_EARLY)
-        for u in range(2):
-            round_on_scalar(0, 0, u, (0, 1))
+        for a in range(2):
+            nc.scalar.copy(*deal_views(1, a, U32))
         for c in range(4):
             for u in range(2):
                 gate_pass(0, c, u, 0)
         for c in range(4):
             gather(table_words(1, CHUNK * c, CHUNK * (c + 1)), tab_w[1], CHUNK * c, CHUNK * (c + 1))
-        round_on_scalar(0, 0, 1, (1, 2))
-        round_on_vector(0, 0, 0, (1, 2))
-        for a in range(2):
-            nc.vector.tensor_copy(*deal_views(1, a, I32))
+        for u in range(2):
+            round_on_vector(0, 0, u, (0, 2))
         for c in range(4):
             for u in range(2):
                 gate_pass(0, c, u, 1)
                 gelu(0, c, u)
 
-        quantize_wu(0, 0, 0, 4)
         round_half_on_vector(1, 0)
+        quantize_wu(0, 0, 0, 4)
         for u in range(2):
             round_on_vector(0, 1, u, (1, 2))
         for u in range(2):

from contextlib import ExitStack

import concourse.mybir as mybir
from concourse.masks import make_identity

K, R, N, T, J = 1024, 1024, 256, 2048, 1024
FLOPS = 2 * (2 * K * R * J + R * N * J)

F32 = mybir.dt.float32
BF16 = mybir.dt.bfloat16
I32 = mybir.dt.int32
U32 = mybir.dt.uint32
U16 = mybir.dt.uint16
U8 = mybir.dt.uint8
FP8X4 = mybir.dt.float8_e4m3fn_x4
GELU = mybir.ActivationFunctionType.Gelu_apprx_tanh
MULT = mybir.AluOpType.mult
ADD = mybir.AluOpType.add

P = 128
BAND = 512
HALF = BAND // 2
CHUNK = 256
KIB = 1024
GPSIMD_COLUMNS = 512

TS_EARLY = 768
EARLY_GATES = 4
EARLY_UP_TILES = 2
GATE_BANK = [[0, 1, 2, 3, 4, 5, 6, 7], [0, 1, 2, 3, 6, 7, 0, 1]]
UP_BANK = [[4, 5, 6, 7, 0, 1, 4, 5], [4, 5, 2, 3, 4, 5, 2, 3]]
DOWN_BANK = {0: 6, 256: 7, 512: 0, 768: 1, 896: 6}


def tile_list_gmlpt_gelu_tsL_kernel(tc, tab_words, tab_scales, wg_words, wg_scales, wu, wd_words, wd_scales, ts, offs, out):
    nc = tc.nc
    with ExitStack() as ctx:
        keep = ctx.enter_context(tc.tile_pool(name="keep", bufs=1))
        shared = ctx.enter_context(tc.tile_pool(name="shared", bufs=1))
        psum = ctx.enter_context(tc.psum_pool(name="psum", bufs=1))

        def held(shape, dtype, name):
            return keep.tile(shape, dtype, name=name, align_bytes=64)

        def placed(shape, dtype, name, offset):
            return shared.tile(shape, dtype, name=name, offset=offset, align_bytes=64)

        def in_bank(number, shape):
            return psum.tile(shape, F32, name="bank%d" % number)

        offsets = keep.tile([P, J // 16], U16, name="offsets")
        tab_s = held([P, T], U8, "tab_s")
        wg_s_raw = placed([P, R], U8, "wg_s_raw", 62 * KIB - R // 2)
        wd_s = held([P, N], U8, "wd_s")
        for scale_tile in (tab_s, wg_s_raw):
            nc.gpsimd.memset(scale_tile[:].bitcast(I32), 0)
        nc.vector.memset(wd_s[:].bitcast(I32), 0)

        tab_w = [held([P, T], U32, "tab_w0"), placed([P, T], U32, "tab_w1", 40 * KIB)]
        wg_raw0 = [held([P, BAND], U32, "wg_raw0%d" % a) for a in range(2)]
        wg_raw1 = held([P, 2, BAND], U32, "wg_raw1")
        wu_raw00 = held([P, 4, BAND], F32, "wu_raw00")
        wu_half = {(a, x): placed([P, 4, HALF], F32, "wu_half%d%d" % (a, x), (64 + 8 * a + 4 * x) * KIB) for a in (1,) for x in range(2)}
        wu_raw1 = [placed([P, 4, BAND], F32, "wu_raw1%d" % a, (80 + 8 * a) * KIB) for a in range(2)]
        wd_w = held([P, 2, N], U32, "wd_w")
        ts_all = held([P, T], F32, "ts_all")
        ts_row = held([P, T // P], F32, "ts_row")

        def load_scales(scale_tile, src):
            for q in range(4):
                nc.sync.dma_start(scale_tile[32 * q : 32 * q + 8, :].bitcast(I32), src[:, 4 * q : 4 * q + 4, :].bitcast(I32))

        def load_tab(a):
            nc.sync.dma_start(tab_w[a][:].bitcast(I32), tab_words[a].rearrange("p t i -> p (t i)").bitcast(I32))

        wg_src = wg_words.rearrange("a p r i -> p a (r i)")

        def load_wg0(a):
            nc.sync.dma_start(wg_raw0[a][:].bitcast(I32), wg_src[:, a, 0 : 4 * BAND].bitcast(I32))

        def load_half(a, x):
            nc.sync.dma_start(wu_half[a, x][:], wu_src(0, a)[:, :, HALF * x : HALF * (x + 1)])

        def wu_src(b, a):
            return wu[BAND * a : BAND * (a + 1), BAND * b : BAND * (b + 1)].rearrange("(p i) c -> p i c", i=4)

        nc.sync.dma_start(offsets[:], offs)
        load_wg0(0)
        load_scales(tab_s, tab_scales)
        nc.sync.dma_start(ts_row[:], ts[0].rearrange("(p c) -> p c", c=T // P))
        load_tab(0)
        load_scales(wg_s_raw, wg_scales)
        load_wg0(1)
        nc.sync.dma_start(wg_raw1[:].bitcast(I32), wg_src[:, :, 4 * BAND : 8 * BAND].bitcast(I32))
        load_tab(1)
        nc.sync.dma_start(wu_raw00[:], wu_src(0, 0))
        for x in range(2):
            load_half(1, x)
        for a in range(2):
            nc.sync.dma_start(wu_raw1[a][:], wu_src(1, a))
        load_scales(wd_s, wd_scales)
        nc.sync.dma_start(wd_w[:].bitcast(I32), wd_words.rearrange("a p n i -> p a (n i)").bitcast(I32))

        warm = keep.tile([P, 8], F32, name="warm")
        nc.vector.memset(warm[:], 0.0)
        nc.scalar.activation(warm[:, 0:1], warm[:, 1:2], GELU)

        ident = held([P, P], F32, "ident")
        make_identity(nc, ident[:])
        for c0 in range(0, T // P, 4):
            bank = in_bank(4 + c0 // 4, [P, 4, P])
            for c in range(4):
                nc.tensor.transpose(bank[:, c, :], ts_row[:, c0 + c : c0 + c + 1].to_broadcast([P, P]), ident[:])
            nc.scalar.copy(ts_all[:].rearrange("q (p c) -> q p c", c=T // P)[:, :, c0 : c0 + 4], bank[:].rearrange("q c p -> q p c"))

        v_w = [[held([P, J // 2], U32, "v_w%d%d" % (a, x)) if (a, x) != (0, 1) else placed([P, J // 2], U32, "v_w01", 62 * KIB) for x in range(2)] for a in range(2)]
        v_s = held([P, J], U8, "v_s")
        ts_early = placed([P, TS_EARLY], F32, "ts_early", 62 * KIB - 4 * TS_EARLY)
        ts_late = placed([P, J - TS_EARLY], F32, "ts_late", 76 * KIB)

        def listed_ts(j0, j1):
            return ts_early[:, j0:j1] if j0 < TS_EARLY else ts_late[:, j0 - TS_EARLY : j1 - TS_EARLY]


        def table_words(a, j0, j1):
            x = j0 // (J // 2)
            return v_w[a][x][:, j0 - x * J // 2 : j1 - x * J // 2]

        def gather(dst, window, j0, j1):
            nc.vector.tensor_copy(dst, window[:].indirect(offsets[:, j0 // 16 : j1 // 16]))

        wg_w = [held([P, 2, 4, P], U32, "wg_w%d" % b) for b in range(2)]
        wg_s = held([P, 2, 4, P], U8, "wg_s")

        def deal_views(b, a, dtype):
            src = wg_raw0[a][:] if b == 0 else wg_raw1[:, a]
            return (
                wg_w[b][:, a].bitcast(dtype).rearrange("p (u e) m -> p u m e", u=2),
                src.bitcast(dtype).rearrange("p (m u e) -> p u m e", u=2, e=2),
            )

        wu_bf = {(b, a): placed([P, 4, P, 4], BF16, "wu_bf%d%d" % (b, a), [[24, 28], [31, 27]][b][a] * KIB) for b in range(2) for a in range(2)}
        wu_w = [held([P, 2, BAND], U32, "wu_w0"), placed([P, 2, BAND], U32, "wu_w1", 4 * KIB)]
        wu_s = [held([P, 2, BAND], U8, "wu_s%d" % b) for b in range(2)]

        def round_views(b, a, u, x, order):
            slots = slice(2 * u, 2 * (u + 1))
            places = slice(P // 2 * x[0], P // 2 * x[1])
            src = wu_half[a, x[0]][:] if (b, a) == (0, 1) else (wu_raw1[a] if b else wu_raw00)[:, :, HALF * x[0] : HALF * x[1]]
            return (
                wu_bf[b, a][:, slots, places, :].rearrange("p t m i -> " + order),
                src.rearrange("p i (m t) -> p t m i", t=4)[:, slots].rearrange("p t m i -> " + order),
            )

        def round_on_gpsimd(b, a, u, x):
            nc.gpsimd.tensor_scalar(*round_views(b, a, u, x, "p m t i"), 1.0, 0.0, MULT, ADD)

        def round_on_scalar(b, a, u, x):
            nc.scalar.copy(*round_views(b, a, u, x, "p m i t"))

        def round_on_vector(b, a, u, x):
            nc.vector.tensor_copy(*round_views(b, a, u, x, "p m i t"))

        def round_half_on_vector(a, x):
            nc.vector.tensor_copy(
                wu_bf[0, a][:, :, P // 2 * x : P // 2 * (x + 1), :].rearrange("p (u e) m i -> p u m i e", u=2),
                wu_half[a, x][:].rearrange("p i (m u e) -> p u m i e", u=2, e=2),
            )

        def quantize_wu(b, a, t0, t1):
            nc.vector.quantize_mx(
                wu_w[b][:, a, P * t0 : P * t1].bitcast(FP8X4),
                wu_s[b][:, a, P * t0 : P * t1],
                wu_bf[b, a][:, t0:t1, :, :].rearrange("p t m i -> p (t m i)"),
            )

        g_first = placed([P, 3, 2, CHUNK, 2], F32, "g_first", 4 * KIB)
        g_last = placed([P, 2, CHUNK, 2], F32, "g_last", 16 * KIB)
        g = {(0, c): g_first[:, c] for c in range(3)}
        g[0, 3] = g_last[:]
        for c in range(4):
            g[1, c] = (held([P, 2, CHUNK, 2], F32, "g1%d" % c) if c != 1 else placed([P, 2, CHUNK, 2], F32, "g11", 88 * KIB))[:]
        gate_bank = {}

        def gate_pass(b, c, u, a):
            j0, j1 = CHUNK * c, CHUNK * (c + 1)
            if a == 0:
                gate_bank[b, c, u] = in_bank(GATE_BANK[b][2 * c + u], [P, 2, CHUNK])
            bank = gate_bank[b, c, u]
            for e in range(2):
                t = 2 * u + e
                nc.tensor.matmul_mx(
                    bank[:, e, :],
                    lhsT=wg_w[b][:, a, t, :].bitcast(FP8X4),
                    lhsT_scale=wg_s[4 * a : P, b, t, :],
                    rhs=table_words(a, j0, j1).bitcast(FP8X4),
                    rhs_scale=v_s[4 * a : P, j0:j1],
                    start=(a == 0 and e == 0),
                    stop=(a == 1 and e == 1),
                )

        def gelu(b, c, u):
            nc.scalar.activation(g[b, c][:, u, :, :], gate_bank[b, c, u][:].rearrange("p e j -> p j e"), GELU)

        h_bf = [held([P, J, 4], BF16, "h_bf%d" % b) for b in range(2)]
        h_w = [placed([P, J], U32, "h_w0", 27 * KIB), held([P, J], U32, "h_w1")]

        h_s = [held([P, J], U8, "h_s%d" % b) for b in range(2)]

        def up(b, i):
            c, d = divmod(i, 2)
            j0, j1 = P * i, P * (i + 1)
            bank = in_bank(UP_BANK[b][i], [P, 4, P])
            passes = (0, 1) if i < EARLY_UP_TILES else (1, 0)
            for a in passes:
                for t in range(4):
                    nc.tensor.matmul_mx(
                        bank[:, t, :],
                        lhsT=wu_w[b][:, a, P * t : P * (t + 1)].bitcast(FP8X4),
                        lhsT_scale=wu_s[b][:, a, P * t : P * (t + 1)],
                        rhs=table_words(a, j0, j1).bitcast(FP8X4),
                        rhs_scale=v_s[4 * a : P, j0:j1],
                        start=(a == passes[0] and t == 0),
                        stop=(a == passes[1] and t == 3),
                    )
            nc.vector.tensor_tensor(
                h_bf[b][:, j0:j1, :].rearrange("p j (u e) -> p j u e", u=2),
                bank[:].rearrange("p (u e) j -> p j u e", u=2),
                g[b, c][:, :, P * d : P * (d + 1), :].rearrange("p u j e -> p j u e"),
                MULT,
            )

        def quantize_h(b, j0, j1):
            nc.vector.quantize_mx(h_w[b][:, j0:j1].bitcast(FP8X4), h_s[b][:, j0:j1], h_bf[b][:, j0:j1, :].rearrange("p j t -> p (j t)"))

        def down(j0, j1):
            width = j1 - j0
            bank = in_bank(DOWN_BANK[j0], [P, 2, width])
            for b in range(2):
                for n in range(2):
                    nc.tensor.matmul_mx(
                        bank[:, n, :],
                        lhsT=wd_w[:, b, P * n : P * (n + 1)].bitcast(FP8X4),
                        lhsT_scale=wd_s[4 * b : P, P * n : P * (n + 1)],
                        rhs=h_w[b][:, j0:j1].bitcast(FP8X4),
                        rhs_scale=h_s[b][:, j0:j1],
                        start=(b == 0 and n == 0),
                        stop=(b == 1 and n == 1),
                    )
            res = keep.tile([P, 2, width], F32, name="res%d" % j0)
            factor = listed_ts(j0, j1).unsqueeze(1).to_broadcast([P, 2, width])
            if j0 < GPSIMD_COLUMNS:
                y_sb = keep.tile([P, 2, width], F32, name="y_sb%d" % j0)
                nc.scalar.copy(y_sb[:], bank[:])
                nc.gpsimd.tensor_tensor(res[:], y_sb[:], factor, MULT)
            else:
                nc.vector.tensor_tensor(res[:], bank[:], factor, MULT)
            nc.sync.dma_start(out[:, j0:j1].rearrange("(n p) j -> p n j", p=P), res[:])

        nc.vector.tensor_copy(*deal_views(0, 0, I32))
        gather(v_s[:], tab_s, 0, J)
        gather(v_w[0][0][:], tab_w[0], 0, J // 2)
        nc.vector.tensor_copy(wg_s[:], wg_s_raw[:].rearrange("p (b m t) -> p b t m", b=2, t=4))
        nc.vector.tensor_copy(*deal_views(0, 1, I32))
        gather(v_w[0][1][:], tab_w[0], J // 2, J)
        gather(ts_early[:], ts_all, 0, TS_EARLY)
        for a in range(2):
            nc.scalar.copy(*deal_views(1, a, U32))
        for c in range(4):
            for u in range(2):
                gate_pass(0, c, u, 0)
        for c in range(4):
            gather(table_words(1, CHUNK * c, CHUNK * (c + 1)), tab_w[1], CHUNK * c, CHUNK * (c + 1))
        for u in range(2):
            round_on_vector(0, 0, u, (0, 2))
        for c in range(4):
            for u in range(2):
                gate_pass(0, c, u, 1)
                gelu(0, c, u)

        round_half_on_vector(1, 0)
        quantize_wu(0, 0, 0, 4)
        for u in range(2):
            round_on_vector(0, 1, u, (1, 2))
        for u in range(2):
            quantize_wu(0, 1, 2 * u, 2 * (u + 1))
        gather(ts_late[:], ts_all, TS_EARLY, J)

        def gate(i):
            c, u = divmod(i, 2)
            for a in range(2):
                gate_pass(1, c, u, a)

        for i in range(EARLY_GATES):
            gate(i)
            if i < 2:
                gelu(1, 0, i)
        for a in range(2):
            round_on_gpsimd(1, a, 0, (0, 1))
            round_on_scalar(1, a, 1, (0, 2))
            round_on_scalar(1, a, 0, (1, 2))
        for u in range(2):
            gelu(1, 1, u)
        for i in range(8):
            up(0, i)
        for a in range(2):
            quantize_wu(1, a, 0, 4)
        for i in range(EARLY_GATES, 8):
            gate(i)
            gelu(1, *divmod(i, 2))

        quantize_h(0, 0, J)
        for c in range(4):
            if c > 1:
                down(CHUNK * (c - 2), CHUNK * (c - 1))
            up(1, 2 * c)
            if c > 0:
                quantize_h(1, CHUNK * (c - 1), CHUNK * c)
            if c == 3:
                quantize_h(1, J - CHUNK, J - P)
            up(1, 2 * c + 1)
        down(J - 2 * CHUNK, J - CHUNK)
        quantize_h(1, J - P, J)
        down(J - CHUNK, J - P)
        down(J - P, J)
